import numpy as np, ml_dtypes
CORES = [10,34,74,98]
N = 4
BF = ml_dtypes.bfloat16
V, K, H, G, W, Q, RO = 1024, 2, 512, 768, 3328, 3, 5
AL = 0.125
def parts(rng):
    nm = np.where(rng.random((N, 8, V, 16)) < 0.4, rng.integers(0, V, (N, 8, V, 16)), rng.integers(0, W, (N, 8, V, 16)))
    dl = rng.integers(0, 1024, (N, 8, V, 16)); ph = rng.integers(0, 1024, (N, 8, V)); rb = rng.integers(0, 1024, (N, 8, V))
    lo = np.exp2(rng.random((N, 8, V, 1)) + 3.0 * rng.random((N, 8, V, 16)) - 1.0)
    fa = 0.875 + 0.125 * rng.random((N, 8, V, 16))
    return nm, dl, ph, rb, lo, fa
def turn(x):
    return np.ascontiguousarray(x.transpose(0, 1, 3, 2)).reshape(N, 128, V)
def pack(nm, dl, ph, rb, lo, fa):
    return {"loud": turn(np.clip(lo, 0.5, 8.0)).astype(BF), "fade": turn(np.clip(fa, 0.875, 1.0)).astype(BF), "ph0": ph.astype(np.int32), "rb": rb.astype(np.int32),
            "nb": turn(nm + 4096 * dl).astype(np.int32)}
def setup_inputs(rng):
    return pack(*parts(rng))
def newl(way, l, x, f):
    if way == 1: l, x, f = l.astype(np.float64), x.astype(np.float64), f.astype(np.float64)
    if way == 2: return (np.float32(1.0 - AL) * l + np.float32(AL) * x) * f
    if way == 3: return l * f + (np.float32(AL) * (x - l)) * f
    v = (l + np.float32(AL) * (x - l)) * f
    if way == 4: v = (np.rint(v.astype(np.float64) * 2.0 ** 21) * 2.0 ** -21).astype(np.float32)
    return v
def rivals(rng):
    n = 2 ** 18
    def some(low, high):
        return (low + (high - low) * rng.random(n)).astype(BF).astype(np.float32)
    z, fz, y, fy, a, fa = some(0.5, 1.0), some(0.875, 1.0), some(0.5, 1.0), some(0.875, 1.0), some(4.5, 7.5), some(0.875, 1.0)
    val = []
    for way in range(5):
        z1 = newl(way, z, z, fz) if K > 1 else z
        val.append(newl(way, newl(way, a, y, fa), newl(way, y, z1, fy), fa))
    o = np.argsort(val[0]); i, j = o[:-1], o[1:]; same = val[0][i] == val[0][j]; kinds = []
    for way in range(1, 5):
        w = val[way]
        m = same & (w[i] != w[j]); b, c = i[m], j[m]; up = w[b] < w[c]
        kinds.append((np.where(up, b, c), np.where(up, c, b)))
        m = ~same & (w[j] <= w[i]); kinds.append((i[m], j[m]))
    kinds = [p for p in kinds if len(p[0]) > 0] or [(np.array([0]), np.array([1]))]
    return kinds, z, fz, y, fy, a, fa
def close(rng, nm, dl, ph, rb, lo, fa):
    kinds, z, fz, y, fy, a, ff = rivals(rng)
    ix = np.zeros((N, 8, 32, 16), np.int64)
    for s in range(16):
        first, second = kinds[s % len(kinds)]; c = rng.integers(0, len(first), (N, 8, 16))
        ix[:, :, s] = first[c]; ix[:, :, 16 + s] = second[c]
    d = int(rng.integers(1, N)); e = int(rng.integers(1, N))
    tw = K * np.arange(32); zs = K * (32 + np.arange(32)); ys = K * (np.arange(32) + (64 if K == 1 else 0)) + K - 1
    ju = K * (H - 1 - np.arange(64)) + (RO - 1) % K
    iy = np.roll(ix, (-d, 1), axis=(0, 1)); iz = np.roll(iy, (-e, 1), axis=(0, 1))
    lo[:, :, tw] = a[ix]; fa[:, :, tw] = ff[ix]
    lo[:, :, ys] = y[iy]; fa[:, :, ys] = fy[iy]
    lo[:, :, zs] = z[iz]; fa[:, :, zs] = fz[iz]
    nm[:, :, tw] = (V + (d - 1) * G + ys)[:, None]
    nm[:, :, ys] = (V + (e - 1) * G + zs)[:, None]
    nm[:, :, zs] = zs[:, None]
    st = np.arange(64) % 16; blk = rng.integers(0, N, (N, 8, 64, 1)); cut = rng.integers(2, 16, (N, 8, 64, 1)); k = np.arange(16)
    base = np.where(blk == 0, 0, V + (blk - 1) * G)
    pair = base + np.where(k < cut, tw[st][:, None], tw[16 + st][:, None])
    nm[:, :, ju] = np.where(k == 0, (V + (d - 1) * G + ys[st])[:, None], pair)
    every = np.concatenate([tw, ys, zs, ju]); wait = rng.integers(0, 1024, (N, 8, len(every)))
    dl[:, :, every] = wait[..., None]; rb[:, :, every] = (-wait) & 1023; ph[:, :, every] = int(rng.integers(0, 1024))
def setup_inputs_spread(rng):
    nm, dl, ph, rb, lo, fa = parts(rng)
    nm = np.where(rng.random(nm.shape) < 0.5, nm, np.minimum((W * rng.random(nm.shape) ** 3).astype(np.int64), W - 1))
    dl = np.minimum(np.exp2(10 * rng.random(dl.shape)).astype(np.int64), 1024) - 1
    ph = np.minimum(np.exp2(10 * rng.random(ph.shape)).astype(np.int64), 1023)
    rb = np.minimum((1024 * rng.random(rb.shape) ** 2).astype(np.int64), 1023)
    lo = 2.0 * np.exp2(rng.integers(-1, 2, (N, 8, V, 1))) * np.exp2(2.0 * rng.random(lo.shape) - 1.0)
    fa = np.where(rng.random(fa.shape) < 0.5, fa, 1.0)
    close(rng, nm, dl, ph, rb, lo, fa)
    return pack(nm, dl, ph, rb, lo, fa)
def setup_inputs_ends(rng):
    nm, dl, ph, rb, lo, fa = parts(rng)
    dl = np.where(rng.random(dl.shape) < 0.9, 1023 * rng.integers(0, 2, dl.shape), dl)
    u = rng.random(nm.shape); low, high = u < 0.35, u > 0.65
    nm = np.where(low, 0, np.where(high, W - 1, nm)); dl = np.where(low, 0, np.where(high, 1023, dl))
    ph = np.where(rng.random(ph.shape) < 0.9, 1023 * rng.integers(0, 2, ph.shape), ph); rb = np.where(rng.random(rb.shape) < 0.9, 1023 * rng.integers(0, 2, rb.shape), rb)
    lo = np.where(rng.random(lo.shape) < 0.75, np.where(rng.random(lo.shape) < 0.5, 0.5, 8.0), lo)
    fa = np.where(rng.random(fa.shape) < 0.8, np.where(rng.random(fa.shape) < 0.5, 0.875, 1.0), fa)
    ph[:, ::2, G - 1] = 0
    lad = V - 1 - K * np.arange(16, 0, -1); b = V - 1 - 17 * K
    lo[:, 3::4, lad] = (8.0 - 0.03125 * (15 - np.arange(16)))[:, None]
    ph[:, 3::4, lad] = 0; ph[:, 3::4, V - 1] = 0; ph[:, 3::4, b] = 0; rb[:, 3::4, V - 1] = 1023
    nm[:, 3::4, V - 1] = lad; dl[:, 3::4, V - 1] = 1008 + np.arange(16)
    nm[:, 3::4, b] = lad[15]; dl[:, 3::4, b] = 1023
    return pack(nm, dl, ph, rb, lo, fa)
def setup_inputs_crowd(rng):
    nm, dl, ph, rb, lo, fa = parts(rng)
    place = np.array([0, V - 1, V, W - 1]); one = np.arange(16)[None, None, :] == rng.integers(0, 16, (N, V, 1))
    nm[:, 0] = 0
    nm[:, 1] = np.where(one, nm[:, 1], W - 1)
    nm[:, 2] = rng.choice(place, (N, V, 1))
    nm[:, 3] = rng.choice(place, (N, V, 16)); dl[:, 3] = rng.choice(np.array([0, 1, 512, 1023]), (N, V, 16))
    nm[:, 4] = V - 1; dl[:, 4] = 1023
    nm[:, 5] = np.where(one, nm[:, 5], V - 1); dl[:, 5] = rng.integers(0, 1024, (N, V, 1))
    return pack(nm, dl, ph, rb, lo, fa)
def setup_inputs_bands(rng):
    nm, dl, ph, rb, lo, fa = parts(rng)
    lev = np.argsort(rng.random((N, 8, V, 16)), axis=3); nm = 16 * rng.integers(0, W // 16, (N, 8, V, 16)) + lev
    for g in (1, 4, 7): nm[:, g] = nm[:, g] % V
    way = rng.integers(0, 3, (N, 8, V, 1)); dl = np.where(way == 0, 64 * lev, np.where(way == 1, 64 * (15 - lev), rng.integers(0, 1024, (N, 8, V, 1))))
    ph[:] = rng.integers(0, 1024); o = rng.permutation(16); rise = 0.5 + 0.4375 * (np.arange(V) % 16)
    for g in range(8):
        n = (16, 16, Q, Q, Q, Q - 1, Q - 1, Q - 1)[g]
        lo[:, g] = 2.0
        for b in o[:n]: lo[:, g, :, b] = rise
    fa[:, 2:] = 1.0
    return pack(nm, dl, ph, rb, lo, fa)
def setup_inputs_calm(rng):
    nm, dl, ph, rb, lo, fa = parts(rng)
    for g in (1, 3): nm[:, g] = nm[:, g] % V
    d8 = np.array([8, 1023, 512, 3, 0, 1, 1023, 16])[None, :, None]; step = np.array([1, 0, 0, -1, 1, 1, 0, 1])[None, :, None]
    ph = rng.integers(0, 4, (N, 8, V)); ph[:, 0] = 0; ph[:, 4] = rng.integers(0, 2, (N, V)); ph[:, 2:4] = 1023 - rng.integers(0, 2, (N, 2, V))
    rb = (step * (rng.random((N, 8, V)) < 0.25) - d8) & 1023
    return pack(nm, np.zeros_like(dl) + d8[..., None], ph, rb, lo, fa)
def check_ranges(d):
    bad = []
    for k, lo, hi in (("loud", 0.5, 8.0), ("fade", 0.875, 1.0), ("ph0", 0, 1023), ("rb", 0, 1023), ("nb", 0, 4096 * 1023 + W - 1)):
        x = np.asarray(d[k], np.float64)
        if not (np.min(x) >= lo and np.max(x) <= hi): bad.append("range of " + k)
    if np.max(np.asarray(d["nb"]).astype(np.int64) & 4095) >= W: bad.append("a name in nb")
    return bad
def reference(loud, fade, ph0, rb, nb):
    L = np.ascontiguousarray(loud.astype(np.float32).reshape(N, 8, 16, V).transpose(0, 1, 3, 2))
    fd = np.ascontiguousarray(fade.astype(np.float32).reshape(N, 8, 16, V).transpose(0, 1, 3, 2))
    lst = np.ascontiguousarray(nb.astype(np.int64).reshape(N, 8, 16, V).transpose(0, 1, 3, 2))
    p = ph0.astype(np.int64); add = rb.astype(np.int64); E = np.zeros((N, 8, V, 16), np.float64)
    gi = np.arange(8)[:, None, None]; kk = np.arange(16)
    for t in range(RO):
        c = slice(t % K, V, K)
        L2, p2, lst2 = L.copy(), p.copy(), lst.copy()
        for r in range(N):
            wl = np.concatenate([L[r]] + [np.roll(L[(r - d) % N][:, :G], -1, axis=0) for d in range(1, N)], axis=1)
            wp = np.concatenate([p[r]] + [np.roll(p[(r - d) % N][:, :G], -1, axis=0) for d in range(1, N)], axis=1)
            mine = lst[r][:, c]
            nm = mine & 4095; a = (wp[gi, nm] + (mine >> 12) - p[r][:, c][:, :, None]) & 1023
            o = np.argsort(16 * a + kk, axis=2)
            nm = np.take_along_axis(nm, o, 2); a = np.take_along_axis(a, o, 2)
            x = wl[gi, nm]
            top = np.maximum.accumulate(x, axis=2); m = np.zeros_like(x); m[:, :, 1:] = top[:, :, :-1]
            free = np.count_nonzero(x > m, axis=3) >= Q
            xf = x[free].astype(np.float64); z = np.zeros(x.shape, np.float64)
            z[free] = xf * np.reciprocal(1.0 + np.exp(m[free].astype(np.float64) - xf))
            E[r][:, c] += np.add.reduce(z, axis=2)
            p2[r][:, c] = (p[r][:, c] + np.maximum.reduce(np.where(free, a, 0), axis=2) + add[r][:, c]) & 1023
            if t < RO - 1:
                own = L[r][:, c]; L2[r][:, c] = (own + np.float32(AL) * (top[:, :, 15] - own)) * fd[r][:, c]
            if t < RO - K:
                first = nm[:, :, 0]; got = lst[r][gi[:, :, 0], np.minimum(first, V - 1)]
                hid = np.zeros(free.shape, bool); np.put_along_axis(hid, o, ~free, 2)
                lst2[r][:, c] = np.where(hid & (first < V)[:, :, None], got, mine)
        L, p, lst = L2, p2, lst2
    return {"ye": np.ascontiguousarray(E.transpose(0, 1, 3, 2)).reshape(N, 128, V).astype(np.float32), "yp": np.asarray(p, np.float32)}

def check_inputs(d):
    bad = list(check_ranges(d))
    if not bad:
        for name, y in reference(**d).items():
            for q in range(N):
                v = np.abs(np.asarray(y[q], np.float64)); s = np.sqrt(np.mean(v * v))
                if v.max() > 6 * s or s < 2.0 ** 2: bad.append('%s of rank %d is uneven or too small' % (name, q))
    return bad

@@ -1,0 +1,666 @@
+import math
+from concourse.bass import DstId, RemoteDMATransfer
+from concourse.mybir import AluOpType as A, ActivationFunctionType as F
+
+R = 1664
+XW = 2056
+LN2 = math.log(2.0)
+f32, bf, f16, i32, u16 = "float32", "bfloat16", "float16", "int32", "uint16"
+
+
+def sb(n, t):
+    return ("sbuf", [128, n], t)
+
+
+SCRATCH = {
+    "LW": sb(6 * R, f32), "PW": sb(6 * R, bf), "xx": sb(4 * XW, f32), "dd": sb(8192, f32),
+    "sg": sb(4096, bf), "pg": sb(4096, bf), "tt": sb(2048, f32), "mm": sb(8192, f16),
+    "L8": sb(512, f32), "nbr": sb(1024, i32), "EE": sb(1024, f32),
+    "fad": sb(1024, bf), "lb": sb(768, bf),
+    "hi": sb(1024, i32), "lo": sb(1024, i32), "ua": sb(1024, u16), "us": sb(512, u16), "um": sb(512, u16),
+    "pp": sb(512, i32), "t1": sb(512, i32), "t2": sb(512, i32), "Ti": sb(256, i32), "ai": sb(256, i32),
+    "ac": sb(512, f16), "Sd": sb(2048, bf), "p2": sb(512, bf), "fs": sb(256, bf), "yy": sb(512, f32),
+    "ls": sb(256, f32), "la": sb(256, f16), "Ht": sb(256, bf), "cp": sb(512, f32), "go": sb(512, f32),
+    "msk": sb(512, bf), "jc": sb(128, f16), "ul": sb(32, u16), "ty": sb(256, f32),
+    "pc": sb(64, i32), "rc": sb(64, i32), "ps": sb(48, i32), "u1": sb(64, i32), "u2": sb(64, i32), "u3": sb(64, i32),
+    "va": sb(256, f32), "vh": sb(256, bf), "vl": sb(256, bf), "vs": sb(48, f32), "cs": sb(96, bf), "pl": sb(288, bf),
+    "ci": sb(160, i32), "cj": sb(144, i32), "ct": sb(48, f32), "cb": sb(8, bf), "Qw": sb(144, f32), "BL": sb(128, f32),
+    "Am": sb(128, f32), "Bo": sb(128, f32), "tm": sb(256, f32), "slf": sb(32, f32),
+    "Wc": sb(144, bf), "W1": sb(144, f16), "W64": sb(144, f16), "Z1": sb(128, f16), "Z64": sb(128, f16),
+    "Wp": sb(144, bf), "Wt": sb(144, f32), "NG": sb(128, bf), "Df": sb(1024, f16), "Rk": sb(1024, bf),
+    "FW": sb(256, bf), "I4": sb(128, bf), "Ih": sb(128, f16), "If": sb(128, f32), "SA": sb(128, f16),
+    "SB": sb(640, bf),
+    "hbL": ("dram", [12 * 256, 128], f32), "hbP": ("dram", [12 * 256, 128], bf),
+}
+for _i in range(8):
+    SCRATCH["B%d" % _i] = ("psum", [128, 512], f32)
+
+SEMAPHORES = (["cV", "cA", "cP", "cG", "lsm", "ip", "il0", "il1"] + ["ha%d" % i for i in range(13)]
+              + ["ap%d" % i for i in range(4)] + ["al%d" % i for i in range(4)] + ["d%d" % i for i in range(40)])
+
+CY, PCY, GA, OV = 0.83, 0.42, 1.56, 20.0
+SL, XL, ITER = 100.0, 250.0, 3
+OFF = [0] * 126
+SEED, TRIES, HEAT = 1, 1500, 200.0
+CACHE = {}
+
+
+def helpers(core, T, topo):
+    ok = [c for c in topo.cores_of(core) if T.rank_of(c) is None
+          and all(topo.may_write(c, o) for o in T.cores if o != core)]
+    same = [c for c in ok if topo.die(c) == topo.die(core)]
+    other = [c for c in ok if topo.die(c) != topo.die(core)]
+    return (same or ok)[0], (other or ok)[0]
+
+
+def emask(topo, src, dst, lo, n):
+    return sum(1 << e for e in topo.engines(src, dst)[lo:lo + n])
+
+
+def did(topo, c):
+    a = topo.addr(c)
+    return DstId(rid=a[0], pnc=a[1])
+
+
+def fan(g, T, topo, me, r, src, dst_of, sem):
+    n = len(T.cores)
+    to = [T.cores[(r + d) % n] for d in range(1, n)]
+    m = topo.mask(me, to[0])
+    for c in to:
+        m &= topo.mask(me, c)
+    g.remote_dma_fused([RemoteDMATransfer(dst_ids=[did(topo, c) for c in to], dma_engine_mask=m, remote_sem=sem,
+                                          srcs=[src], dsts=[dst_of(d) for d in range(1, n)])], local_sem=T.sem.lsm)
+    return bin(m).count("1")
+
+
+def gcol(reg, d, c):
+    return reg * R + 512 + (d - 1) * 384 + 128 * c
+
+
+def helper_program(g, core, T, topo, r, kind):
+    tot = 0
+    if kind == "L":
+        g.wait_ge(T.sem.ha12, 8)
+        tot += fan(g, T, topo, core, r, T.lb[:, 384:768],
+                   lambda d: T.sg[:, 1152 + (d - 1) * 384:1152 + d * 384], T.sem.il1)
+    for t in range(4):
+        for c in range(3):
+            q = 3 * t + c
+            g.wait_ge(T.sem["ha%d" % q], 16 if kind == "L" else 8)
+            hb, win, sem = (T.hbL, T.LW, "al%d") if kind == "L" else (T.hbP, T.PW, "ap%d")
+            tot += fan(g, T, topo, core, r, hb[256 * q + 16:256 * q + 144, :],
+                       lambda d: win[:, gcol(t + 2, d, c):gcol(t + 2, d, c) + 128], T.sem[sem % t])
+    g.wait_ge(T.sem.lsm, tot)
+
+
+def build(g, core, T, topo, r):
+    V, S, P, Y = g.vector, g.scalar, g.tensor, g.sync
+    ops = []
+    nd = [0]
+    lsm = [0]
+    tag = [0]
+    hP, hL = helpers(core, T, topo)
+
+    def op(e, fn, cost, rd, wr, bk=(), tok=None, lat=0.0, pri=0.0):
+        ops.append(dict(e=e, fn=fn, c=cost, r=list(rd), w=list(wr), b=list(bk), tok=tok, lat=lat, tag=tag[0]))
+
+    def vc(n, k=1.0):
+        return OV + CY * max(64.0, n * k)
+
+    def ts(o, i, s1, s2, o0, o1, n, rd, wr, bk=(), k=1.0):
+        if o1 is None:
+            op("V", lambda: V.tensor_scalar(o, i, s1, None, o0), vc(n, k), rd, wr, bk)
+        else:
+            op("V", lambda: V.tensor_scalar(o, i, s1, s2, o0, o1), vc(n, k), rd, wr, bk)
+
+    def tt(o, a, b, o0, n, rd, wr, bk=(), k=None):
+        op("V", lambda: V.tensor_tensor(o, a, b, o0), vc(n, k or (1.0 if bk else 2.0)), rd, wr, bk)
+
+    def cp(o, i, n, rd, wr, bk=(), k=1.0):
+        op("V", lambda: V.tensor_copy(o, i), vc(n, k), rd, wr, bk)
+
+    def act(o, i, f, n, rd, wr, bk=(), bias=0.0, scale=1.0, k=1.0):
+        op("A", lambda: S.activation(o, i, f, bias=bias, scale=scale), vc(n, k), rd, wr, bk)
+
+    def mm(items, cost, rd, wr, bk, first=True, last=True):
+        def fn():
+            for j, (o, l, x) in enumerate(items):
+                ins = P.matmul(o, l, x, first and j == 0, last and j == len(items) - 1)
+            return ins
+        op("P", fn, OV + PCY * cost, rd, wr, bk)
+
+    def dma(e, pairs, rd, wr, lat=2200.0):
+        sem = "d%d" % nd[0]
+        nd[0] += 1
+        q = {"S": Y, "A": S, "G": g}[e]
+
+        def fn():
+            for o, i in pairs:
+                q.dma_start(o, i).then_inc(T.sem[sem], 16)
+        op(e, fn, (1000.0 if e == "G" else 100.0) * len(pairs), rd, wr, tok=(sem, 16 * len(pairs)), lat=lat)
+
+    def iota(o, pat, base, cm, n, wr, fl=False):
+        if fl:
+            op("G", lambda: g.iota(o, pat, base, cm, allow_small_or_imprecise_dtypes=True), 130 + 2 * CY * n, [], wr)
+        else:
+            op("G", lambda: g.iota(o, pat, base, cm), 130 + 2 * CY * n, [], wr)
+
+    def send(fn, rd, wr):
+        op("G", fn, 300.0, rd, wr, tok="none")
+
+    def ext(sem, cnt, rd, wr, lat):
+        op("X", None, 0.0, rd, wr, tok=(sem, cnt), lat=lat)
+
+    B = [T["B%d" % i] for i in range(8)]
+    ct = T.ct
+
+    dma("S", [(T.ps[0:112, :], T.ph0[1:8, 0:768]), (T.ps[112:128, :], T.ph0[0:1, 0:768])], [], ["ps"])
+    dma("A", [(T.nbr[:, :], T.nb[:, :])], [], ["nb0", "nb1"])
+    dma("S", [(T.pc[:, :], T.ph0[:, :]), (T.rc[:, :], T.rb[:, :])], [], ["pc"])
+    dma("A", [(T.sg[0:112, 2304:3072], T.loud[16:128, 0:768]), (T.sg[112:128, 2304:3072], T.loud[0:16, 0:768])], [], ["los"])
+    dma("S", [(T.sg[:, 3072:4096], T.loud[:, :]), (T.fad[:, :], T.fade[:, :])], [], ["lou", "fad"])
+    op("V", lambda: V.memset(T.PW[:, 0:2 * R], 0.0), vc(2 * R, 0.5), [], ["Pz"])
+
+    for p in range(2):
+        ts(T.vs[:, 24 * p:24 * p + 24], T.ps[:, p:48:2], -512.0, None, A.add, None, 24, ["ps"], ["vs%d" % p])
+    cp(T.cs[:, 0:48], T.vs[:, :], 48, ["vs0", "vs1"], ["cs0"])
+    tt(T.cs[:, 48:96], T.vs[:, :], T.cs[:, 0:48], A.subtract, 48, ["vs0", "vs1", "cs0"], ["cs1"])
+
+    def s_ip():
+        lsm[0] += fan(g, T, topo, core, r, T.cs[:, :], lambda d: T.pl[:, 96 * (d - 1):96 * d], T.sem.ip)
+    send(s_ip, ["cs0", "cs1"], ["s_ip"])
+    ext("ip", 24, ["s_ip"], ["pl"], 4000.0)
+    for p in range(2):
+        prs = []
+        for d in range(1, 4):
+            for h in range(2):
+                o = 96 * (d - 1) + 48 * h + 24 * p
+                prs.append((T.PW[h:128:16, gcol(p, d, 0):gcol(p, d, 0) + 384], T.pl[:, o:o + 24]))
+        dma("SA"[p], prs, ["pl", "Pz"], ["P%dg" % p])
+    for p in range(2):
+        cp(T.lb[:, 384 * p:384 * p + 384], T.sg[:, 2304 + p:3072:2], 384, ["los"], ["lb%d" % p], k=0.5)
+
+    def s_l1():
+        a = topo.addr(hL)
+        g.remote_dma(T.lb[:, 384:768], T.lb[:, 384:768], T.sem.ha12, T.sem.lsm, a[1], a[0], emask(topo, core, hL, 8, 8))
+        lsm[0] += 8
+
+    def s_l0():
+        lsm[0] += fan(g, T, topo, core, r, T.lb[:, 0:384], lambda d: T.sg[:, (d - 1) * 384:d * 384], T.sem.il0)
+    send(s_l1, ["lb1", "s_ip"], ["s_l1"])
+    send(s_l0, ["lb0", "s_l1"], ["s_l0"])
+    ext("il0", 24, ["s_l0"], ["ll0"], 6000.0)
+    ext("il1", 24, ["s_l1"], ["ll1"], 8000.0)
+    for p in range(2):
+        dma("G", [(T.LW[:, p * R + 512:(p + 1) * R], T.sg[:, 1152 * p:1152 * p + 1152])], ["ll%d" % p, "s_l0"],
+            ["L%dg" % p], lat=3000.0)
+        act(T.LW[:, p * R:p * R + 512], T.sg[:, 3072 + p:4096:2], F.Identity, 512, ["lou"], ["L%do%d" % (p, c) for c in range(4)])
+
+    def de(q, a, b, o0, rd, wr):
+        for p in range(2):
+            o = T.va[:, 64 * q + 32 * p:64 * q + 32 * p + 32]
+            if b is None:
+                ts(o, a[:, p:64:2], -512.0, None, A.add, None, 32, rd, [wr + str(p)])
+            else:
+                tt(o, a[:, p:64:2], b[:, p:64:2], o0, 32, rd, [wr + str(p)])
+    de(0, T.pc, None, None, ["pc"], "va0")
+    cp(T.vh[:, 0:64], T.va[:, 0:64], 64, ["va00", "va01"], ["vh0"])
+    tt(T.vl[:, 0:64], T.va[:, 0:64], T.vh[:, 0:64], A.subtract, 64, ["va00", "va01", "vh0"], ["vl0"])
+    for p in range(2):
+        dma("SA"[p], [(T.PW[h:128:16, p * R:p * R + 512], (T.vh, T.vl)[h][:, 32 * p:32 * p + 32]) for h in range(2)],
+            ["vh0", "vl0", "Pz"], ["P%do%d" % (p, c) for c in range(4)])
+    ts(T.u3[:, :], T.rc[:, :], 512.0, None, A.add, None, 64, ["pc"], ["u3"])
+    tt(T.u1[:, :], T.u3[:, :], T.pc[:, :], A.add, 64, ["u3", "pc"], ["u1"])
+    ts(T.u1[:, :], T.u1[:, :], 1023, None, A.bitwise_and, None, 64, ["u1"], ["u1"])
+    tt(T.u2[:, :], T.u3[:, :], T.u1[:, :], A.add, 64, ["u3", "u1"], ["u2"])
+    ts(T.u2[:, :], T.u2[:, :], 1023, None, A.bitwise_and, None, 64, ["u2"], ["u2"])
+    de(1, T.u1, T.pc, A.subtract, ["u1", "pc"], "va1")
+    de(2, T.u2, T.u1, A.subtract, ["u1", "u2"], "va2")
+    de(3, T.rc, None, None, ["pc"], "va3")
+    vk = ["va%d%d" % (q, p) for q in range(1, 4) for p in range(2)]
+    cp(T.vh[:, 64:256], T.va[:, 64:256], 192, vk, ["vh1"])
+    tt(T.vl[:, 64:256], T.va[:, 64:256], T.vh[:, 64:256], A.subtract, 192, vk + ["vh1"], ["vl1"])
+    for p in range(2):
+        dma("S", [(T.PW[2 * q + h:128:16, p * R:p * R + 512], (T.vh, T.vl)[h][:, 64 * q + 32 * p:64 * q + 32 * p + 32])
+                  for q in range(1, 4 - p) for h in range(2)], ["vh1", "vl1", "Pz"], ["P%dd" % p])
+
+    iota(T.ci[:, 0:1], [[1, 1]], 0, 1, 1, ["ci0"])
+    iota(T.cj[:, :], [[1, 144]], 0, -1, 144, ["cj"])
+    iota(T.tm[:, 0:128], [[1, 8], [0, 16]], 0, 0, 128, ["tm0"], True)
+    iota(T.tm[:, 128:256], [[0, 64], [1, 2]], 0, 0, 128, ["tm1"], True)
+    iota(T.msk[:, :], [[0, 32], [1, 16]], 0, 0, 512, ["msk"], True)
+    iota(T.ty[:, 0:128], [[16, 128]], 8 - 1024, 0, 128, ["ty"], True)
+    act(T.msk[:, :], T.msk[:, :], F.Sign, 512, ["msk"], ["msk"])
+    act(T.fad[:, :], T.fad[:, :], F.Identity, 1024, ["fad"], ["fad"], scale=0.125)
+    ts(T.ci[:, 1:2], T.ci[:, 0:1], 15, None, A.bitwise_and, None, 1, ["ci0"], ["ci1"])
+    ts(T.ci[:, 2:3], T.ci[:, 0:1], 4, None, A.arith_shift_right, None, 1, ["ci0"], ["ci2"])
+    cp(ct[:, 0:2], T.ci[:, 1:3], 2, ["ci1", "ci2"], ["k"])
+    kc = ct[:, 0:1]
+    ts(T.Qw[:, :], T.cj[:, :], kc, None, A.add, None, 144, ["cj", "k"], ["Qw"])
+    ts(T.BL[:, :], T.tm[:, 0:128], ct[:, 1:2], None, A.is_equal, None, 128, ["tm0", "k"], ["BL"])
+    ts(ct[:, 2:3], kc, 1.5, 4096.0, A.is_lt, A.mult, 1, ["k"], ["c2"])
+    ts(T.Wp[:, :], T.Qw[:, :], 15.0, ct[:, 2:3], A.is_equal, A.mult, 144, ["Qw", "c2"], ["Wp"])
+    ts(ct[:, 7:8], kc, 1.5, -4096.0, A.is_lt, A.mult, 1, ["k"], ["c7"])
+    act(T.NG[:, :], T.BL[:, :], F.Identity, 128, ["BL", "c7"], ["NG"], scale=ct[:, 7:8])
+    ts(T.ci[:, 16:144], T.cj[:, 0:128], 15, None, A.bitwise_and, None, 128, ["cj"], ["ci3"])
+    ts(T.Bo[:, :], T.BL[:, :], 1.0, 100.0, A.subtract, A.mult, 128, ["BL"], ["Bo"])
+    tt(T.Am[:, :], T.ci[:, 16:144], T.Bo[:, :], A.add, 128, ["ci3", "Bo"], ["Am"])
+    Ip = B[0][:, 0:128]
+    ts(Ip, T.Am[:, :], 0.0, None, A.is_equal, None, 128, ["Am"], ["M0"], [0])
+    act(T.If[:, :], Ip, F.Identity, 128, ["M0"], ["If"], [0])
+    cp(T.Ih[:, :], Ip, 128, ["M0"], ["Ih"], [0])
+    iota(T.ty[:, 128:136], [[1, 8]], 1, 0, 8, ["I8"], True)
+    ts(ct[:, 9:17], T.ty[:, 128:136], kc, 15.5, A.add, A.is_ge, 8, ["k", "I8"], ["bs"])
+    ts(ct[:, 9:17], ct[:, 9:17], -0.5, None, A.add, None, 8, ["bs"], ["bs"])
+    for d in range(1, 9):
+        o = T.Df[:, 128 * (d - 1):128 * d]
+        ts(o, T.Am[:, :], 16.0 - d, None, A.is_equal, None, 128, ["Am"], ["Df%d" % d])
+        tt(o, Ip, o, A.subtract, 128, ["M0", "Df%d" % d], ["Df%d" % d], [0])
+        h, j = divmod(d - 1, 4)
+        mm([(B[2 + h][:, 128 * j:128 * j + 128], o if d < 8 else T.Ih[:, :], T.Ih[:, :])], 128, ["Df%d" % d, "Ih"], ["D%d" % d], [2 + h])
+    for h in range(2):
+        act(T.Rk[:, 512 * h:512 * h + 512], B[2 + h][:, :], F.Identity, 512, ["D%d" % (4 * h + j + 1) for j in range(4)],
+            ["Rk%d" % h], [2 + h], scale=32.0)
+    ts(T.Wc[:, :], T.Qw[:, :], 15.0, None, A.is_equal, None, 144, ["Qw"], ["Wc"])
+    ts(T.W1[:, :], T.Qw[:, :], 14.0, None, A.is_equal, None, 144, ["Qw"], ["W1"])
+    tt(T.W1[:, :], T.Wc[:, :], T.W1[:, :], A.subtract, 144, ["Wc", "W1"], ["W1"])
+    ts(T.W64[:, :], T.W1[:, :], 64.0, None, A.mult, None, 144, ["W1"], ["W64"])
+    ts(T.Z1[:, :], T.Qw[:, 0:128], 0.0, None, A.is_equal, None, 128, ["Qw"], ["Z1"])
+    ts(T.Z64[:, :], T.Qw[:, 0:128], 0.0, 64.0, A.is_equal, A.mult, 128, ["Qw"], ["Z64"])
+    ts(ct[:, 3:4], kc, 0.0, None, A.is_equal, None, 1, ["k"], ["c3"])
+    act(T.Wt[:, :], T.Wc[:, :], F.Identity, 144, ["Wc", "c3"], ["Wt"], scale=ct[:, 3:4])
+    ts(ct[:, 4:5], kc, 1.0, 4160.0, A.add, A.mult, 1, ["k"], ["c4"])
+    ts(ct[:, 5:6], kc, 15.0, -(65.0 * 7680 + 16 * 4160.0), A.is_equal, A.mult, 1, ["k"], ["c5"])
+    tt(ct[:, 4:5], ct[:, 4:5], ct[:, 5:6], A.add, 1, ["c4", "c5"], ["c4"])
+    ts(ct[:, 5:6], ct[:, 4:5], -float(R), None, A.add, None, 1, ["c4"], ["c5"])
+    ts(ct[:, 6:7], ct[:, 3:4], 16.0, kc, A.mult, A.add, 1, ["c3", "k"], ["c6"])
+    act(T.cb[:, 0:1], ct[:, 6:7], F.Sigmoid, 1600, ["c6"], ["cb"], bias=-40.0 * LN2, scale=LN2)
+    ts(T.FW[:, 0:128], T.BL[:, :], T.cb[:, 0:1], 2.0 ** 59, A.mult, A.mult, 128, ["BL", "cb"], ["FW0"])
+    ts(T.FW[:, 128:256], T.BL[:, :], ct[:, 3:4], 2.0 ** 19, A.mult, A.mult, 128, ["BL", "c3"], ["FW1"])
+    act(T.I4[:, :], T.If[:, :], F.Identity, 128, ["If"], ["I4"], scale=4096.0)
+    ts(T.jc[:, :], T.ty[:, 0:128], kc, None, A.add, None, 128, ["ty", "k"], ["jc"])
+    ts(T.slf[:, :], T.ty[:, 0:32], kc, 1016.0, A.add, A.add, 32, ["ty", "k"], ["slf"])
+    ts(T.slf[:, :], T.slf[:, :], 2.0, None, A.mult, None, 32, ["slf"], ["slf"])
+    tt(T.Bo[:, :], T.BL[:, :], T.tm[:, 128:256], A.mult, 128, ["BL", "tm1"], ["Bo"])
+    ts(T.SA[:, :], T.Bo[:, :], 0.5, None, A.mult, None, 128, ["Bo"], ["SA"])
+    ts(ct[:, 20:21], kc, 1.5, None, A.is_lt, None, 1, ["k"], ["r0"])
+    ts(ct[:, 21:22], kc, 3.5, None, A.is_lt, None, 1, ["k"], ["r1"])
+    ts(ct[:, 22:23], kc, 5.5, ct[:, 21:22], A.is_lt, A.subtract, 1, ["k", "r1"], ["r2"])
+    ts(ct[:, 25:26], kc, 5.5, None, A.is_lt, None, 1, ["k"], ["r5"])
+    ts(ct[:, 23:24], kc, 7.5, ct[:, 25:26], A.is_lt, A.subtract, 1, ["k", "r5"], ["r3"])
+    ts(ct[:, 24:25], kc, 1.0, None, A.is_equal, None, 1, ["k"], ["r4"])
+    for j in range(4):
+        act(T.SB[:, 128 * j:128 * j + 128], T.Bo[:, :], F.Identity, 128, ["Bo", "r%d" % j], ["SB%d" % j],
+            scale=ct[:, 20 + j:21 + j])
+    ts(T.tm[:, 0:128], T.Bo[:, :], -2.0, None, A.mult, None, 128, ["Bo"], ["tm0"])
+    tt(T.tm[:, 0:128], T.tm[:, 0:128], T.BL[:, :], A.add, 128, ["tm0", "BL"], ["tm0"])
+    act(T.SB[:, 512:640], T.tm[:, 0:128], F.Identity, 128, ["tm0", "r4"], ["SB4"], scale=ct[:, 24:25])
+    for c in range(4):
+        op("V", lambda c=c: V.memset(T.xx[:, c * XW:c * XW + 8], 0.0), vc(8), [], ["xz%d" % c])
+
+    Z = B[7][:, 256:512]
+
+    def decode(p):
+        for h in range(2):
+            e = T.nbr[:, 512 * h + p:512 * h + 512:2]
+            hs = slice(256 * h, 256 * h + 256)
+            ps_ = slice(512 * p + 256 * h, 512 * p + 256 * h + 256)
+            ek, k = "nb%d" % p, "%d%d" % (p, h)
+            ts(T.t1[:, hs], e, 1, 2047, A.arith_shift_right, A.bitwise_and, 256, [ek], ["t1%d" % h])
+            ts(T.t2[:, hs], e, 1, None, A.bitwise_and, None, 256, [ek], ["t2%d" % h])
+            ts(Z, T.t2[:, hs], float(R - 2 * R * p), float(R * p), A.mult, A.add, 256, ["t2%d" % h], ["Z"], [7])
+            tt(T.pp[:, hs], Z, T.t1[:, hs], A.add, 256, ["Z", "t1%d" % h], ["pp%d" % h], [7])
+            cp(T.ua[:, ps_], T.pp[:, hs], 256, ["pp%d" % h], ["ua" + k])
+            ts(T.hi[:, ps_], T.pp[:, hs], 6, None, A.arith_shift_right, None, 256, ["pp%d" % h], ["hi" + k])
+            ts(T.lo[:, ps_], T.pp[:, hs], 63, None, A.bitwise_and, None, 256, ["pp%d" % h], ["lo" + k])
+
+    decode(0)
+    decode(1)
+
+    for t in range(5):
+        p = t & 1
+        Lk = ["L%d%s" % (q, s) for q in (t, t + 1) for s in ("o0", "o1", "o2", "o3", "g")]
+        Pk = ["P%d%s" % (q, s) for q in (t, t + 1) for s in ("o0", "o1", "o2", "o3", "g")] + ["P0d", "P1d"] * (t < 2)
+        Pk = [k for k in Pk if not (t == 1 and k == "P0d")]
+        Lwin, Pwin = T.LW[:, t * R:(t + 2) * R], T.PW[:, t * R:(t + 2) * R]
+        for c in range(4):
+            b = c & 1
+            cs = slice(128 * c, 128 * c + 128)
+            pcs = slice(512 * p + 128 * c, 512 * p + 128 * c + 128)
+            bs = slice(128 * b, 128 * b + 128)
+            own = slice(t * R + 128 * c, t * R + 128 * c + 128)
+            new = slice((t + 2) * R + 128 * c, (t + 2) * R + 128 * c + 128)
+            sb_ = str(b)
+            sc = str(c)
+            hk = "%d%d" % (p, c // 2)
+            tg = 1 + 25 * t + 6 * c
+            tag[0] = tg
+            for h in range(2):
+                o = 512 * p + 128 * c + 64 * h
+                act(T.pg[:, 2048 * b + 1024 * h:2048 * b + 1024 * h + 1024], Pwin.indirect(T.ua[:, o:o + 64]), F.Identity, 1024,
+                    Pk + ["ua" + hk], ["pg%d%d" % (b, h)], k=GA)
+            tag[0] = tg + 1
+            Tp = B[4][:, bs]
+            mm([(Tp, T.Wp[:, 15 - k:143 - k], T.pg[:, 2048 * b + k:2048 * b + 2048:16]) for k in range(16)]
+               + [(Tp, T.NG[:, :], T.PW[:, own])], 17 * 128, ["pg%d0" % b, "pg%d1" % b, "Wp", "NG", "P%do%d" % (t, c)], ["T" + sb_], [4])
+            tt(T.Ti[:, bs], Tp, T.nbr[:, 256 * c + p:256 * c + 256:2], A.add, 128, ["T" + sb_, "nb%d" % p], ["Ti" + sb_], [4])
+            ts(T.ai[:, bs], T.Ti[:, bs], 12, 1023, A.arith_shift_right, A.bitwise_and, 128, ["Ti" + sb_], ["ai" + sb_])
+            ts(T.ac[:, cs], T.ai[:, bs], -512.0, None, A.add, None, 128, ["ai" + sb_], ["ac" + sc])
+            for h in range(2):
+                for j in range(4):
+                    d = 4 * h + j + 1
+                    mm([(B[2 + h][:, 128 * j:128 * j + 128], T.Df[:, 128 * (d - 1):128 * d], T.ac[:, cs])], 128,
+                       ["ac" + sc, "Df%d" % d], ["D%d" % d], [2 + h])
+                for j in range(4):
+                    d = 4 * h + j + 1
+                    o = 1024 * b + 128 * (d - 1)
+                    act(T.Sd[:, o:o + 128], B[2 + h][:, 128 * j:128 * j + 128], F.Sign, 128, ["D%d" % d, "bs"],
+                        ["Sd%d%d" % (b, d)], [2 + h], bias=ct[:, 8 + d:9 + d])
+            Rp = B[5][:, bs]
+            mm([(Rp, T.Rk[:, 128 * j:128 * j + 128], T.Sd[:, 1024 * b + 128 * j:1024 * b + 128 * j + 128]) for j in range(8)],
+               8 * 128, ["Sd%d%d" % (b, d) for d in range(1, 9)] + ["Rk0", "Rk1"], ["R" + sb_], [5])
+            mo = 4096 * b
+            tt(T.mm[:, mo:mo + 128], Rp, T.hi[:, pcs], A.add, 128, ["R" + sb_, "hi" + hk], ["wh" + sb_], [5])
+            tt(T.mm[:, mo + 128:mo + 256], Rp, T.lo[:, pcs], A.add, 128, ["R" + sb_, "lo" + hk], ["wl" + sb_], [5])
+            act(T.p2[:, cs], Rp, F.Sigmoid, 128, ["R" + sb_], ["p2" + sc], [5], bias=-27.5 * LN2, scale=-LN2 / 64)
+            for s in range(1, 16):
+                ts(T.mm[:, mo + 256 * s:mo + 256 * s + 256], T.mm[:, mo:mo + 256], 64.0 * s - 480, None, A.max, None, 256,
+                   ["wh" + sb_, "wl" + sb_], ["m%d_%d" % (b, s)], k=0.5)
+            Op = B[4][:, 256 + 128 * b:384 + 128 * b]
+            its = [(Op, T.Z64[:, :], T.mm[:, mo:mo + 128]), (Op, T.Z1[:, :], T.mm[:, mo + 128:mo + 256])]
+            for s in range(1, 16):
+                o = mo + 256 * s
+                its += [(Op, T.W64[:, 15 - s:143 - s], T.mm[:, o:o + 128]), (Op, T.W1[:, 15 - s:143 - s], T.mm[:, o + 128:o + 256])]
+            mm(its, 32 * 128, ["wh" + sb_, "wl" + sb_, "Z1", "Z64", "W1", "W64"] + ["m%d_%d" % (b, s) for s in range(1, 16)],
+               ["O" + sb_], [4])
+            ts(T.us[:, cs], Op, ct[:, 4:5], None, A.add, None, 128, ["O" + sb_, "c4"], ["us" + sc], [4])
+            if t < 3:
+                act(T.cp[:, cs], Op, F.Identity, 128, ["O" + sb_, "c5"], ["cp" + sc], [4], bias=ct[:, 5:6])
+            tag[0] = tg + 2
+            xo = c * XW + 8
+            do = 2048 * c
+            for h in range(2):
+                xk, dk = "x%d%d" % (c, h), "d%d%d" % (c, h)
+                act(T.xx[:, xo + 1024 * h:xo + 1024 * h + 1024], Lwin.indirect(T.us[:, 128 * c + 64 * h:128 * c + 64 * h + 64]),
+                    F.Identity, 1024, Lk + ["us" + sc], [xk], k=GA)
+                for j in range(2):
+                    o = 1024 * h + 512 * j
+                    M = B[j]
+                    op("V", lambda M=M, o=o, xo=xo: V.tensor_tensor_scan(M[:, :], T.xx[:, xo + o - 1:xo + o + 511], T.msk[:, :],
+                                                                        0.0, A.max, A.mult), vc(512),
+                       [xk, "msk", "xz" + sc] + ["x%d0" % c] * h, ["M%d" % j], [j])
+                    tt(T.dd[:, do + o:do + o + 512], T.xx[:, xo + o:xo + o + 512], M[:, :], A.subtract, 512,
+                       [xk, "M%d" % j], [dk + str(j)], [j])
+                    if t < 4:
+                        q = 2 * h + j
+                        tt(B[5][:, 384 + 32 * q:416 + 32 * q], T.xx[:, xo + o + 15:xo + o + 512:16], M[:, 15:512:16], A.max, 32,
+                           [xk, "M%d" % j], ["X%d" % q], [j, 5])
+                act(T.sg[:, 2048 * b + 1024 * h:2048 * b + 1024 * h + 1024], T.dd[:, do + 1024 * h:do + 1024 * h + 1024], F.Sign,
+                    1024, [dk + "0", dk + "1"], ["sg%d%d" % (b, h)] + ["los", "lou", "ll0", "ll1"] * (t + c + h == 0), bias=-1e-9)
+            if t < 4:
+                X = B[5][:, 384:512]
+                Xk = ["X%d" % q for q in range(4)]
+                ok = "L%do%d" % (t, c)
+                tt(X, X, T.LW[:, own], A.subtract, 128, Xk + [ok], Xk, [5])
+                act(T.L8[:, cs], T.LW[:, own], F.Identity, 128, [ok], ["L8" + sc], scale=8.0)
+                tt(X, X, T.L8[:, cs], A.add, 128, Xk + ["L8" + sc], Xk, [5])
+                tt(T.LW[:, new], X, T.fad[:, 256 * c + p:256 * c + 256:2], A.mult, 128, Xk + ["fad"], ["L%do%d" % (t + 2, c)], [5])
+            tag[0] = tg + 3
+            Cp = B[6][:, 0:128]
+            mm([(Cp, T.Wc[:, 15 - s:143 - s], T.sg[:, 2048 * b + s:2048 * b + 2048:16]) for s in range(16)], 16 * 128,
+               ["sg%d0" % b, "sg%d1" % b, "Wc"], ["C"], [6])
+            act(T.fs[:, bs], Cp, F.Sign, 128, ["C"], ["fs" + sb_], [6], bias=11.0)
+            Fp = B[5][:, 256:384]
+            mm([(Fp, T.FW[:, 0:128], T.fs[:, bs]), (Fp, T.FW[:, 128:256], T.fs[:, bs])], 256, ["fs" + sb_, "FW0", "FW1"], ["F"], [5])
+            tt(T.yy[:, cs], Fp, T.p2[:, cs], A.mult, 128, ["F", "p2" + sc], ["yy" + sc], [5])
+            act(T.ls[:, bs], T.yy[:, cs], F.Abs, 128, ["yy" + sc], ["ls" + sb_], bias=-1.5)
+            act(Fp, T.ls[:, bs], F.Sign, 128, ["ls" + sb_], ["F"], [5], bias=0.5, scale=-1.0)
+            tt(T.la[:, bs], Fp, T.ac[:, cs], A.mult, 128, ["F", "ac" + sc], ["la" + sb_], [5])
+            base = slice(p * R + 128 * c, p * R + 128 * c + 128)
+
+            def sm(o):
+                its = [(o, T.SA[:, :], T.la[:, bs]), (o, T.SA[:, :], T.ac[:, cs])]
+                if t < 2:
+                    return its + [(o, T.SB[:, 128:256], T.PW[:, own])]
+                j = 1 + t // 2
+                return its + [(o, T.SB[:, 0:128], T.PW[:, own]), (o, T.SB[:, 128 * j:128 * j + 128], T.PW[:, base])]
+            sk = ["la" + sb_, "ac" + sc, "SA", "SB0", "SB1", "SB2", "SB3", "P%do%d" % (t, c), "P%dd" % p, "P%do%d" % (p, c)]
+            S1, S2 = B[6][:, 128:256], B[6][:, 256:384]
+            mm(sm(S1), 384, sk, ["S1"], [6])
+            if t < 4:
+                act(T.Ht[:, bs], S1, F.Identity, 128, ["S1"], ["Ht" + sb_], [6])
+                mm(sm(S2) + [(S2, T.SB[:, 512:640], T.Ht[:, bs])], 512, sk + ["Ht" + sb_, "SB4"], ["S2"], [6])
+                act(T.PW[:, new], S2, F.Identity, 128, ["S2"], ["P%do%d" % (t + 2, c)], [6])
+            if t >= 3:
+                ts(T.t1[:, cs], S1, 512.0, None, A.add, None, 128, ["S1"], ["t1%d" % (c // 2), "y1" + sc], [6])
+                ts(T.t2[:, cs], T.t1[:, cs], 1023, None, A.bitwise_and, None, 128, ["y1" + sc], ["t2%d" % (c // 2), "y2" + sc])
+                cp(T.LW[:, 256 * c + p:256 * c + 256:2], T.t2[:, cs], 128, ["y2" + sc],
+                   ["yo%d%d" % (p, c)] + ["L0o0", "L0o1", "L0o2", "L0o3", "L0g"] * (t == 3 and c == 0))
+            if t < 4 and c < 3:
+                q = 3 * t + c
+                for kind, hc, hb, win, lo_, ne in (("L", hL, T.hbL, T.LW, 8, 8), ("P", hP, T.hbP, T.PW, 0, 4)):
+                    def s_h(hc=hc, hb=hb, win=win, lo_=lo_, ne=ne, q=q, new=new):
+                        g.remote_dma_fused([RemoteDMATransfer(
+                            dst_ids=[did(topo, hc), did(topo, hc)], dma_engine_mask=emask(topo, core, hc, lo_, ne),
+                            remote_sem=T.sem["ha%d" % q], srcs=[win[:, new]],
+                            dsts=[hb[256 * q:256 * q + 128, :], hb[256 * q + 128:256 * q + 256, :]])], local_sem=T.sem.lsm)
+                        lsm[0] += ne
+                    send(s_h, ["%s%do%d" % (kind, t + 2, c)], ["s%s%d" % (kind, q)])
+            Up = B[6][:, 384:512]
+            mm([(Up, T.I4[:, :], T.fs[:, bs]), (Up, T.Ih[:, :], T.jc[:, :])], 256, ["fs" + sb_, "I4", "Ih", "jc"], ["U"], [6])
+            ts(T.um[:, cs], Up, -3072.0, None, A.add, None, 128, ["U"], ["um" + sc], [6])
+            for h in range(2):
+                tag[0] = tg + 4 + h
+                dk = ["d%d%d0" % (c, h), "d%d%d1" % (c, h)]
+                dv = T.dd[:, do + 1024 * h:do + 1024 * h + 1024]
+                act(dv, dv, F.Sigmoid, 1024, dk, dk)
+                tt(T.tt[:, 1024 * h:1024 * h + 1024],
+                   T.xx[:, c * XW:(c + 1) * XW].indirect(T.um[:, 128 * c + 64 * h:128 * c + 64 * h + 64]), dv, A.mult, 1024,
+                   dk + ["x%d0" % c, "x%d1" % c, "xz" + sc, "um" + sc], ["tt%d" % h], k=GA)
+                Ep = B[7][:, 64 * h:64 * h + 64]
+                ev = T.EE[:, 256 * c + 128 * h + p:256 * c + 128 * h + 128:2]
+                ek = "E%d%d%d" % (p, c, h)
+                its = [(Ep, T.If[:, :], T.tt[:, 1024 * h + s:1024 * h + 1024:16]) for s in range(16)] + [(Ep, T.If[:, :], ev)] * (t >= 2)
+                mm(its[:8], 8 * 256, ["tt%d" % h, "If"], ["Ep%d" % h, "Eg"], [7], last=False)
+                mm(its[8:], len(its[8:]) * 256, ["tt%d" % h, "If", "Ep%d" % h] + [ek] * (t >= 2), ["Ep%d" % h, "Eg"], [7], first=False)
+                act(ev, Ep, F.Identity, 64, ["Ep%d" % h], [ek], [7])
+            if t == 4:
+                dma("S", [(T.ye[:, 256 * c:256 * c + 256], T.EE[:, 256 * c:256 * c + 256])],
+                    ["E%d%d%d" % (a, c, h) for a in range(2) for h in range(2)], ["ye" + sc])
+        if t < 4:
+            ext("al%d" % t, 72, ["sL%d" % (3 * t + c) for c in range(3)], ["L%dg" % (t + 2)], 7000.0)
+            ext("ap%d" % t, 72, ["sP%d" % (3 * t + c) for c in range(3)], ["P%dg" % (t + 2)], 6000.0)
+        if t < 3:
+            tag[0] = 25 * t + 25
+            Cq = B[7][:, 128:160]
+            mm([(Cq, T.Wt[:, 15 - j:143 - j], T.cp[:, j:512:16]) for j in range(16)], 16 * 256,
+               ["cp%d" % c for c in range(4)] + ["Wt"], ["Cq", "Eg"], [7])
+            a0, a1, a2 = T.ty[:, 0:32], T.ty[:, 32:64], T.ty[:, 64:96]
+            ts(a0, Cq, 0.0, -float(R), A.is_ge, A.mult, 32, ["Cq"], ["ty", "a0"], [7])
+            ts(a1, Cq, 0.0, 1.0 - 2 * p, A.is_ge, A.mult, 32, ["Cq"], ["ty", "a1"], [7])
+            tt(a0, Cq, a0, A.add, 32, ["Cq", "a0"], ["a0"], [7])
+            ts(a2, a0, float(R), 2.0, A.add, A.mult, 32, ["a0"], ["ty", "a2"])
+            tt(a1, a1, T.slf[:, :], A.subtract, 32, ["a1", "slf"], ["a1"])
+            ts(a0, a0, 511.5 - R, None, A.is_lt, None, 32, ["a0"], ["a0"])
+            tt(a1, a1, a2, A.add, 32, ["a1", "a2"], ["a1"])
+            tt(a2, a1, a0, A.mult, 32, ["a0", "a1"], ["a2"])
+            tt(a2, a2, T.slf[:, :], A.add, 32, ["a2", "slf"], ["a2"])
+            ts(T.ul[:, :], a2, float(p), None, A.add, None, 32, ["a2"], ["ul"])
+            mk = "nb%d" % p
+            act(T.go[:, :], T.nbr[:, :].indirect(T.ul[:, :]), F.Identity, 512, ["ul", "nb0", "nb1"], ["go"], k=GA)
+            ts(T.t1[:, :], T.yy[:, :], 0.5, None, A.add, None, 512, ["yy%d" % c for c in range(4)], ["t10", "t11"])
+            ts(T.t2[:, :], T.t1[:, :], 1, None, A.bitwise_and, None, 512, ["t10", "t11"], ["t20", "t21"])
+            for h in range(2):
+                hs = slice(256 * h, 256 * h + 256)
+                e = T.nbr[:, 512 * h + p:512 * h + 512:2]
+                tt(Z, T.go[:, hs], e, A.subtract, 256, ["go", mk], ["Z"], [7], k=2.0)
+                tt(Z, Z, T.t2[:, hs], A.mult, 256, ["Z", "t2%d" % h], ["Z"], [7])
+                tt(e, Z, e, A.add, 256, ["Z", mk], [mk], [7])
+            decode(p)
+    dma("S", [(T.yp[:, :], T.LW[1:128:16, 0:1024])], ["yo%d%d" % (a, c) for a in range(2) for c in range(4)], ["yp"])
+    return ops, lsm
+
+
+def schedule(ops):
+    n = len(ops)
+    deps = [set() for _ in range(n)]
+    lw, rd = {}, {}
+    for i, o in enumerate(ops):
+        for k in o["r"]:
+            if k in lw:
+                deps[i].add(lw[k])
+        for k in o["w"]:
+            if k in lw:
+                deps[i].add(lw[k])
+            deps[i].update(rd.get(k, ()))
+        deps[i].discard(i)
+        for k in o["r"]:
+            rd.setdefault(k, []).append(i)
+        for k in o["w"]:
+            lw[k] = i
+            rd[k] = []
+    suc = [[] for _ in range(n)]
+    for i in range(n):
+        for j in deps[i]:
+            suc[j].append(i)
+    bl = [0.0] * n
+    for i in range(n - 1, -1, -1):
+        bl[i] = ops[i]["c"] + ops[i]["lat"] + 150.0 + max([bl[j] for j in suc[i]] + [0.0])
+
+    def place(pred, succ, pri, back):
+        left = [len(d) for d in pred]
+        ready = [i for i in range(n) if left[i] == 0]
+        st, rt, busy = [0.0] * n, [0.0] * n, {}
+        while ready:
+            i = max(ready, key=lambda x: pri[x])
+            ready.remove(i)
+            o = ops[i]
+            e, c, s = o["e"], o["c"], rt[i]
+            res = ([(e, 0.0)] if e != "X" else []) + [(b, XL) for b in o["b"]]
+            moved = True
+            while moved:
+                moved = False
+                for k, pad in res:
+                    iv = busy.setdefault(k, [])
+                    lo, hi = 0, len(iv)
+                    while lo < hi:
+                        m = (lo + hi) // 2
+                        if iv[m][0] < s - 4000.0:
+                            lo = m + 1
+                        else:
+                            hi = m
+                    while lo < len(iv) and iv[lo][0] < s + c + pad:
+                        if iv[lo][1] + pad > s and (pad == 0.0 or iv[lo][2] != e):
+                            s = iv[lo][1] + pad
+                            moved = True
+                        lo += 1
+            for k, pad in res:
+                iv = busy[k]
+                m = len(iv)
+                while m > 0 and iv[m - 1][0] > s:
+                    m -= 1
+                iv.insert(m, (s, s + c, e))
+            st[i] = s
+            for j in succ[i]:
+                left[j] -= 1
+                rt[j] = max(rt[j], s + c + ops[j if back else i]["lat"] + (SL if ops[j]["e"] == e else XL))
+                if left[j] == 0:
+                    ready.append(j)
+        return [st[i] + ops[i]["c"] for i in range(n)]
+
+    arr = [i for i in range(n) if ops[i]["e"] == "X"]
+
+    def measure(end):
+        return max(end[i] + ops[i]["lat"] for i in range(n)) + 0.05 * sum(end[i] for i in arr)
+
+    best, pri = None, [bl[i] + 100.0 * OFF[ops[i]["tag"]] for i in range(n)]
+    for _ in range(ITER):
+        end = place(deps, suc, pri, False)
+        span = measure(end)
+        if best is None or span < best[0]:
+            best = (span, end)
+        pri = place(suc, deps, [end[i] + ops[i]["lat"] for i in range(n)], True)
+    seed = [SEED]
+
+    def rnd():
+        seed[0] = (seed[0] * 1103515245 + 12345) % 2147483648
+        return seed[0] / 2147483648.0
+    cur = best
+    for _ in range(TRIES):
+        a = ops[int(rnd() * n)]
+        dl = (rnd() - 0.5) * (3000.0, 12000.0)[rnd() < 0.5]
+        one = rnd() < 0.5
+        pri = [ops[i]["c"] - cur[1][i] + (dl if ops[i]["tag"] == a["tag"] and (not one or ops[i]["e"] == a["e"]) else 0.0)
+               for i in range(n)]
+        end = place(deps, suc, pri, False)
+        if rnd() < 0.1:
+            end = place(deps, suc, place(suc, deps, [end[i] + ops[i]["lat"] for i in range(n)], True), False)
+        span = measure(end)
+        if span <= cur[0] + HEAT * rnd():
+            cur = (span, end)
+            if span < best[0]:
+                best = cur
+    end = best[1]
+    order = sorted(range(n), key=lambda i: (end[i] - ops[i]["c"], end[i], i))
+    bank = {}
+    for i in order:
+        for b in ops[i]["b"]:
+            for e, j in bank.get(b, {}).items():
+                if e != ops[i]["e"]:
+                    deps[i].add(j)
+            bank.setdefault(b, {})[ops[i]["e"]] = i
+    return order, deps, [end[i] + ops[i]["lat"] for i in range(n)]
+
+
+def rank_program(g, core, T, topo):
+    r = T.rank_of(core)
+    if r is None:
+        for q, c in enumerate(T.cores):
+            hP, hL = helpers(c, T, topo)
+            if core == hP:
+                helper_program(g, core, T, topo, q, "P")
+            if core == hL:
+                helper_program(g, core, T, topo, q, "L")
+        return
+    ops, lsm = build(g, core, T, topo, r)
+    if "s" not in CACHE:
+        CACHE["s"] = schedule(ops)
+    order, deps, fin = CACHE["s"]
+    Q = {"V": g.vector, "A": g.scalar, "P": g.tensor, "G": g, "S": g.sync}
+    know = {e: {} for e in Q}
+    cnt = {e: 0 for e in Q}
+    tok, snap = {}, {}
+    for i in order:
+        o = ops[i]
+        e = o["e"]
+        if e == "X":
+            tok[i], snap[i] = o["tok"], {}
+            continue
+        kn = know[e]
+        need = {}
+        for j in deps[i]:
+            if tok[j] is not None and kn.get(tok[j][0], 0) < tok[j][1] and need.get(tok[j][0], (0, 0))[0] < tok[j][1]:
+                need[tok[j][0]] = (tok[j][1], j)
+        for s, (v, j) in sorted(need.items(), key=lambda x: -fin[x[1][1]]):
+            if kn.get(s, 0) < v:
+                Q[e].wait_ge(T.sem[s], v)
+                kn[s] = v
+                for s2, v2 in snap[j].items():
+                    if kn.get(s2, 0) < v2:
+                        kn[s2] = v2
+        snap[i] = dict(kn)
+        ins = o["fn"]()
+        if o["tok"] is None:
+            cnt[e] += 1
+            ins.then_inc(T.sem["c" + e], 1)
+            tok[i] = ("c" + e, cnt[e])
+        else:
+            tok[i] = None if o["tok"] == "none" else o["tok"]
+    last = {}
+    for t in tok.values():
+        if t is not None:
+            last[t[0]] = max(last.get(t[0], 0), t[1])
+    g.wait_ge(T.sem.lsm, lsm[0])
+    for s, v in last.items():
+        if know["S"].get(s, 0) < v:
+            g.sync.wait_ge(T.sem[s], v)

@@ -4,6 +4,7 @@ from concourse.mybir import AluOpType as A, ActivationFunctionType as F
 
 R = 1664
 XW = 2056
+NT = 4
 LN2 = math.log(2.0)
 f32, bf, f16, i32, u16 = "float32", "bfloat16", "float16", "int32", "uint16"
 
@@ -14,25 +15,26 @@ def sb(n, t):
 
 SCRATCH = {
     "LW": sb(6 * R, f32), "PW": sb(6 * R, bf), "xx": sb(4 * XW, f32), "dd": sb(8192, f32),
-    "sg": sb(4096, bf), "pg": sb(4096, bf), "tt": sb(2048, f32), "mm": sb(8192, f16),
-    "L8": sb(512, f32), "nbr": sb(1024, i32), "EE": sb(1024, f32),
+    "sg": sb(4096, bf), "pg": sb(4096, bf), "tt": sb(NT * 1024, f32), "mm": sb(8192, f16),
+    "uu": sb(256, f32), "nbr": sb(1024, i32), "EE": sb(1024, f32),
     "fad": sb(1024, bf), "lb": sb(768, bf),
     "hi": sb(1024, i32), "lo": sb(1024, i32), "ua": sb(1024, u16), "us": sb(512, u16), "um": sb(512, u16),
-    "pp": sb(512, i32), "t1": sb(512, i32), "t2": sb(512, i32), "Ti": sb(256, i32), "ai": sb(256, i32),
+    "t1": sb(512, i32), "t2": sb(512, i32), "Ti": sb(256, i32), "ai": sb(256, i32),
     "ac": sb(512, f16), "Sd": sb(2048, bf), "p2": sb(512, bf), "fs": sb(256, bf), "yy": sb(512, f32),
-    "ls": sb(256, f32), "la": sb(256, f16), "Ht": sb(256, bf), "cp": sb(512, f32), "go": sb(512, f32),
-    "msk": sb(512, bf), "jc": sb(128, f16), "ul": sb(32, u16), "ty": sb(256, f32),
+    "ls": sb(256, f32), "la": sb(256, f16), "Ht": sb(256, bf), "hq": sb(256, bf), "cp": sb(512, f16), "go": sb(512, f32),
+    "msk": sb(512, bf), "jc": sb(128, f16), "kk": sb(128, f16), "ul": sb(32, u16), "su": sb(64, u16), "ty": sb(256, f32),
     "pc": sb(64, i32), "rc": sb(64, i32), "ps": sb(48, i32), "u1": sb(64, i32), "u2": sb(64, i32), "u3": sb(64, i32),
     "va": sb(256, f32), "vh": sb(256, bf), "vl": sb(256, bf), "vs": sb(48, f32), "cs": sb(96, bf), "pl": sb(288, bf),
     "ci": sb(160, i32), "cj": sb(144, i32), "ct": sb(48, f32), "cb": sb(8, bf), "Qw": sb(144, f32), "BL": sb(128, f32),
     "Am": sb(128, f32), "Bo": sb(128, f32), "tm": sb(256, f32), "slf": sb(32, f32),
-    "Wc": sb(144, bf), "W1": sb(144, f16), "W64": sb(144, f16), "Z1": sb(128, f16), "Z64": sb(128, f16),
-    "Wp": sb(144, bf), "Wt": sb(144, f32), "NG": sb(128, bf), "Df": sb(1024, f16), "Rk": sb(1024, bf),
+    "Wc": sb(144, bf), "W1": sb(144, f16), "W64": sb(144, f16), "Z1": sb(128, f16), "Z64": sb(128, f16), "I8": sb(128, f32),
+    "Wp": sb(144, bf), "Wt": sb(144, f16), "NG": sb(128, bf), "Df": sb(1024, f16), "Rk": sb(1024, bf),
     "FW": sb(256, bf), "I4": sb(128, bf), "Ih": sb(128, f16), "If": sb(128, f32), "SA": sb(128, f16),
     "SB": sb(640, bf),
     "hbL": ("dram", [12 * 256, 128], f32), "hbP": ("dram", [12 * 256, 128], bf),
 }
-for _i in range(8):
+SCRATCH["MM"] = ("psum", [128, 1024], f32)
+for _i in range(2, 8):
     SCRATCH["B%d" % _i] = ("psum", [128, 512], f32)
 
 SEMAPHORES = (["cV", "cA", "cP", "cG", "lsm", "ip", "il0", "il1"] + ["ha%d" % i for i in range(13)]
@@ -41,7 +43,9 @@ SEMAPHORES = (["cV", "cA", "cP", "cG", "lsm", "ip", "il0", "il1"] + ["ha%d" % i 
 CY, PCY, GA, OV = 0.83, 0.42, 1.56, 20.0
 SL, XL, ITER = 100.0, 250.0, 3
 OFF = [0] * 126
-SEED, TRIES, HEAT = 1, 1500, 200.0
+SEED, TRIES, HEAT = 2, 3500, 100.0
+WS = 0.3
+ONV = ["p001", "p301", "p401"]
 CACHE = {}
 
 
@@ -151,7 +155,7 @@ def build(g, core, T, topo, r):
     def ext(sem, cnt, rd, wr, lat):
         op("X", None, 0.0, rd, wr, tok=(sem, cnt), lat=lat)
 
-    B = [T["B%d" % i] for i in range(8)]
+    B = [T.MM, T.MM] + [T["B%d" % i] for i in range(2, 8)]
     ct = T.ct
 
     dma("S", [(T.ps[0:112, :], T.ph0[1:8, 0:768]), (T.ps[112:128, :], T.ph0[0:1, 0:768])], [], ["ps"])
@@ -159,7 +163,9 @@ def build(g, core, T, topo, r):
     dma("S", [(T.pc[:, :], T.ph0[:, :]), (T.rc[:, :], T.rb[:, :])], [], ["pc"])
     dma("A", [(T.sg[0:112, 2304:3072], T.loud[16:128, 0:768]), (T.sg[112:128, 2304:3072], T.loud[0:16, 0:768])], [], ["los"])
     dma("S", [(T.sg[:, 3072:4096], T.loud[:, :]), (T.fad[:, :], T.fade[:, :])], [], ["lou", "fad"])
-    op("V", lambda: V.memset(T.PW[:, 0:2 * R], 0.0), vc(2 * R, 0.5), [], ["Pz"])
+    op("V", lambda: V.memset(T.PW[:, 0:832], 0.0), vc(832, 0.5), [], ["Pz0"])
+    for j in range(1, 4):
+        act(T.PW[:, 832 * j:832 * j + 832], T.PW[:, 0:832], F.Identity, 832, ["Pz0"], ["Pz"])
 
     for p in range(2):
         ts(T.vs[:, 24 * p:24 * p + 24], T.ps[:, p:48:2], -512.0, None, A.add, None, 24, ["ps"], ["vs%d" % p])
@@ -178,7 +184,7 @@ def build(g, core, T, topo, r):
                 prs.append((T.PW[h:128:16, gcol(p, d, 0):gcol(p, d, 0) + 384], T.pl[:, o:o + 24]))
         dma("SA"[p], prs, ["pl", "Pz"], ["P%dg" % p])
     for p in range(2):
-        cp(T.lb[:, 384 * p:384 * p + 384], T.sg[:, 2304 + p:3072:2], 384, ["los"], ["lb%d" % p], k=0.5)
+        act(T.lb[:, 384 * p:384 * p + 384], T.sg[:, 2304 + p:3072:2], F.Identity, 384, ["los"], ["lb%d" % p])
 
     def s_l1():
         a = topo.addr(hL)
@@ -218,7 +224,7 @@ def build(g, core, T, topo, r):
     de(2, T.u2, T.u1, A.subtract, ["u1", "u2"], "va2")
     de(3, T.rc, None, None, ["pc"], "va3")
     vk = ["va%d%d" % (q, p) for q in range(1, 4) for p in range(2)]
-    cp(T.vh[:, 64:256], T.va[:, 64:256], 192, vk, ["vh1"])
+    act(T.vh[:, 64:256], T.va[:, 64:256], F.Identity, 192, vk, ["vh1"])
     tt(T.vl[:, 64:256], T.va[:, 64:256], T.vh[:, 64:256], A.subtract, 192, vk + ["vh1"], ["vl1"])
     for p in range(2):
         dma("S", [(T.PW[2 * q + h:128:16, p * R:p * R + 512], (T.vh, T.vl)[h][:, 64 * q + 32 * p:64 * q + 32 * p + 32])
@@ -231,7 +237,6 @@ def build(g, core, T, topo, r):
     iota(T.msk[:, :], [[0, 32], [1, 16]], 0, 0, 512, ["msk"], True)
     iota(T.ty[:, 0:128], [[16, 128]], 8 - 1024, 0, 128, ["ty"], True)
     act(T.msk[:, :], T.msk[:, :], F.Sign, 512, ["msk"], ["msk"])
-    act(T.fad[:, :], T.fad[:, :], F.Identity, 1024, ["fad"], ["fad"], scale=0.125)
     ts(T.ci[:, 1:2], T.ci[:, 0:1], 15, None, A.bitwise_and, None, 1, ["ci0"], ["ci1"])
     ts(T.ci[:, 2:3], T.ci[:, 0:1], 4, None, A.arith_shift_right, None, 1, ["ci0"], ["ci2"])
     cp(ct[:, 0:2], T.ci[:, 1:3], 2, ["ci1", "ci2"], ["k"])
@@ -264,11 +269,12 @@ def build(g, core, T, topo, r):
     ts(T.Wc[:, :], T.Qw[:, :], 15.0, None, A.is_equal, None, 144, ["Qw"], ["Wc"])
     ts(T.W1[:, :], T.Qw[:, :], 14.0, None, A.is_equal, None, 144, ["Qw"], ["W1"])
     tt(T.W1[:, :], T.Wc[:, :], T.W1[:, :], A.subtract, 144, ["Wc", "W1"], ["W1"])
-    ts(T.W64[:, :], T.W1[:, :], 64.0, None, A.mult, None, 144, ["W1"], ["W64"])
     ts(T.Z1[:, :], T.Qw[:, 0:128], 0.0, None, A.is_equal, None, 128, ["Qw"], ["Z1"])
-    ts(T.Z64[:, :], T.Qw[:, 0:128], 0.0, 64.0, A.is_equal, A.mult, 128, ["Qw"], ["Z64"])
+    ts(T.W64[:, :], T.W1[:, :], 64.0, None, A.mult, None, 144, ["W1"], ["W64"], k=0.5)
+    ts(T.Z64[:, :], T.Z1[:, :], 64.0, None, A.mult, None, 128, ["Z1"], ["Z64"], k=0.5)
+    act(T.fad[:, :], T.fad[:, :], F.Identity, 1024, ["fad"], ["fad"], scale=0.125)
     ts(ct[:, 3:4], kc, 0.0, None, A.is_equal, None, 1, ["k"], ["c3"])
-    act(T.Wt[:, :], T.Wc[:, :], F.Identity, 144, ["Wc", "c3"], ["Wt"], scale=ct[:, 3:4])
+    ts(T.Wt[:, :], T.Wc[:, :], ct[:, 3:4], None, A.mult, None, 144, ["Wc", "c3"], ["Wt"], k=0.5)
     ts(ct[:, 4:5], kc, 1.0, 4160.0, A.add, A.mult, 1, ["k"], ["c4"])
     ts(ct[:, 5:6], kc, 15.0, -(65.0 * 7680 + 16 * 4160.0), A.is_equal, A.mult, 1, ["k"], ["c5"])
     tt(ct[:, 4:5], ct[:, 4:5], ct[:, 5:6], A.add, 1, ["c4", "c5"], ["c4"])
@@ -298,7 +304,7 @@ def build(g, core, T, topo, r):
     for c in range(4):
         op("V", lambda c=c: V.memset(T.xx[:, c * XW:c * XW + 8], 0.0), vc(8), [], ["xz%d" % c])
 
-    Z = B[7][:, 256:512]
+    Z = B[4][:, 256:512]
 
     def decode(p):
         for h in range(2):
@@ -308,11 +314,11 @@ def build(g, core, T, topo, r):
             ek, k = "nb%d" % p, "%d%d" % (p, h)
             ts(T.t1[:, hs], e, 1, 2047, A.arith_shift_right, A.bitwise_and, 256, [ek], ["t1%d" % h])
             ts(T.t2[:, hs], e, 1, None, A.bitwise_and, None, 256, [ek], ["t2%d" % h])
-            ts(Z, T.t2[:, hs], float(R - 2 * R * p), float(R * p), A.mult, A.add, 256, ["t2%d" % h], ["Z"], [7])
-            tt(T.pp[:, hs], Z, T.t1[:, hs], A.add, 256, ["Z", "t1%d" % h], ["pp%d" % h], [7])
-            cp(T.ua[:, ps_], T.pp[:, hs], 256, ["pp%d" % h], ["ua" + k])
-            ts(T.hi[:, ps_], T.pp[:, hs], 6, None, A.arith_shift_right, None, 256, ["pp%d" % h], ["hi" + k])
-            ts(T.lo[:, ps_], T.pp[:, hs], 63, None, A.bitwise_and, None, 256, ["pp%d" % h], ["lo" + k])
+            ts(Z, T.t2[:, hs], float(R - 2 * R * p), float(R * p), A.mult, A.add, 256, ["t2%d" % h], ["Z"], [4])
+            tt(T.t1[:, hs], Z, T.t1[:, hs], A.add, 256, ["Z", "t1%d" % h], ["t1%d" % h], [4])
+            cp(T.ua[:, ps_], T.t1[:, hs], 256, ["t1%d" % h], ["ua" + k])
+            ts(T.hi[:, ps_], T.t1[:, hs], 6, None, A.arith_shift_right, None, 256, ["t1%d" % h], ["hi" + k])
+            ts(T.lo[:, ps_], T.t1[:, hs], 63, None, A.bitwise_and, None, 256, ["t1%d" % h], ["lo" + k])
 
     decode(0)
     decode(1)
@@ -337,45 +343,53 @@ def build(g, core, T, topo, r):
             tag[0] = tg
             for h in range(2):
                 o = 512 * p + 128 * c + 64 * h
-                act(T.pg[:, 2048 * b + 1024 * h:2048 * b + 1024 * h + 1024], Pwin.indirect(T.ua[:, o:o + 64]), F.Identity, 1024,
-                    Pk + ["ua" + hk], ["pg%d%d" % (b, h)], k=GA)
+                po, pi = T.pg[:, 2048 * b + 1024 * h:2048 * b + 1024 * h + 1024], Pwin.indirect(T.ua[:, o:o + 64])
+                if "p%d%d%d" % (t, c, h) in ONV:
+                    cp(po, pi, 1024, Pk + ["ua" + hk], ["pg%d%d" % (b, h)], k=GA)
+                else:
+                    act(po, pi, F.Identity, 1024, Pk + ["ua" + hk], ["pg%d%d" % (b, h)], k=GA)
             tag[0] = tg + 1
-            Tp = B[4][:, bs]
+            Tp = B[6][:, 384:512]
             mm([(Tp, T.Wp[:, 15 - k:143 - k], T.pg[:, 2048 * b + k:2048 * b + 2048:16]) for k in range(16)]
-               + [(Tp, T.NG[:, :], T.PW[:, own])], 17 * 128, ["pg%d0" % b, "pg%d1" % b, "Wp", "NG", "P%do%d" % (t, c)], ["T" + sb_], [4])
-            tt(T.Ti[:, bs], Tp, T.nbr[:, 256 * c + p:256 * c + 256:2], A.add, 128, ["T" + sb_, "nb%d" % p], ["Ti" + sb_], [4])
+               + [(Tp, T.NG[:, :], T.PW[:, own])], 17 * 128, ["pg%d0" % b, "pg%d1" % b, "Wp", "NG", "P%do%d" % (t, c)], ["T"], [6])
+            tt(T.Ti[:, bs], Tp, T.nbr[:, 256 * c + p:256 * c + 256:2], A.add, 128, ["T", "nb%d" % p], ["Ti" + sb_], [6])
             ts(T.ai[:, bs], T.Ti[:, bs], 12, 1023, A.arith_shift_right, A.bitwise_and, 128, ["Ti" + sb_], ["ai" + sb_])
             ts(T.ac[:, cs], T.ai[:, bs], -512.0, None, A.add, None, 128, ["ai" + sb_], ["ac" + sc])
             for h in range(2):
-                for j in range(4):
-                    d = 4 * h + j + 1
-                    mm([(B[2 + h][:, 128 * j:128 * j + 128], T.Df[:, 128 * (d - 1):128 * d], T.ac[:, cs])], 128,
-                       ["ac" + sc, "Df%d" % d], ["D%d" % d], [2 + h])
-                for j in range(4):
-                    d = 4 * h + j + 1
+                ds = range(4 * h + 1, 4 * h + 5)
+
+                def dfn(ds=ds, h=h, cs=cs):
+                    for j, d in enumerate(ds):
+                        o, l = B[2 + h][:, 128 * j:128 * j + 128], T.Df[:, 128 * (d - 1):128 * d]
+                        ins = P.matmul(o, l, T.ac[:, cs], True, True)
+                    return ins
+                op("P", dfn, OV + PCY * 512, ["ac" + sc] + ["Df%d" % d for d in ds], ["D%d" % d for d in ds], [2 + h])
+                for j, d in enumerate(ds):
                     o = 1024 * b + 128 * (d - 1)
                     act(T.Sd[:, o:o + 128], B[2 + h][:, 128 * j:128 * j + 128], F.Sign, 128, ["D%d" % d, "bs"],
                         ["Sd%d%d" % (b, d)], [2 + h], bias=ct[:, 8 + d:9 + d])
-            Rp = B[5][:, bs]
-            mm([(Rp, T.Rk[:, 128 * j:128 * j + 128], T.Sd[:, 1024 * b + 128 * j:1024 * b + 128 * j + 128]) for j in range(8)],
-               8 * 128, ["Sd%d%d" % (b, d) for d in range(1, 9)] + ["Rk0", "Rk1"], ["R" + sb_], [5])
+            Rp = B[5][:, 0:128]
+            js = [j for j in range(8) for _ in range(1 + ("s%d%d%d" % (t, c, j // 4) in ONV))]
+            mm([(Rp, T.Rk[:, 128 * j:128 * j + 128], T.Sd[:, 1024 * b + 128 * j:1024 * b + 128 * j + 128]) for j in js],
+               len(js) * 128, ["Sd%d%d" % (b, d) for d in range(1, 9)] + ["Rk0", "Rk1"], ["R"], [5])
             mo = 4096 * b
-            tt(T.mm[:, mo:mo + 128], Rp, T.hi[:, pcs], A.add, 128, ["R" + sb_, "hi" + hk], ["wh" + sb_], [5])
-            tt(T.mm[:, mo + 128:mo + 256], Rp, T.lo[:, pcs], A.add, 128, ["R" + sb_, "lo" + hk], ["wl" + sb_], [5])
-            act(T.p2[:, cs], Rp, F.Sigmoid, 128, ["R" + sb_], ["p2" + sc], [5], bias=-27.5 * LN2, scale=-LN2 / 64)
+            tt(T.mm[:, mo:mo + 128], Rp, T.hi[:, pcs], A.add, 128, ["R", "hi" + hk], ["m%d_0" % b], [5])
+            tt(T.mm[:, mo + 128:mo + 256], Rp, T.lo[:, pcs], A.add, 128, ["R", "lo" + hk], ["wl" + sb_], [5])
+            act(T.p2[:, cs], Rp, F.Sigmoid, 128, ["R"], ["p2" + sc], [5], bias=-27.5 * LN2, scale=-LN2 / 64)
             for s in range(1, 16):
                 ts(T.mm[:, mo + 256 * s:mo + 256 * s + 256], T.mm[:, mo:mo + 256], 64.0 * s - 480, None, A.max, None, 256,
-                   ["wh" + sb_, "wl" + sb_], ["m%d_%d" % (b, s)], k=0.5)
-            Op = B[4][:, 256 + 128 * b:384 + 128 * b]
+                   ["m%d_0" % b, "wl" + sb_], ["m%d_%d" % (b, s)], k=0.5)
+            Op = B[4][:, bs]
             its = [(Op, T.Z64[:, :], T.mm[:, mo:mo + 128]), (Op, T.Z1[:, :], T.mm[:, mo + 128:mo + 256])]
             for s in range(1, 16):
                 o = mo + 256 * s
                 its += [(Op, T.W64[:, 15 - s:143 - s], T.mm[:, o:o + 128]), (Op, T.W1[:, 15 - s:143 - s], T.mm[:, o + 128:o + 256])]
-            mm(its, 32 * 128, ["wh" + sb_, "wl" + sb_, "Z1", "Z64", "W1", "W64"] + ["m%d_%d" % (b, s) for s in range(1, 16)],
-               ["O" + sb_], [4])
+            for q in range(2):
+                mm(its[16 * q:16 * q + 16], 16 * 128, ["Z1", "Z64", "W1", "W64", "wl" + sb_] + ["O" + sb_] * q
+                   + ["m%d_%d" % (b, s) for s in range(8 * q, 8 * q + 8)], ["O" + sb_, "G4"], [4], first=q == 0, last=q == 1)
             ts(T.us[:, cs], Op, ct[:, 4:5], None, A.add, None, 128, ["O" + sb_, "c4"], ["us" + sc], [4])
             if t < 3:
-                act(T.cp[:, cs], Op, F.Identity, 128, ["O" + sb_, "c5"], ["cp" + sc], [4], bias=ct[:, 5:6])
+                ts(T.cp[:, cs], Op, ct[:, 5:6], None, A.add, None, 128, ["O" + sb_, "c5"], ["cp" + sc], [4])
             tag[0] = tg + 2
             xo = c * XW + 8
             do = 2048 * c
@@ -385,33 +399,41 @@ def build(g, core, T, topo, r):
                     F.Identity, 1024, Lk + ["us" + sc], [xk], k=GA)
                 for j in range(2):
                     o = 1024 * h + 512 * j
-                    M = B[j]
-                    op("V", lambda M=M, o=o, xo=xo: V.tensor_tensor_scan(M[:, :], T.xx[:, xo + o - 1:xo + o + 511], T.msk[:, :],
-                                                                        0.0, A.max, A.mult), vc(512),
+                    op("V", lambda j=j, o=o, xo=xo: V.tensor_tensor_scan(
+                        T.MM[:, 512 * j:512 * j + 512], T.xx[:, xo + o - 1:xo + o + 511], T.msk[:, :], 0.0, A.max, A.mult), vc(512),
                        [xk, "msk", "xz" + sc] + ["x%d0" % c] * h, ["M%d" % j], [j])
-                    tt(T.dd[:, do + o:do + o + 512], T.xx[:, xo + o:xo + o + 512], M[:, :], A.subtract, 512,
+                    tt(T.dd[:, do + o:do + o + 512], T.xx[:, xo + o:xo + o + 512], T.MM[:, 512 * j:512 * j + 512], A.subtract, 512,
                        [xk, "M%d" % j], [dk + str(j)], [j])
-                    if t < 4:
-                        q = 2 * h + j
-                        tt(B[5][:, 384 + 32 * q:416 + 32 * q], T.xx[:, xo + o + 15:xo + o + 512:16], M[:, 15:512:16], A.max, 32,
-                           [xk, "M%d" % j], ["X%d" % q], [j, 5])
+                if t < 4:
+                    o = 1024 * h
+                    tt(B[5][:, 384 + 64 * h:448 + 64 * h], T.xx[:, xo + o + 15:xo + o + 1024:16], T.MM[:, 15:1024:16], A.max, 64,
+                       [xk, "M0", "M1"], ["X%d" % h], [0, 1, 5])
                 act(T.sg[:, 2048 * b + 1024 * h:2048 * b + 1024 * h + 1024], T.dd[:, do + 1024 * h:do + 1024 * h + 1024], F.Sign,
                     1024, [dk + "0", dk + "1"], ["sg%d%d" % (b, h)] + ["los", "lou", "ll0", "ll1"] * (t + c + h == 0), bias=-1e-9)
             if t < 4:
                 X = B[5][:, 384:512]
-                Xk = ["X%d" % q for q in range(4)]
+                Xk = ["X%d" % q for q in range(2)]
                 ok = "L%do%d" % (t, c)
                 tt(X, X, T.LW[:, own], A.subtract, 128, Xk + [ok], Xk, [5])
-                act(T.L8[:, cs], T.LW[:, own], F.Identity, 128, [ok], ["L8" + sc], scale=8.0)
-                tt(X, X, T.L8[:, cs], A.add, 128, Xk + ["L8" + sc], Xk, [5])
+                act(T.uu[:, bs], T.LW[:, own], F.Identity, 128, [ok], ["uu" + sb_], scale=8.0)
+                tt(X, X, T.uu[:, bs], A.add, 128, Xk + ["uu" + sb_], Xk, [5])
                 tt(T.LW[:, new], X, T.fad[:, 256 * c + p:256 * c + 256:2], A.mult, 128, Xk + ["fad"], ["L%do%d" % (t + 2, c)], [5])
             tag[0] = tg + 3
-            Cp = B[6][:, 0:128]
-            mm([(Cp, T.Wc[:, 15 - s:143 - s], T.sg[:, 2048 * b + s:2048 * b + 2048:16]) for s in range(16)], 16 * 128,
-               ["sg%d0" % b, "sg%d1" % b, "Wc"], ["C"], [6])
-            act(T.fs[:, bs], Cp, F.Sign, 128, ["C"], ["fs" + sb_], [6], bias=11.0)
+            parts = [(0, 1), (1, 2)] if (t, c) == (4, 3) else [(0, 2)]
+            Up = B[5][:, 128:256]
+            for h0, h1 in parts:
+                w = 64 * (h1 - h0)
+                ky = lambda a: [a + str(h) for h in range(h0, h1)]
+                cq, fq = B[6][:, 64 * h0:64 * h1], T.fs[:, 128 * b + 64 * h0:128 * b + 64 * h1]
+                mm([(cq, T.Wc[:, 15 - s:143 - s], T.sg[:, 2048 * b + 1024 * h0 + s:2048 * b + 1024 * h1:16]) for s in range(1, 16)],
+                   15 * w, ky("sg" + sb_) + ["Wc"], ky("C"), [6])
+                act(fq, cq, F.Sign, w, ky("C"), ky("fs" + sb_), [6], bias=11.0)
+                uq = B[5][:, 128 + 64 * h0:128 + 64 * h1]
+                mm([(uq, T.I4[:, :], fq), (uq, T.Ih[:, :], T.jc[:, 64 * h0:64 * h1])], 2 * w, ky("fs" + sb_) + ["I4", "Ih", "jc"],
+                   ky("U"), [5])
+                ts(T.um[:, 128 * c + 64 * h0:128 * c + 64 * h1], uq, -3072.0, None, A.add, None, w, ky("U"), ky("um" + sc), [5])
             Fp = B[5][:, 256:384]
-            mm([(Fp, T.FW[:, 0:128], T.fs[:, bs]), (Fp, T.FW[:, 128:256], T.fs[:, bs])], 256, ["fs" + sb_, "FW0", "FW1"], ["F"], [5])
+            mm([(Fp, T.FW[:, 0:128], T.fs[:, bs]), (Fp, T.FW[:, 128:256], T.fs[:, bs])], 256, ["fs%d0" % b, "fs%d1" % b, "FW0", "FW1"], ["F"], [5])
             tt(T.yy[:, cs], Fp, T.p2[:, cs], A.mult, 128, ["F", "p2" + sc], ["yy" + sc], [5])
             act(T.ls[:, bs], T.yy[:, cs], F.Abs, 128, ["yy" + sc], ["ls" + sb_], bias=-1.5)
             act(Fp, T.ls[:, bs], F.Sign, 128, ["ls" + sb_], ["F"], [5], bias=0.5, scale=-1.0)
@@ -432,10 +454,10 @@ def build(g, core, T, topo, r):
                 mm(sm(S2) + [(S2, T.SB[:, 512:640], T.Ht[:, bs])], 512, sk + ["Ht" + sb_, "SB4"], ["S2"], [6])
                 act(T.PW[:, new], S2, F.Identity, 128, ["S2"], ["P%do%d" % (t + 2, c)], [6])
             if t >= 3:
-                ts(T.t1[:, cs], S1, 512.0, None, A.add, None, 128, ["S1"], ["t1%d" % (c // 2), "y1" + sc], [6])
-                ts(T.t2[:, cs], T.t1[:, cs], 1023, None, A.bitwise_and, None, 128, ["y1" + sc], ["t2%d" % (c // 2), "y2" + sc])
-                cp(T.LW[:, 256 * c + p:256 * c + 256:2], T.t2[:, cs], 128, ["y2" + sc],
-                   ["yo%d%d" % (p, c)] + ["L0o0", "L0o1", "L0o2", "L0o3", "L0g"] * (t == 3 and c == 0))
+                act(T.hq[:, bs], S1, F.Identity, 128, ["S1"], ["hq" + sb_], [6], bias=196607.5, scale=-1.0)
+                mm(sm(S1) + [(S1, T.SB[:, 0:128], T.hq[:, bs])], 640, sk + ["hq" + sb_], ["S1"], [6])
+                act(T.LW[:, 256 * c + p:256 * c + 256:2], S1, F.Identity, 128, ["S1"],
+                    ["yo%d%d" % (p, c)] + ["L0o0", "L0o1", "L0o2", "L0o3", "L0g"] * (t == 3 and c == 0), [6], bias=512.0 - 393216.0)
             if t < 4 and c < 3:
                 q = 3 * t + c
                 for kind, hc, hb, win, lo_, ne in (("L", hL, T.hbL, T.LW, 8, 8), ("P", hP, T.hbP, T.PW, 0, 4)):
@@ -446,24 +468,27 @@ def build(g, core, T, topo, r):
                             dsts=[hb[256 * q:256 * q + 128, :], hb[256 * q + 128:256 * q + 256, :]])], local_sem=T.sem.lsm)
                         lsm[0] += ne
                     send(s_h, ["%s%do%d" % (kind, t + 2, c)], ["s%s%d" % (kind, q)])
-            Up = B[6][:, 384:512]
-            mm([(Up, T.I4[:, :], T.fs[:, bs]), (Up, T.Ih[:, :], T.jc[:, :])], 256, ["fs" + sb_, "I4", "Ih", "jc"], ["U"], [6])
-            ts(T.um[:, cs], Up, -3072.0, None, A.add, None, 128, ["U"], ["um" + sc], [6])
             for h in range(2):
                 tag[0] = tg + 4 + h
                 dk = ["d%d%d0" % (c, h), "d%d%d1" % (c, h)]
                 dv = T.dd[:, do + 1024 * h:do + 1024 * h + 1024]
-                act(dv, dv, F.Sigmoid, 1024, dk, dk)
-                tt(T.tt[:, 1024 * h:1024 * h + 1024],
+                for j in range(2):
+                    dq = T.dd[:, do + 1024 * h + 512 * j:do + 1024 * h + 512 * j + 512]
+                    act(dq, dq, F.Sigmoid, 512, [dk[j]], [dk[j]])
+                u = (8 * t + 2 * c + h) % NT
+                w = 2 * c + h
+                tt(T.tt[:, 1024 * u:1024 * u + 1024],
                    T.xx[:, c * XW:(c + 1) * XW].indirect(T.um[:, 128 * c + 64 * h:128 * c + 64 * h + 64]), dv, A.mult, 1024,
-                   dk + ["x%d0" % c, "x%d1" % c, "xz" + sc, "um" + sc], ["tt%d" % h], k=GA)
-                Ep = B[7][:, 64 * h:64 * h + 64]
+                   dk + ["x%d0" % c, "x%d1" % c, "xz" + sc, "um%d%d" % (c, h)], ["tt%d" % u], k=GA)
+                Ep = B[7][:, 64 * w:64 * w + 64]
                 ev = T.EE[:, 256 * c + 128 * h + p:256 * c + 128 * h + 128:2]
                 ek = "E%d%d%d" % (p, c, h)
-                its = [(Ep, T.If[:, :], T.tt[:, 1024 * h + s:1024 * h + 1024:16]) for s in range(16)] + [(Ep, T.If[:, :], ev)] * (t >= 2)
-                mm(its[:8], 8 * 256, ["tt%d" % h, "If"], ["Ep%d" % h, "Eg"], [7], last=False)
-                mm(its[8:], len(its[8:]) * 256, ["tt%d" % h, "If", "Ep%d" % h] + [ek] * (t >= 2), ["Ep%d" % h, "Eg"], [7], first=False)
-                act(ev, Ep, F.Identity, 64, ["Ep%d" % h], [ek], [7])
+                its = [(Ep, T.If[:, :], T.tt[:, 1024 * u + s:1024 * u + 1024:16]) for s in range(16)] + [(Ep, T.If[:, :], ev)] * (t >= 2)
+                mm(its[:8], 8 * 256, ["tt%d" % u, "If"], ["Ep%d" % w, "Eg"], [7], last=False)
+                mm(its[8:], len(its[8:]) * 256, ["tt%d" % u, "If", "Ep%d" % w] + [ek] * (t >= 2), ["Ep%d" % w, "Eg"], [7], first=False)
+                if h == 1:
+                    act(T.EE[:, 256 * c + p:256 * c + 256:2], B[7][:, 128 * c:128 * c + 128], F.Identity, 128,
+                        ["Ep%d" % (w - 1), "Ep%d" % w], [ek, "E%d%d0" % (p, c)], [7])
             if t == 4:
                 dma("S", [(T.ye[:, 256 * c:256 * c + 256], T.EE[:, 256 * c:256 * c + 256])],
                     ["E%d%d%d" % (a, c, h) for a in range(2) for h in range(2)], ["ye" + sc])
@@ -472,13 +497,13 @@ def build(g, core, T, topo, r):
             ext("ap%d" % t, 72, ["sP%d" % (3 * t + c) for c in range(3)], ["P%dg" % (t + 2)], 6000.0)
         if t < 3:
             tag[0] = 25 * t + 25
-            Cq = B[7][:, 128:160]
-            mm([(Cq, T.Wt[:, 15 - j:143 - j], T.cp[:, j:512:16]) for j in range(16)], 16 * 256,
-               ["cp%d" % c for c in range(4)] + ["Wt"], ["Cq", "Eg"], [7])
+            Cq = B[2][:, 0:32]
+            mm([(Cq, T.Wt[:, 15 - j:143 - j], T.cp[:, j:512:16]) for j in range(16)], 16 * 64,
+               ["cp%d" % c for c in range(4)] + ["Wt"], ["D1"], [2])
             a0, a1, a2 = T.ty[:, 0:32], T.ty[:, 32:64], T.ty[:, 64:96]
-            ts(a0, Cq, 0.0, -float(R), A.is_ge, A.mult, 32, ["Cq"], ["ty", "a0"], [7])
-            ts(a1, Cq, 0.0, 1.0 - 2 * p, A.is_ge, A.mult, 32, ["Cq"], ["ty", "a1"], [7])
-            tt(a0, Cq, a0, A.add, 32, ["Cq", "a0"], ["a0"], [7])
+            ts(a0, Cq, 0.0, -float(R), A.is_ge, A.mult, 32, ["D1"], ["ty", "a0"], [2])
+            ts(a1, Cq, 0.0, 1.0 - 2 * p, A.is_ge, A.mult, 32, ["D1"], ["ty", "a1"], [2])
+            tt(a0, Cq, a0, A.add, 32, ["D1", "a0"], ["a0"], [2])
             ts(a2, a0, float(R), 2.0, A.add, A.mult, 32, ["a0"], ["ty", "a2"])
             tt(a1, a1, T.slf[:, :], A.subtract, 32, ["a1", "slf"], ["a1"])
             ts(a0, a0, 511.5 - R, None, A.is_lt, None, 32, ["a0"], ["a0"])
@@ -493,9 +518,9 @@ def build(g, core, T, topo, r):
             for h in range(2):
                 hs = slice(256 * h, 256 * h + 256)
                 e = T.nbr[:, 512 * h + p:512 * h + 512:2]
-                tt(Z, T.go[:, hs], e, A.subtract, 256, ["go", mk], ["Z"], [7], k=2.0)
-                tt(Z, Z, T.t2[:, hs], A.mult, 256, ["Z", "t2%d" % h], ["Z"], [7])
-                tt(e, Z, e, A.add, 256, ["Z", mk], [mk], [7])
+                tt(Z, T.go[:, hs], e, A.subtract, 256, ["go", mk], ["Z"], [4], k=2.0)
+                tt(Z, Z, T.t2[:, hs], A.mult, 256, ["Z", "t2%d" % h], ["Z"], [4])
+                tt(e, Z, e, A.add, 256, ["Z", mk], [mk], [4])
             decode(p)
     dma("S", [(T.yp[:, :], T.LW[1:128:16, 0:1024])], ["yo%d%d" % (a, c) for a in range(2) for c in range(4)], ["yp"])
     return ops, lsm
@@ -530,48 +555,72 @@ def schedule(ops):
     def place(pred, succ, pri, back):
         left = [len(d) for d in pred]
         ready = [i for i in range(n) if left[i] == 0]
-        st, rt, busy = [0.0] * n, [0.0] * n, {}
+        en, rt = [0.0] * n, [0.0] * n
+        busy = {k: [] for k in keys}
+        key = lambda x: pri[x]
+        edge = gap[back]
         while ready:
-            i = max(ready, key=lambda x: pri[x])
+            i = max(ready, key=key) if len(ready) > 1 else ready[0]
             ready.remove(i)
-            o = ops[i]
-            e, c, s = o["e"], o["c"], rt[i]
-            res = ([(e, 0.0)] if e != "X" else []) + [(b, XL) for b in o["b"]]
+            e, c, s, res = eng[i], cost[i], rt[i], need[i]
             moved = True
             while moved:
                 moved = False
                 for k, pad in res:
-                    iv = busy.setdefault(k, [])
-                    lo, hi = 0, len(iv)
-                    while lo < hi:
-                        m = (lo + hi) // 2
-                        if iv[m][0] < s - 4000.0:
-                            lo = m + 1
-                        else:
-                            hi = m
-                    while lo < len(iv) and iv[lo][0] < s + c + pad:
-                        if iv[lo][1] + pad > s and (pad == 0.0 or iv[lo][2] != e):
-                            s = iv[lo][1] + pad
-                            moved = True
-                        lo += 1
+                    iv = busy[k]
+                    m = len(iv)
+                    while m > 0 and iv[m - 1][1] + pad > s:
+                        m -= 1
+                    for a, z, w in iv[m:]:
+                        if a >= s + c + pad:
+                            break
+                        if z + pad > s and (pad == 0.0 or w != e):
+                            s = z + pad
+                            moved = len(res) > 1
             for k, pad in res:
                 iv = busy[k]
                 m = len(iv)
                 while m > 0 and iv[m - 1][0] > s:
                     m -= 1
                 iv.insert(m, (s, s + c, e))
-            st[i] = s
-            for j in succ[i]:
+            s += c
+            en[i] = s
+            for j, d in edge[i]:
                 left[j] -= 1
-                rt[j] = max(rt[j], s + c + ops[j if back else i]["lat"] + (SL if ops[j]["e"] == e else XL))
+                if s + d > rt[j]:
+                    rt[j] = s + d
                 if left[j] == 0:
                     ready.append(j)
-        return [st[i] + ops[i]["c"] for i in range(n)]
+        return en
+
+    eng, cost = [o["e"] for o in ops], [o["c"] for o in ops]
+    need = [([(o["e"], 0.0)] if o["e"] != "X" else []) + [(b, XL) for b in o["b"]] for o in ops]
+    keys = set(k for x in need for k, _ in x)
+    gap = ([[(j, ops[i]["lat"] + (SL if eng[i] == eng[j] else XL)) for j in suc[i]] for i in range(n)],
+           [[(j, ops[j]["lat"] + (SL if eng[i] == eng[j] else XL)) for j in sorted(deps[i])] for i in range(n)])
 
     arr = [i for i in range(n) if ops[i]["e"] == "X"]
 
     def measure(end):
-        return max(end[i] + ops[i]["lat"] for i in range(n)) + 0.05 * sum(end[i] for i in arr)
+        fin, free, bank = [0.0] * n, {}, {}
+        for i in sorted(range(n), key=lambda x: (end[x] - cost[x], end[x], x)):
+            e = eng[i]
+            s = free.get(e, 0.0) if e != "X" else 0.0
+            for j, d in back[i]:
+                if fin[j] + d > s:
+                    s = fin[j] + d
+            for b in ops[i]["b"]:
+                w = bank.get(b)
+                if w is not None and w[0] != e and w[1] > s:
+                    s = w[1]
+            s += slow[i]
+            fin[i] = free[e] = s
+            for b in ops[i]["b"]:
+                bank[b] = (e, s + XL)
+        return max(end[i] + ops[i]["lat"] for i in range(n)) + 0.05 * sum(end[i] for i in arr) + WS * max(fin)
+
+    back = [[(j, ops[j]["lat"] + (SL if eng[i] == eng[j] else XL)) for j in sorted(deps[i])] for i in range(n)]
+    slow = [o["c"] * (2.0 if o["e"] == "P" else 1.0) for o in ops]
 
     best, pri = None, [bl[i] + 100.0 * OFF[ops[i]["tag"]] for i in range(n)]
     for _ in range(ITER):

@@ -4,7 +4,10 @@ from concourse.mybir import AluOpType as A, ActivationFunctionType as F
 
 R = 1664
 XW = 2056
-NT = 4
+NQ = 2
+G = 16 // NQ
+TWO = [0, 2]
+NT = 3
 LN2 = math.log(2.0)
 f32, bf, f16, i32, u16 = "float32", "bfloat16", "float16", "int32", "uint16"
 
@@ -15,46 +18,49 @@ def sb(n, t):
 
 SCRATCH = {
     "LW": sb(6 * R, f32), "PW": sb(6 * R, bf), "xx": sb(4 * XW, f32), "dd": sb(8192, f32),
-    "sg": sb(4096, bf), "pg": sb(4096, bf), "tt": sb(NT * 1024, f32), "mm": sb(8192, f16),
-    "uu": sb(256, f32), "nbr": sb(1024, i32), "EE": sb(1024, f32),
+    "sg": sb(4096, bf), "pg": sb(4096, bf), "tt": sb(NT * 2048, f32), "mm": sb(6144 - 2048 * len(TWO), f32),
+    "uu": sb(512, f32), "nbr": sb(1024, i32), "nbs": sb(1024, i32), "EE": sb(1024, f32),
     "fad": sb(1024, bf), "lb": sb(768, bf),
-    "hi": sb(1024, i32), "lo": sb(1024, i32), "ua": sb(1024, u16), "us": sb(512, u16), "um": sb(512, u16),
-    "t1": sb(512, i32), "t2": sb(512, i32), "Ti": sb(256, i32), "ai": sb(256, i32),
+    "ua": sb(1024, u16), "us": sb(512, u16), "um": sb(512, u16),
+    "t1": sb(256, i32), "t2": sb(256, i32), "Ti": sb(256, i32),
     "ac": sb(512, f16), "Sd": sb(2048, bf), "p2": sb(512, bf), "fs": sb(256, bf), "yy": sb(512, f32),
-    "ls": sb(256, f32), "la": sb(256, f16), "Ht": sb(256, bf), "hq": sb(256, bf), "cp": sb(512, f16), "go": sb(512, f32),
-    "msk": sb(512, bf), "jc": sb(128, f16), "kk": sb(128, f16), "ul": sb(32, u16), "su": sb(64, u16), "ty": sb(256, f32),
+    "la": sb(256, f16), "Sh": sb(128, bf), "hq": sb(256, bf), "cp": sb(512, f16), "go": sb(512, f32),
+    "msk": sb(512, bf), "jc": sb(128, f16), "ul": sb(32, u16), "ty": sb(136, f32),
     "pc": sb(64, i32), "rc": sb(64, i32), "ps": sb(48, i32), "u1": sb(64, i32), "u2": sb(64, i32), "u3": sb(64, i32),
-    "va": sb(256, f32), "vh": sb(256, bf), "vl": sb(256, bf), "vs": sb(48, f32), "cs": sb(96, bf), "pl": sb(288, bf),
-    "ci": sb(160, i32), "cj": sb(144, i32), "ct": sb(48, f32), "cb": sb(8, bf), "Qw": sb(144, f32), "BL": sb(128, f32),
-    "Am": sb(128, f32), "Bo": sb(128, f32), "tm": sb(256, f32), "slf": sb(32, f32),
-    "Wc": sb(144, bf), "W1": sb(144, f16), "W64": sb(144, f16), "Z1": sb(128, f16), "Z64": sb(128, f16), "I8": sb(128, f32),
+    "vh": sb(256, bf), "vl": sb(256, bf), "vs": sb(48, f32), "cs": sb(96, bf), "pl": sb(288, bf),
+    "ci": sb(8, i32), "cj": sb(144, i32), "ct": sb(48, f32), "cb": sb(8, bf), "BL": sb(144, f32),
+    "slf": sb(32, f32),
+    "Wc": sb(144, bf), "W1": sb(272, f32), "Pm": sb(144 * NQ, bf),
     "Wp": sb(144, bf), "Wt": sb(144, f16), "NG": sb(128, bf), "Df": sb(1024, f16), "Rk": sb(1024, bf),
-    "FW": sb(256, bf), "I4": sb(128, bf), "Ih": sb(128, f16), "If": sb(128, f32), "SA": sb(128, f16),
-    "SB": sb(640, bf),
-    "hbL": ("dram", [12 * 256, 128], f32), "hbP": ("dram", [12 * 256, 128], bf),
+    "FW": sb(256, bf), "Ib": sb(128, bf), "Ih": sb(128, f16), "If": sb(128, f32), "SA": sb(144, f16),
+    "SB": sb(720, bf), "Ps": sb(384, bf), "Hs": sb(128, bf), "mh": sb(4096, f16), "hl": sb(512 * len(TWO), i32), "Wh": sb(544, f16),
+    "hbL": ("dram", [12 * 256, 128], f32),
 }
 SCRATCH["MM"] = ("psum", [128, 1024], f32)
 for _i in range(2, 8):
     SCRATCH["B%d" % _i] = ("psum", [128, 512], f32)
 
 SEMAPHORES = (["cV", "cA", "cP", "cG", "lsm", "ip", "il0", "il1"] + ["ha%d" % i for i in range(13)]
-              + ["ap%d" % i for i in range(4)] + ["al%d" % i for i in range(4)] + ["d%d" % i for i in range(40)])
+              + ["ap%d" % i for i in range(4)] + ["al%d" % i for i in range(4)] + ["d%d" % i for i in range(24)]
+              + ["ad%d" % i for i in range(NT)] + ["lp0", "lp1", "lp2"])
 
 CY, PCY, GA, OV = 0.83, 0.42, 1.56, 20.0
-SL, XL, ITER = 100.0, 250.0, 3
-OFF = [0] * 126
-SEED, TRIES, HEAT = 2, 3500, 100.0
-WS = 0.3
-ONV = ["p001", "p301", "p401"]
+SL, XL, GD = 100.0, 250.0, 1300.0
+MEAN = (1.05, 1.1, 1.1)
+CASES = ((0.45, 1.0, 1.0, 1.15), (0.3, 1.3, 1.0, 0.85), (0.25, 0.75, 1.3, 1.4))
+SEED, SHIFTS, MOVES = 5, ((2200, 100.0), (800, 50.0), (800, 50.0)), (6000, 2500, 11)
+ONV = ["001", "011"]
+NV = [[0, 15, 0, 0], [0] * 4, [0] * 4, [0] * 4, [0, 4, 0, 4]]
+SGN = [3, 3, 3, 3, 3]
+DIR = ["43"]
+HALF = [0]
 CACHE = {}
 
 
-def helpers(core, T, topo):
+def helper(core, T, topo):
     ok = [c for c in topo.cores_of(core) if T.rank_of(c) is None
           and all(topo.may_write(c, o) for o in T.cores if o != core)]
-    same = [c for c in ok if topo.die(c) == topo.die(core)]
-    other = [c for c in ok if topo.die(c) != topo.die(core)]
-    return (same or ok)[0], (other or ok)[0]
+    return ([c for c in ok if topo.die(c) != topo.die(core)] or ok)[0]
 
 
 def emask(topo, src, dst, lo, n):
@@ -66,14 +72,14 @@ def did(topo, c):
     return DstId(rid=a[0], pnc=a[1])
 
 
-def fan(g, T, topo, me, r, src, dst_of, sem):
+def fan(g, T, topo, me, r, src, dst_of, sem, loc):
     n = len(T.cores)
     to = [T.cores[(r + d) % n] for d in range(1, n)]
     m = topo.mask(me, to[0])
     for c in to:
         m &= topo.mask(me, c)
     g.remote_dma_fused([RemoteDMATransfer(dst_ids=[did(topo, c) for c in to], dma_engine_mask=m, remote_sem=sem,
-                                          srcs=[src], dsts=[dst_of(d) for d in range(1, n)])], local_sem=T.sem.lsm)
+                                          srcs=[src], dsts=[dst_of(d) for d in range(1, n)])], local_sem=loc)
     return bin(m).count("1")
 
 
@@ -81,19 +87,16 @@ def gcol(reg, d, c):
     return reg * R + 512 + (d - 1) * 384 + 128 * c
 
 
-def helper_program(g, core, T, topo, r, kind):
-    tot = 0
-    if kind == "L":
-        g.wait_ge(T.sem.ha12, 8)
-        tot += fan(g, T, topo, core, r, T.lb[:, 384:768],
-                   lambda d: T.sg[:, 1152 + (d - 1) * 384:1152 + d * 384], T.sem.il1)
+def helper_program(g, core, T, topo, r):
+    g.wait_ge(T.sem.ha12, 8)
+    tot = fan(g, T, topo, core, r, T.lb[:, 384:768],
+              lambda d: T.sg[:, 1152 + (d - 1) * 384:1152 + d * 384], T.sem.il1, T.sem.lsm)
     for t in range(4):
         for c in range(3):
             q = 3 * t + c
-            g.wait_ge(T.sem["ha%d" % q], 16 if kind == "L" else 8)
-            hb, win, sem = (T.hbL, T.LW, "al%d") if kind == "L" else (T.hbP, T.PW, "ap%d")
-            tot += fan(g, T, topo, core, r, hb[256 * q + 16:256 * q + 144, :],
-                       lambda d: win[:, gcol(t + 2, d, c):gcol(t + 2, d, c) + 128], T.sem[sem % t])
+            g.wait_ge(T.sem["ha%d" % q], 16)
+            tot += fan(g, T, topo, core, r, T.hbL[256 * q + 16:256 * q + 144, :],
+                       lambda d: T.LW[:, gcol(t + 2, d, c):gcol(t + 2, d, c) + 128], T.sem["al%d" % t], T.sem.lsm)
     g.wait_ge(T.sem.lsm, tot)
 
 
@@ -103,10 +106,11 @@ def build(g, core, T, topo, r):
     nd = [0]
     lsm = [0]
     tag = [0]
-    hP, hL = helpers(core, T, topo)
+    hL = helper(core, T, topo)
+    ne = min(len(topo.engines(core, c)) for c in T.cores if c != core)
 
-    def op(e, fn, cost, rd, wr, bk=(), tok=None, lat=0.0, pri=0.0):
-        ops.append(dict(e=e, fn=fn, c=cost, r=list(rd), w=list(wr), b=list(bk), tok=tok, lat=lat, tag=tag[0]))
+    def op(e, fn, cost, rd, wr, bk=(), tok=None, lat=0.0, k=1.0):
+        ops.append(dict(e=e, fn=fn, c=cost, r=list(rd), w=list(wr), b=list(bk), tok=tok, lat=lat, tag=tag[0], g=k == GA))
 
     def vc(n, k=1.0):
         return OV + CY * max(64.0, n * k)
@@ -118,13 +122,13 @@ def build(g, core, T, topo, r):
             op("V", lambda: V.tensor_scalar(o, i, s1, s2, o0, o1), vc(n, k), rd, wr, bk)
 
     def tt(o, a, b, o0, n, rd, wr, bk=(), k=None):
-        op("V", lambda: V.tensor_tensor(o, a, b, o0), vc(n, k or (1.0 if bk else 2.0)), rd, wr, bk)
+        op("V", lambda: V.tensor_tensor(o, a, b, o0), vc(n, k or (1.0 if bk else 2.0)), rd, wr, bk, k=k)
 
     def cp(o, i, n, rd, wr, bk=(), k=1.0):
-        op("V", lambda: V.tensor_copy(o, i), vc(n, k), rd, wr, bk)
+        op("V", lambda: V.tensor_copy(o, i), vc(n, k), rd, wr, bk, k=k)
 
     def act(o, i, f, n, rd, wr, bk=(), bias=0.0, scale=1.0, k=1.0):
-        op("A", lambda: S.activation(o, i, f, bias=bias, scale=scale), vc(n, k), rd, wr, bk)
+        op("A", lambda: S.activation(o, i, f, bias=bias, scale=scale), vc(n, k), rd, wr, bk, k=k)
 
     def mm(items, cost, rd, wr, bk, first=True, last=True):
         def fn():
@@ -143,6 +147,18 @@ def build(g, core, T, topo, r):
                 q.dma_start(o, i).then_inc(T.sem[sem], 16)
         op(e, fn, (1000.0 if e == "G" else 100.0) * len(pairs), rd, wr, tok=(sem, 16 * len(pairs)), lat=lat)
 
+    used = {}
+
+    def gdma(sem, o, i, rd, wr, lat):
+        used[sem] = used.get(sem, 0) + 16
+        op("G", lambda: g.dma_start(o, i, accum_op=A.add).then_inc(T.sem[sem], 16), GD, rd, wr, tok=(sem, used[sem]), lat=lat)
+
+    def aff(e, o, i, scale, bias, n, rd, wr, bk=()):
+        if e == "V":
+            ts(o, i, scale, bias, A.mult, A.add, n, rd, wr, bk)
+        else:
+            act(o, i, F.Identity, n, rd, wr, bk, bias=bias, scale=scale)
+
     def iota(o, pat, base, cm, n, wr, fl=False):
         if fl:
             op("G", lambda: g.iota(o, pat, base, cm, allow_small_or_imprecise_dtypes=True), 130 + 2 * CY * n, [], wr)
@@ -150,7 +166,7 @@ def build(g, core, T, topo, r):
             op("G", lambda: g.iota(o, pat, base, cm), 130 + 2 * CY * n, [], wr)
 
     def send(fn, rd, wr):
-        op("G", fn, 300.0, rd, wr, tok="none")
+        op("G", fn, 600.0, rd, wr, tok="none")
 
     def ext(sem, cnt, rd, wr, lat):
         op("X", None, 0.0, rd, wr, tok=(sem, cnt), lat=lat)
@@ -163,9 +179,9 @@ def build(g, core, T, topo, r):
     dma("S", [(T.pc[:, :], T.ph0[:, :]), (T.rc[:, :], T.rb[:, :])], [], ["pc"])
     dma("A", [(T.sg[0:112, 2304:3072], T.loud[16:128, 0:768]), (T.sg[112:128, 2304:3072], T.loud[0:16, 0:768])], [], ["los"])
     dma("S", [(T.sg[:, 3072:4096], T.loud[:, :]), (T.fad[:, :], T.fade[:, :])], [], ["lou", "fad"])
+    dma("S", [(T.nbs[:, :], T.nb[:, :])], [], ["nbs"])
     op("V", lambda: V.memset(T.PW[:, 0:832], 0.0), vc(832, 0.5), [], ["Pz0"])
-    for j in range(1, 4):
-        act(T.PW[:, 832 * j:832 * j + 832], T.PW[:, 0:832], F.Identity, 832, ["Pz0"], ["Pz"])
+    dma("S", [(T.PW[:, 832 * j:832 * j + 832], T.PW[:, 0:832]) for j in range(1, 4)], ["Pz0"], ["Pz"])
 
     for p in range(2):
         ts(T.vs[:, 24 * p:24 * p + 24], T.ps[:, p:48:2], -512.0, None, A.add, None, 24, ["ps"], ["vs%d" % p])
@@ -173,9 +189,9 @@ def build(g, core, T, topo, r):
     tt(T.cs[:, 48:96], T.vs[:, :], T.cs[:, 0:48], A.subtract, 48, ["vs0", "vs1", "cs0"], ["cs1"])
 
     def s_ip():
-        lsm[0] += fan(g, T, topo, core, r, T.cs[:, :], lambda d: T.pl[:, 96 * (d - 1):96 * d], T.sem.ip)
+        lsm[0] += fan(g, T, topo, core, r, T.cs[:, :], lambda d: T.pl[:, 96 * (d - 1):96 * d], T.sem.ip, T.sem.lsm)
     send(s_ip, ["cs0", "cs1"], ["s_ip"])
-    ext("ip", 24, ["s_ip"], ["pl"], 4000.0)
+    ext("ip", 3 * ne, ["s_ip"], ["pl"], 4000.0)
     for p in range(2):
         prs = []
         for d in range(1, 4):
@@ -192,11 +208,11 @@ def build(g, core, T, topo, r):
         lsm[0] += 8
 
     def s_l0():
-        lsm[0] += fan(g, T, topo, core, r, T.lb[:, 0:384], lambda d: T.sg[:, (d - 1) * 384:d * 384], T.sem.il0)
+        lsm[0] += fan(g, T, topo, core, r, T.lb[:, 0:384], lambda d: T.sg[:, (d - 1) * 384:d * 384], T.sem.il0, T.sem.lsm)
     send(s_l1, ["lb1", "s_ip"], ["s_l1"])
     send(s_l0, ["lb0", "s_l1"], ["s_l0"])
-    ext("il0", 24, ["s_l0"], ["ll0"], 6000.0)
-    ext("il1", 24, ["s_l1"], ["ll1"], 8000.0)
+    ext("il0", 3 * ne, ["s_l0"], ["ll0"], 6000.0)
+    ext("il1", 3 * ne, ["s_l1"], ["ll1"], 8000.0)
     for p in range(2):
         dma("G", [(T.LW[:, p * R + 512:(p + 1) * R], T.sg[:, 1152 * p:1152 * p + 1152])], ["ll%d" % p, "s_l0"],
             ["L%dg" % p], lat=3000.0)
@@ -204,18 +220,18 @@ def build(g, core, T, topo, r):
 
     def de(q, a, b, o0, rd, wr):
         for p in range(2):
-            o = T.va[:, 64 * q + 32 * p:64 * q + 32 * p + 32]
+            o = T.uu[:, 64 * q + 32 * p:64 * q + 32 * p + 32]
             if b is None:
-                ts(o, a[:, p:64:2], -512.0, None, A.add, None, 32, rd, [wr + str(p)])
+                aff("A", o, a[:, p:64:2], 1.0, -512.0, 32, rd, [wr + str(p)])
             else:
                 tt(o, a[:, p:64:2], b[:, p:64:2], o0, 32, rd, [wr + str(p)])
     de(0, T.pc, None, None, ["pc"], "va0")
-    cp(T.vh[:, 0:64], T.va[:, 0:64], 64, ["va00", "va01"], ["vh0"])
-    tt(T.vl[:, 0:64], T.va[:, 0:64], T.vh[:, 0:64], A.subtract, 64, ["va00", "va01", "vh0"], ["vl0"])
+    act(T.vh[:, 0:64], T.uu[:, 0:64], F.Identity, 64, ["va00", "va01"], ["vh0"])
+    tt(T.vl[:, 0:64], T.uu[:, 0:64], T.vh[:, 0:64], A.subtract, 64, ["va00", "va01", "vh0"], ["vl0"])
     for p in range(2):
         dma("SA"[p], [(T.PW[h:128:16, p * R:p * R + 512], (T.vh, T.vl)[h][:, 32 * p:32 * p + 32]) for h in range(2)],
             ["vh0", "vl0", "Pz"], ["P%do%d" % (p, c) for c in range(4)])
-    ts(T.u3[:, :], T.rc[:, :], 512.0, None, A.add, None, 64, ["pc"], ["u3"])
+    aff("A", T.u3[:, :], T.rc[:, :], 1.0, 512.0, 64, ["pc"], ["u3"])
     tt(T.u1[:, :], T.u3[:, :], T.pc[:, :], A.add, 64, ["u3", "pc"], ["u1"])
     ts(T.u1[:, :], T.u1[:, :], 1023, None, A.bitwise_and, None, 64, ["u1"], ["u1"])
     tt(T.u2[:, :], T.u3[:, :], T.u1[:, :], A.add, 64, ["u3", "u1"], ["u2"])
@@ -224,101 +240,114 @@ def build(g, core, T, topo, r):
     de(2, T.u2, T.u1, A.subtract, ["u1", "u2"], "va2")
     de(3, T.rc, None, None, ["pc"], "va3")
     vk = ["va%d%d" % (q, p) for q in range(1, 4) for p in range(2)]
-    act(T.vh[:, 64:256], T.va[:, 64:256], F.Identity, 192, vk, ["vh1"])
-    tt(T.vl[:, 64:256], T.va[:, 64:256], T.vh[:, 64:256], A.subtract, 192, vk + ["vh1"], ["vl1"])
+    act(T.vh[:, 64:256], T.uu[:, 64:256], F.Identity, 192, vk, ["vh1"])
+    tt(T.vl[:, 64:256], T.uu[:, 64:256], T.vh[:, 64:256], A.subtract, 192, vk + ["vh1"], ["vl1"])
     for p in range(2):
         dma("S", [(T.PW[2 * q + h:128:16, p * R:p * R + 512], (T.vh, T.vl)[h][:, 64 * q + 32 * p:64 * q + 32 * p + 32])
                   for q in range(1, 4 - p) for h in range(2)], ["vh1", "vl1", "Pz"], ["P%dd" % p])
 
     iota(T.ci[:, 0:1], [[1, 1]], 0, 1, 1, ["ci0"])
     iota(T.cj[:, :], [[1, 144]], 0, -1, 144, ["cj"])
-    iota(T.tm[:, 0:128], [[1, 8], [0, 16]], 0, 0, 128, ["tm0"], True)
-    iota(T.tm[:, 128:256], [[0, 64], [1, 2]], 0, 0, 128, ["tm1"], True)
+    Am, Qw = T.EE[:, 256:384], T.EE[:, 384:528]
+    iota(T.EE[:, 0:256], [[0, 2], [1, 8], [0, 16]], 0, 0, 256, ["tm0"], True)
     iota(T.msk[:, :], [[0, 32], [1, 16]], 0, 0, 512, ["msk"], True)
-    iota(T.ty[:, 0:128], [[16, 128]], 8 - 1024, 0, 128, ["ty"], True)
-    act(T.msk[:, :], T.msk[:, :], F.Sign, 512, ["msk"], ["msk"])
+    iota(T.ty[:, 0:128], [[1, NQ], [16 * NQ, 128 // NQ]], 8 - 1024, 0, 128, ["ty"], True)
+    ts(T.msk[:, :], T.msk[:, :], 1.0, None, A.min, None, 512, ["msk"], ["msk"], k=0.5)
     ts(T.ci[:, 1:2], T.ci[:, 0:1], 15, None, A.bitwise_and, None, 1, ["ci0"], ["ci1"])
     ts(T.ci[:, 2:3], T.ci[:, 0:1], 4, None, A.arith_shift_right, None, 1, ["ci0"], ["ci2"])
     cp(ct[:, 0:2], T.ci[:, 1:3], 2, ["ci1", "ci2"], ["k"])
     kc = ct[:, 0:1]
-    ts(T.Qw[:, :], T.cj[:, :], kc, None, A.add, None, 144, ["cj", "k"], ["Qw"])
-    ts(T.BL[:, :], T.tm[:, 0:128], ct[:, 1:2], None, A.is_equal, None, 128, ["tm0", "k"], ["BL"])
+    ts(Qw, T.cj[:, :], kc, None, A.add, None, 144, ["cj", "k"], ["Qw"])
+    ts(T.BL[:, :], T.EE[:, 0:144], ct[:, 1:2], None, A.is_equal, None, 144, ["tm0", "k"], ["BL"])
+    BL = T.BL[:, 0:128]
     ts(ct[:, 2:3], kc, 1.5, 4096.0, A.is_lt, A.mult, 1, ["k"], ["c2"])
-    ts(T.Wp[:, :], T.Qw[:, :], 15.0, ct[:, 2:3], A.is_equal, A.mult, 144, ["Qw", "c2"], ["Wp"])
+    ts(T.Wp[:, :], Qw, 15.0, ct[:, 2:3], A.is_equal, A.mult, 144, ["Qw", "c2"], ["Wp"])
     ts(ct[:, 7:8], kc, 1.5, -4096.0, A.is_lt, A.mult, 1, ["k"], ["c7"])
-    act(T.NG[:, :], T.BL[:, :], F.Identity, 128, ["BL", "c7"], ["NG"], scale=ct[:, 7:8])
-    ts(T.ci[:, 16:144], T.cj[:, 0:128], 15, None, A.bitwise_and, None, 128, ["cj"], ["ci3"])
-    ts(T.Bo[:, :], T.BL[:, :], 1.0, 100.0, A.subtract, A.mult, 128, ["BL"], ["Bo"])
-    tt(T.Am[:, :], T.ci[:, 16:144], T.Bo[:, :], A.add, 128, ["ci3", "Bo"], ["Am"])
+    act(T.NG[:, :], BL, F.Identity, 128, ["BL", "c7"], ["NG"], scale=ct[:, 7:8])
+    ts(T.Ti[:, 0:128], T.cj[:, 0:128], 15, None, A.bitwise_and, None, 128, ["cj"], ["Ti00", "Ti01"])
+    ts(B[1][:, 512:640], BL, 1.0, 100.0, A.subtract, A.mult, 128, ["BL"], ["M1"], [1])
+    tt(Am, T.Ti[:, 0:128], B[1][:, 512:640], A.add, 128, ["Ti00", "Ti01", "M1"], ["Am"], [1])
     Ip = B[0][:, 0:128]
-    ts(Ip, T.Am[:, :], 0.0, None, A.is_equal, None, 128, ["Am"], ["M0"], [0])
+    ts(Ip, Am, 0.0, None, A.is_equal, None, 128, ["Am"], ["M0"], [0])
     act(T.If[:, :], Ip, F.Identity, 128, ["M0"], ["If"], [0])
-    cp(T.Ih[:, :], Ip, 128, ["M0"], ["Ih"], [0])
+    act(T.Ih[:, :], T.If[:, :], F.Identity, 128, ["If"], ["Ih"])
     iota(T.ty[:, 128:136], [[1, 8]], 1, 0, 8, ["I8"], True)
     ts(ct[:, 9:17], T.ty[:, 128:136], kc, 15.5, A.add, A.is_ge, 8, ["k", "I8"], ["bs"])
-    ts(ct[:, 9:17], ct[:, 9:17], -0.5, None, A.add, None, 8, ["bs"], ["bs"])
+    ts(ct[:, 9:17], ct[:, 9:17], -4096.0, 2048.0, A.mult, A.add, 8, ["bs"], ["bs"])
+    act(T.Ib[:, :], Ip, F.Identity, 128, ["M0"], ["Ib"], [0])
     for d in range(1, 9):
-        o = T.Df[:, 128 * (d - 1):128 * d]
-        ts(o, T.Am[:, :], 16.0 - d, None, A.is_equal, None, 128, ["Am"], ["Df%d" % d])
-        tt(o, Ip, o, A.subtract, 128, ["M0", "Df%d" % d], ["Df%d" % d], [0])
+        o, x = T.Rk[:, 128 * (d - 1):128 * d], T.Sd[:, 128 * (d - 1):128 * d]
+        k = "Sd0%d" % ((d - 1) // 4)
+        ts(x, Am, float(d), None, A.is_equal, None, 128, ["Am"], [k, "x%d" % d])
+        tt(x, Ip, x, A.subtract, 128, ["M0", "x%d" % d], ["x%d" % d], [0])
+        if d == 8:
+            act(o, T.Ib[:, :], F.Identity, 128, ["Ib", "bs"], ["Rq8"], scale=ct[:, 16:17])
+            o = x
+        act(o, x, F.Identity, 128, ["x%d" % d, "bs"], ["Rk%d" % d, k], scale=ct[:, 8 + d:9 + d])
         h, j = divmod(d - 1, 4)
-        mm([(B[2 + h][:, 128 * j:128 * j + 128], o if d < 8 else T.Ih[:, :], T.Ih[:, :])], 128, ["Df%d" % d, "Ih"], ["D%d" % d], [2 + h])
+        mm([(B[2 + h][:, 128 * j:128 * j + 128], o, T.Ib[:, :])], 128, ["Rk%d" % d, "Ib", k], ["D%d" % h], [2 + h])
     for h in range(2):
-        act(T.Rk[:, 512 * h:512 * h + 512], B[2 + h][:, :], F.Identity, 512, ["D%d" % (4 * h + j + 1) for j in range(4)],
-            ["Rk%d" % h], [2 + h], scale=32.0)
-    ts(T.Wc[:, :], T.Qw[:, :], 15.0, None, A.is_equal, None, 144, ["Qw"], ["Wc"])
-    ts(T.W1[:, :], T.Qw[:, :], 14.0, None, A.is_equal, None, 144, ["Qw"], ["W1"])
-    tt(T.W1[:, :], T.Wc[:, :], T.W1[:, :], A.subtract, 144, ["Wc", "W1"], ["W1"])
-    ts(T.Z1[:, :], T.Qw[:, 0:128], 0.0, None, A.is_equal, None, 128, ["Qw"], ["Z1"])
-    ts(T.W64[:, :], T.W1[:, :], 64.0, None, A.mult, None, 144, ["W1"], ["W64"], k=0.5)
-    ts(T.Z64[:, :], T.Z1[:, :], 64.0, None, A.mult, None, 128, ["Z1"], ["Z64"], k=0.5)
-    act(T.fad[:, :], T.fad[:, :], F.Identity, 1024, ["fad"], ["fad"], scale=0.125)
+        aff("A", T.Df[:, 512 * h:512 * h + 512], B[2 + h][:, :], 2.0 ** -11, 0.0, 512, ["D%d" % h], ["Df%d" % h], [2 + h])
+    ts(T.Wc[:, :], Qw, 15.0, None, A.is_equal, None, 144, ["Qw"], ["Wc"])
+    ts(T.W1[:, 0:144], Qw, 14.0, None, A.is_equal, None, 144, ["Qw"], ["W1"])
+    tt(T.W1[:, 0:144], T.Wc[:, :], T.W1[:, 0:144], A.subtract, 144, ["Wc", "W1"], ["W1"])
+    ts(T.W1[:, 144:272], T.EE[:, 384:512], 0.0, None, A.is_equal, None, 128, ["Qw"], ["Z1"])
+    for j in range(2):
+        aff("A", T.Wh[:, 272 * j:272 * j + 272], T.W1[:, :], 64.0 ** -j, 0.0, 272, ["W1", "Z1"], ["Wh%d" % j])
+    ts(Qw, Qw, float(NQ), kc, A.mult, A.subtract, 144, ["Qw", "k"], ["Qw"])
+    for q in range(NQ):
+        ts(T.Pm[:, 144 * q:144 * q + 144], Qw, float(NQ * (16 - G) - q), 4096.0, A.is_equal, A.mult, 144, ["Qw"], ["Pm%d" % q])
+    aff("A", T.fad[:, :], T.fad[:, :], 0.125, 0.0, 1024, ["fad"], ["fad"])
     ts(ct[:, 3:4], kc, 0.0, None, A.is_equal, None, 1, ["k"], ["c3"])
-    ts(T.Wt[:, :], T.Wc[:, :], ct[:, 3:4], None, A.mult, None, 144, ["Wc", "c3"], ["Wt"], k=0.5)
-    ts(ct[:, 4:5], kc, 1.0, 4160.0, A.add, A.mult, 1, ["k"], ["c4"])
-    ts(ct[:, 5:6], kc, 15.0, -(65.0 * 7680 + 16 * 4160.0), A.is_equal, A.mult, 1, ["k"], ["c5"])
+    aff("A", T.Wt[:, :], T.Wc[:, :], ct[:, 3:4], 0.0, 144, ["Wc", "c3"], ["Wt"])
+    ts(ct[:, 4:5], kc, -15.0, 4096.0, A.add, A.mult, 1, ["k"], ["c4"])
+    ts(ct[:, 5:6], ct[:, 3:4], 16 * 30720.0, None, A.mult, None, 1, ["c3"], ["c5"])
     tt(ct[:, 4:5], ct[:, 4:5], ct[:, 5:6], A.add, 1, ["c4", "c5"], ["c4"])
-    ts(ct[:, 5:6], ct[:, 4:5], -float(R), None, A.add, None, 1, ["c4"], ["c5"])
+    aff("A", ct[:, 5:6], ct[:, 4:5], 2.0, -2.0 * R, 1, ["c4"], ["c5"])
+    aff("A", ct[:, 27:28], ct[:, 4:5], 65.0 / 64, 0.0, 1, ["c4"], ["c4h"])
+    aff("A", ct[:, 28:29], ct[:, 27:28], 2.0, -2.0 * R, 1, ["c4h"], ["c5h"])
     ts(ct[:, 6:7], ct[:, 3:4], 16.0, kc, A.mult, A.add, 1, ["c3", "k"], ["c6"])
     act(T.cb[:, 0:1], ct[:, 6:7], F.Sigmoid, 1600, ["c6"], ["cb"], bias=-40.0 * LN2, scale=LN2)
-    ts(T.FW[:, 0:128], T.BL[:, :], T.cb[:, 0:1], 2.0 ** 59, A.mult, A.mult, 128, ["BL", "cb"], ["FW0"])
-    ts(T.FW[:, 128:256], T.BL[:, :], ct[:, 3:4], 2.0 ** 19, A.mult, A.mult, 128, ["BL", "c3"], ["FW1"])
-    act(T.I4[:, :], T.If[:, :], F.Identity, 128, ["If"], ["I4"], scale=4096.0)
-    ts(T.jc[:, :], T.ty[:, 0:128], kc, None, A.add, None, 128, ["ty", "k"], ["jc"])
-    ts(T.slf[:, :], T.ty[:, 0:32], kc, 1016.0, A.add, A.add, 32, ["ty", "k"], ["slf"])
-    ts(T.slf[:, :], T.slf[:, :], 2.0, None, A.mult, None, 32, ["slf"], ["slf"])
-    tt(T.Bo[:, :], T.BL[:, :], T.tm[:, 128:256], A.mult, 128, ["BL", "tm1"], ["Bo"])
-    ts(T.SA[:, :], T.Bo[:, :], 0.5, None, A.mult, None, 128, ["Bo"], ["SA"])
+    aff("A", ct[:, 30:31], T.cb[:, 0:1], 2.0 ** 59, 0.0, 1, ["cb"], ["c30"])
+    aff("A", ct[:, 31:32], ct[:, 3:4], 2.0 ** 19, 0.0, 1, ["c3"], ["c31"])
+    for j in range(2):
+        aff("A", T.FW[:, 128 * j:128 * j + 128], BL, ct[:, 30 + j:31 + j], 0.0, 128, ["BL", "c3%d" % j], ["FW%d" % j])
+    aff("A", ct[:, 26:27], kc, float(NQ), 0.0, 1, ["k"], ["k2"])
+    aff("A", T.jc[:, :], T.ty[:, 0:128], 1.0, ct[:, 26:27], 128, ["ty", "k2"], ["jc"])
+    aff("A", T.slf[:, :], T.jc[:, 0:32], 2.0 / NQ, 2032.0 / NQ - 2 * R, 32, ["jc"], ["slf"])
+    act(T.SA[:, :], T.BL[:, :], F.Identity, 144, ["BL"], ["SA"])
+    ts(T.cj[:, 0:128], T.cj[:, 0:128], 127, None, A.bitwise_and, None, 128, ["cj"], ["cj"])
+    ts(T.Sh[:, :], T.cj[:, 0:128], 16.0, None, A.is_equal, None, 128, ["cj"], ["Sh"])
     ts(ct[:, 20:21], kc, 1.5, None, A.is_lt, None, 1, ["k"], ["r0"])
     ts(ct[:, 21:22], kc, 3.5, None, A.is_lt, None, 1, ["k"], ["r1"])
     ts(ct[:, 22:23], kc, 5.5, ct[:, 21:22], A.is_lt, A.subtract, 1, ["k", "r1"], ["r2"])
     ts(ct[:, 25:26], kc, 5.5, None, A.is_lt, None, 1, ["k"], ["r5"])
     ts(ct[:, 23:24], kc, 7.5, ct[:, 25:26], A.is_lt, A.subtract, 1, ["k", "r5"], ["r3"])
     ts(ct[:, 24:25], kc, 1.0, None, A.is_equal, None, 1, ["k"], ["r4"])
-    for j in range(4):
-        act(T.SB[:, 128 * j:128 * j + 128], T.Bo[:, :], F.Identity, 128, ["Bo", "r%d" % j], ["SB%d" % j],
+    for j in range(5):
+        act(T.SB[:, 144 * j:144 * j + 144], T.BL[:, :], F.Identity, 144, ["BL", "r%d" % j], ["SB%d" % j],
             scale=ct[:, 20 + j:21 + j])
-    ts(T.tm[:, 0:128], T.Bo[:, :], -2.0, None, A.mult, None, 128, ["Bo"], ["tm0"])
-    tt(T.tm[:, 0:128], T.tm[:, 0:128], T.BL[:, :], A.add, 128, ["tm0", "BL"], ["tm0"])
-    act(T.SB[:, 512:640], T.tm[:, 0:128], F.Identity, 128, ["tm0", "r4"], ["SB4"], scale=ct[:, 24:25])
     for c in range(4):
-        op("V", lambda c=c: V.memset(T.xx[:, c * XW:c * XW + 8], 0.0), vc(8), [], ["xz%d" % c])
+        iota(T.xx[:, c * XW:c * XW + 8], [[0, 8]], 0, 0, 8, ["xz%d" % c], True)
 
     Z = B[4][:, 256:512]
 
     def decode(p):
         for h in range(2):
             e = T.nbr[:, 512 * h + p:512 * h + 512:2]
-            hs = slice(256 * h, 256 * h + 256)
             ps_ = slice(512 * p + 256 * h, 512 * p + 256 * h + 256)
             ek, k = "nb%d" % p, "%d%d" % (p, h)
-            ts(T.t1[:, hs], e, 1, 2047, A.arith_shift_right, A.bitwise_and, 256, [ek], ["t1%d" % h])
-            ts(T.t2[:, hs], e, 1, None, A.bitwise_and, None, 256, [ek], ["t2%d" % h])
-            ts(Z, T.t2[:, hs], float(R - 2 * R * p), float(R * p), A.mult, A.add, 256, ["t2%d" % h], ["Z"], [4])
-            tt(T.t1[:, hs], Z, T.t1[:, hs], A.add, 256, ["Z", "t1%d" % h], ["t1%d" % h], [4])
-            cp(T.ua[:, ps_], T.t1[:, hs], 256, ["t1%d" % h], ["ua" + k])
-            ts(T.hi[:, ps_], T.t1[:, hs], 6, None, A.arith_shift_right, None, 256, ["t1%d" % h], ["hi" + k])
-            ts(T.lo[:, ps_], T.t1[:, hs], 63, None, A.bitwise_and, None, 256, ["t1%d" % h], ["lo" + k])
+            ts(T.t1[:, :], e, 1, 2047, A.arith_shift_right, A.bitwise_and, 256, [ek], ["t1"])
+            ts(T.t2[:, :], e, 1, None, A.bitwise_and, None, 256, [ek], ["t2"])
+            aff("A", Z, T.t2[:, :], float(R - 2 * R * p), float(R * p), 256, ["t2"], ["Z"], [4])
+            tt(T.ua[:, ps_], Z, T.t1[:, :], A.add, 256, ["Z", "t1"], ["ua" + k], [4])
+            if 2 * h not in TWO:
+                continue
+            o = 256 * (len(TWO) * p + h)
+            x = T.hl[:, o + 128:o + 256]
+            aff("A", x, T.ua[:, ps_.start:ps_.start + 128], 64.0, 0.0, 128, ["ua" + k], ["lo" + k])
+            ts(T.hl[:, o:o + 128], x, 6, 0xFC0, A.arith_shift_right, A.bitwise_and, 128, ["lo" + k], ["hi" + k])
+            ts(x, x, 0xFC0, None, A.bitwise_and, None, 128, ["lo" + k], ["lo" + k])
 
     decode(0)
     decode(1)
@@ -344,59 +373,79 @@ def build(g, core, T, topo, r):
             for h in range(2):
                 o = 512 * p + 128 * c + 64 * h
                 po, pi = T.pg[:, 2048 * b + 1024 * h:2048 * b + 1024 * h + 1024], Pwin.indirect(T.ua[:, o:o + 64])
-                if "p%d%d%d" % (t, c, h) in ONV:
+                if "%d%d%d" % (t, c, h) in ONV:
                     cp(po, pi, 1024, Pk + ["ua" + hk], ["pg%d%d" % (b, h)], k=GA)
                 else:
                     act(po, pi, F.Identity, 1024, Pk + ["ua" + hk], ["pg%d%d" % (b, h)], k=GA)
             tag[0] = tg + 1
-            Tp = B[6][:, 384:512]
-            mm([(Tp, T.Wp[:, 15 - k:143 - k], T.pg[:, 2048 * b + k:2048 * b + 2048:16]) for k in range(16)]
-               + [(Tp, T.NG[:, :], T.PW[:, own])], 17 * 128, ["pg%d0" % b, "pg%d1" % b, "Wp", "NG", "P%do%d" % (t, c)], ["T"], [6])
-            tt(T.Ti[:, bs], Tp, T.nbr[:, 256 * c + p:256 * c + 256:2], A.add, 128, ["T", "nb%d" % p], ["Ti" + sb_], [6])
-            ts(T.ai[:, bs], T.Ti[:, bs], 12, 1023, A.arith_shift_right, A.bitwise_and, 128, ["Ti" + sb_], ["ai" + sb_])
-            ts(T.ac[:, cs], T.ai[:, bs], -512.0, None, A.add, None, 128, ["ai" + sb_], ["ac" + sc])
-            for h in range(2):
-                ds = range(4 * h + 1, 4 * h + 5)
-
-                def dfn(ds=ds, h=h, cs=cs):
-                    for j, d in enumerate(ds):
-                        o, l = B[2 + h][:, 128 * j:128 * j + 128], T.Df[:, 128 * (d - 1):128 * d]
-                        ins = P.matmul(o, l, T.ac[:, cs], True, True)
-                    return ins
-                op("P", dfn, OV + PCY * 512, ["ac" + sc] + ["Df%d" % d for d in ds], ["D%d" % d for d in ds], [2 + h])
-                for j, d in enumerate(ds):
-                    o = 1024 * b + 128 * (d - 1)
-                    act(T.Sd[:, o:o + 128], B[2 + h][:, 128 * j:128 * j + 128], F.Sign, 128, ["D%d" % d, "bs"],
-                        ["Sd%d%d" % (b, d)], [2 + h], bias=ct[:, 8 + d:9 + d])
-            Rp = B[5][:, 0:128]
-            js = [j for j in range(8) for _ in range(1 + ("s%d%d%d" % (t, c, j // 4) in ONV))]
-            mm([(Rp, T.Rk[:, 128 * j:128 * j + 128], T.Sd[:, 1024 * b + 128 * j:1024 * b + 128 * j + 128]) for j in js],
-               len(js) * 128, ["Sd%d%d" % (b, d) for d in range(1, 9)] + ["Rk0", "Rk1"], ["R"], [5])
-            mo = 4096 * b
-            tt(T.mm[:, mo:mo + 128], Rp, T.hi[:, pcs], A.add, 128, ["R", "hi" + hk], ["m%d_0" % b], [5])
-            tt(T.mm[:, mo + 128:mo + 256], Rp, T.lo[:, pcs], A.add, 128, ["R", "lo" + hk], ["wl" + sb_], [5])
-            act(T.p2[:, cs], Rp, F.Sigmoid, 128, ["R"], ["p2" + sc], [5], bias=-27.5 * LN2, scale=-LN2 / 64)
-            for s in range(1, 16):
-                ts(T.mm[:, mo + 256 * s:mo + 256 * s + 256], T.mm[:, mo:mo + 256], 64.0 * s - 480, None, A.max, None, 256,
-                   ["m%d_0" % b, "wl" + sb_], ["m%d_%d" % (b, s)], k=0.5)
-            Op = B[4][:, bs]
-            its = [(Op, T.Z64[:, :], T.mm[:, mo:mo + 128]), (Op, T.Z1[:, :], T.mm[:, mo + 128:mo + 256])]
-            for s in range(1, 16):
-                o = mo + 256 * s
-                its += [(Op, T.W64[:, 15 - s:143 - s], T.mm[:, o:o + 128]), (Op, T.W1[:, 15 - s:143 - s], T.mm[:, o + 128:o + 256])]
-            for q in range(2):
-                mm(its[16 * q:16 * q + 16], 16 * 128, ["Z1", "Z64", "W1", "W64", "wl" + sb_] + ["O" + sb_] * q
-                   + ["m%d_%d" % (b, s) for s in range(8 * q, 8 * q + 8)], ["O" + sb_, "G4"], [4], first=q == 0, last=q == 1)
-            ts(T.us[:, cs], Op, ct[:, 4:5], None, A.add, None, 128, ["O" + sb_, "c4"], ["us" + sc], [4])
+            for h0, h1 in ([(0, 1), (1, 2)] if c in HALF else [(0, 2)]):
+                w = 64 * (h1 - h0)
+                ky = lambda a: [a + str(h) for h in range(h0, h1)]
+                sl = lambda o: slice(o + 64 * h0, o + 64 * h1)
+                Tp = B[6][:, sl(384)]
+                mm([(Tp, T.Wp[:, 15 - k:143 - k], T.pg[:, 2048 * b + 1024 * h0 + k:2048 * b + 1024 * h1:16]) for k in range(16)]
+                   + [(Tp, T.NG[:, :], T.PW[:, sl(own.start)])], 17 * w, ky("pg" + sb_) + ["Wp", "NG", "P%do%d" % (t, c)], ky("T"), [6])
+                tt(T.Ti[:, sl(128 * b)], Tp, T.nbr[:, 256 * c + 128 * h0 + p:256 * c + 128 * h1:2], A.add, w, ky("T") + ["nb%d" % p],
+                   ky("Ti" + sb_), [6])
+                ts(T.Ti[:, sl(128 * b)], T.Ti[:, sl(128 * b)], 12, 1023, A.arith_shift_right, A.bitwise_and, w, ky("Ti" + sb_), ky("Ti" + sb_))
+                aff("V" if c in HALF else "A", T.ac[:, sl(128 * c)], T.Ti[:, sl(128 * b)], 1.0, -512.0, w, ky("Ti" + sb_), ky("ac" + sc))
+                for h in range(h0, h1):
+                    def dfn(h=h, x=T.ac[:, 128 * c + 64 * h:128 * c + 64 * h + 64]):
+                        for j in range(8):
+                            ins = P.matmul(B[2 + h][:, 64 * j:64 * j + 64], T.Df[:, 128 * j:128 * j + 128], x, True, True)
+                        return ins
+                    op("P", dfn, OV + PCY * 512, ["ac%d%d" % (c, h), "Df0", "Df1"], ["D%d" % h], [2 + h])
+                    o = 1024 * b + 512 * h
+                    act(T.Sd[:, o:o + 512], B[2 + h][:, :], F.Sign, 512, ["D%d" % h], ["Sd%d%d" % (b, h)], [2 + h], bias=-0.5)
+                    mm([(B[5][:, 64 * h:64 * h + 64], T.Rk[:, 128 * j:128 * j + 128], T.Sd[:, o + 64 * j:o + 64 * j + 64]) for j in range(8)],
+                       512, ["Sd%d%d" % (b, h), "Rq8"] + ["Rk%d" % d for d in range(1, 9)], ["R%d" % h], [5])
+                Rp = B[5][:, sl(0)]
+                two = c in TWO
+                mk = lambda s: ky("m%d_%d_" % (2 if two else b, s))
+                Op = B[4][:, sl(128 * b)]
+                wt = lambda W, a, s: W[:, a + 15 - s:a + 143 - s] if s else W[:, a + 144:a + 272]
+                if two:
+                    mo = 128 * h0
+                    for j in range(2):
+                        tt(T.mh[:, mo + w * j:mo + w * j + w], Rp, T.hl[:, sl(256 * (len(TWO) * p + c // 2) + 128 * j)], A.add, w,
+                           ky("R") + [("hi", "lo")[j] + hk], mk((0, 16)[j]), [5])
+                    for s in range(1, 16):
+                        ts(T.mh[:, mo + 256 * s:mo + 256 * s + 2 * w], T.mh[:, mo:mo + 2 * w], 30720.0 - 4096.0 * s, 0.0, A.add, A.max,
+                           2 * w, mk(0) + mk(16), mk(s), k=0.5)
+                    its = [(Op, wt(T.Wh, 272 * j, s), T.mh[:, mo + 256 * s + w * j:mo + 256 * s + w * j + w])
+                           for s in range(16) for j in range(2)]
+                    nq, cy = 2, 16 * w
+                else:
+                    mo = 2048 * (1 - b)
+                    key = T.mm[:, sl(mo)]
+                    tt(key, Rp, T.ua[:, sl(pcs.start)], A.add, w, ky("R") + ["ua" + hk], mk(0), [5])
+                    onv = [s for s in range(1, 16) if (s * NV[t][c]) // 15 > ((s - 1) * NV[t][c]) // 15]
+                    for s in range(1, 16):
+                        o, th = T.mm[:, sl(mo + 128 * s)], 30720.0 - 4096.0 * s
+                        if s in onv:
+                            ts(o, key, th, 0.0, A.add, A.max, w, mk(0), mk(s))
+                        else:
+                            act(o, key, F.Relu, w, mk(0), mk(s), bias=th)
+                    its = [(Op, wt(T.W1, 0, s), T.mm[:, sl(mo + 128 * s)]) for s in range(16)]
+                    nq, cy = 4, 16 * w
+                act(T.p2[:, sl(128 * c)], Rp, F.Sigmoid, w, ky("R"), ky("p2" + sc), [5], bias=-27.5 * LN2, scale=-LN2 / 4096)
+                for q in range(nq):
+                    m = len(its) // nq
+                    mm(its[m * q:m * q + m], cy, ["Z1", "W1", "Wh0", "Wh1"] + ky("O" + sb_) * (q > 0) + mk(16) * two
+                       + [k for s in range(16 // nq * q, 16 // nq * (q + 1)) for k in mk(s)], ky("O" + sb_) + ["G4"], [4],
+                       first=q == 0, last=q == nq - 1)
+                aff("A", T.us[:, sl(128 * c)], Op, 1.0, ct[:, 27:28] if two else ct[:, 4:5], w, ky("O" + sb_) + ["c4", "c4h"],
+                    ky("us" + sc), [4])
             if t < 3:
-                ts(T.cp[:, cs], Op, ct[:, 5:6], None, A.add, None, 128, ["O" + sb_, "c5"], ["cp" + sc], [4])
+                aff("A", T.cp[:, cs], B[4][:, bs], 2.0, ct[:, 28:29] if two else ct[:, 5:6], 128, ["O%d0" % b, "O%d1" % b, "c5", "c5h"],
+                    ["cp" + sc], [4])
             tag[0] = tg + 2
             xo = c * XW + 8
             do = 2048 * c
             for h in range(2):
                 xk, dk = "x%d%d" % (c, h), "d%d%d" % (c, h)
                 act(T.xx[:, xo + 1024 * h:xo + 1024 * h + 1024], Lwin.indirect(T.us[:, 128 * c + 64 * h:128 * c + 64 * h + 64]),
-                    F.Identity, 1024, Lk + ["us" + sc], [xk], k=GA)
+                    F.Identity, 1024, Lk + ["us%d%d" % (c, h)], [xk], k=GA)
                 for j in range(2):
                     o = 1024 * h + 512 * j
                     op("V", lambda j=j, o=o, xo=xo: V.tensor_tensor_scan(
@@ -408,15 +457,26 @@ def build(g, core, T, topo, r):
                     o = 1024 * h
                     tt(B[5][:, 384 + 64 * h:448 + 64 * h], T.xx[:, xo + o + 15:xo + o + 1024:16], T.MM[:, 15:1024:16], A.max, 64,
                        [xk, "M0", "M1"], ["X%d" % h], [0, 1, 5])
-                act(T.sg[:, 2048 * b + 1024 * h:2048 * b + 1024 * h + 1024], T.dd[:, do + 1024 * h:do + 1024 * h + 1024], F.Sign,
-                    1024, [dk + "0", dk + "1"], ["sg%d%d" % (b, h)] + ["los", "lou", "ll0", "ll1"] * (t + c + h == 0), bias=-1e-9)
+                so, dv = T.sg[:, 2048 * b + 1024 * h:2048 * b + 1024 * h + 1024], T.dd[:, do + 1024 * h:do + 1024 * h + 1024]
+                sk = ["sg%d%d" % (b, h)]
+                s0 = [dk + "0", dk + "1"] + ["L0g", "L1g", "lb0", "lb1", "L0o0", "L1o0"] * (t == 0 and c < 2)
+                if c >= SGN[t]:
+                    act(so, dv, F.Sign, 1024, s0, sk, bias=-1e-9)
+                else:
+                    for j in range(2):
+                        o = 1024 * h + 512 * j
+                        op("G", lambda a=T.sg[:, 2048 * b + o:2048 * b + o + 512], x=T.dd[:, do + o:do + o + 512]:
+                           g.affine_select(a, x, [[0, 512]], A.is_ge, 0.0, 0, 0), 170 + 2 * CY * 512, [dk + str(j)] + s0[2:] + sk * j, sk)
+                    ts(so, so, 0.0, 0.5, A.is_gt, A.subtract, 1024, sk, sk, k=0.5)
             if t < 4:
                 X = B[5][:, 384:512]
                 Xk = ["X%d" % q for q in range(2)]
                 ok = "L%do%d" % (t, c)
                 tt(X, X, T.LW[:, own], A.subtract, 128, Xk + [ok], Xk, [5])
-                act(T.uu[:, bs], T.LW[:, own], F.Identity, 128, [ok], ["uu" + sb_], scale=8.0)
-                tt(X, X, T.uu[:, bs], A.add, 128, Xk + ["uu" + sb_], Xk, [5])
+                if c == 0:
+                    act(T.uu[:, :], T.LW[:, t * R:t * R + 512], F.Identity, 512,
+                        ["L%do%d" % (t, j) for j in range(4)] + ["vl0", "vl1"] * (t == 0), ["uu"], scale=8.0)
+                tt(X, X, T.uu[:, cs], A.add, 128, Xk + ["uu"], Xk, [5])
                 tt(T.LW[:, new], X, T.fad[:, 256 * c + p:256 * c + 256:2], A.mult, 128, Xk + ["fad"], ["L%do%d" % (t + 2, c)], [5])
             tag[0] = tg + 3
             parts = [(0, 1), (1, 2)] if (t, c) == (4, 3) else [(0, 2)]
@@ -427,101 +487,135 @@ def build(g, core, T, topo, r):
                 cq, fq = B[6][:, 64 * h0:64 * h1], T.fs[:, 128 * b + 64 * h0:128 * b + 64 * h1]
                 mm([(cq, T.Wc[:, 15 - s:143 - s], T.sg[:, 2048 * b + 1024 * h0 + s:2048 * b + 1024 * h1:16]) for s in range(1, 16)],
                    15 * w, ky("sg" + sb_) + ["Wc"], ky("C"), [6])
-                act(fq, cq, F.Sign, w, ky("C"), ky("fs" + sb_), [6], bias=11.0)
-                uq = B[5][:, 128 + 64 * h0:128 + 64 * h1]
-                mm([(uq, T.I4[:, :], fq), (uq, T.Ih[:, :], T.jc[:, 64 * h0:64 * h1])], 2 * w, ky("fs" + sb_) + ["I4", "Ih", "jc"],
-                   ky("U"), [5])
-                ts(T.um[:, 128 * c + 64 * h0:128 * c + 64 * h1], uq, -3072.0, None, A.add, None, w, ky("U"), ky("um" + sc), [5])
+                act(fq, cq, F.Sign, w, ky("C"), ky("fs" + sb_), [6], bias=11.0 if c >= SGN[t] else 5.5)
+
+                def ufn(h0=h0, h1=h1, b=b, m=w // NQ):
+                    for q in range(NQ):
+                        o, a = B[5][:, 128 + 64 * h0 + m * q:128 + 64 * h0 + m * q + m], (128 * q + 64 * h0) // NQ
+                        for vb in range(NQ):
+                            z = 144 * q + 16 - G - G * vb
+                            P.matmul(o, T.Pm[:, z:z + 128], T.fs[:, 128 * b + 64 * h0 + vb:128 * b + 64 * h1:NQ], vb == 0, False)
+                        ins = P.matmul(o, T.Ih[:, :], T.jc[:, a:a + m], False, True)
+                    return ins
+                op("P", ufn, OV + PCY * 64 * NQ * (NQ + 1), ky("fs" + sb_) + ["Pm%d" % q for q in range(NQ)] + ["Ih", "jc"], ky("U"), [5])
+                aff("A", T.um[:, 128 * c + 64 * h0:128 * c + 64 * h1], B[5][:, 128 + 64 * h0:128 + 64 * h1], 1.0, -3072.0, w,
+                    ky("U"), ky("um" + sc), [5])
             Fp = B[5][:, 256:384]
-            mm([(Fp, T.FW[:, 0:128], T.fs[:, bs]), (Fp, T.FW[:, 128:256], T.fs[:, bs])], 256, ["fs%d0" % b, "fs%d1" % b, "FW0", "FW1"], ["F"], [5])
-            tt(T.yy[:, cs], Fp, T.p2[:, cs], A.mult, 128, ["F", "p2" + sc], ["yy" + sc], [5])
-            act(T.ls[:, bs], T.yy[:, cs], F.Abs, 128, ["yy" + sc], ["ls" + sb_], bias=-1.5)
-            act(Fp, T.ls[:, bs], F.Sign, 128, ["ls" + sb_], ["F"], [5], bias=0.5, scale=-1.0)
-            tt(T.la[:, bs], Fp, T.ac[:, cs], A.mult, 128, ["F", "ac" + sc], ["la" + sb_], [5])
+            mm([(Fp, T.FW[:, 0:128], T.fs[:, bs]), (Fp, T.FW[:, 128:256], T.fs[:, bs])], 256, ["fs%d0" % b, "fs%d1" % b, "FW0", "FW1"],
+               ["F"], [5])
+            tt(T.yy[:, cs], Fp, T.p2[:, cs], A.mult, 128, ["F", "p2%d0" % c, "p2%d1" % c], ["yy" + sc], [5])
+            ts(Fp, T.yy[:, cs], 2.0 ** 23 - 0.5, 2.0 ** 23 + 1, A.add, A.is_equal, 128, ["yy" + sc], ["F"], [5])
+            tt(T.la[:, bs], Fp, T.ac[:, cs], A.mult, 128, ["F", "ac%d0" % c, "ac%d1" % c], ["la" + sb_], [5])
             base = slice(p * R + 128 * c, p * R + 128 * c + 128)
 
-            def sm(o):
-                its = [(o, T.SA[:, :], T.la[:, bs]), (o, T.SA[:, :], T.ac[:, cs])]
+            def sm(o, a=0):
+                its = [(o, T.SA[:, a:a + 128], T.la[:, bs])]
                 if t < 2:
-                    return its + [(o, T.SB[:, 128:256], T.PW[:, own])]
-                j = 1 + t // 2
-                return its + [(o, T.SB[:, 0:128], T.PW[:, own]), (o, T.SB[:, 128 * j:128 * j + 128], T.PW[:, base])]
-            sk = ["la" + sb_, "ac" + sc, "SA", "SB0", "SB1", "SB2", "SB3", "P%do%d" % (t, c), "P%dd" % p, "P%do%d" % (p, c)]
+                    return its + [(o, T.SB[:, 144 + a:272 + a], T.PW[:, own])]
+                j = 144 * (1 + t // 2) + a
+                return its + [(o, T.SB[:, a:a + 128], T.PW[:, own]), (o, T.SB[:, j:j + 128], T.PW[:, base])]
+            sk = ["la" + sb_, "SA", "SB0", "SB1", "SB2", "SB3", "P%do%d" % (t, c), "P%dd" % p, "P%do%d" % (p, c)]
             S1, S2 = B[6][:, 128:256], B[6][:, 256:384]
-            mm(sm(S1), 384, sk, ["S1"], [6])
-            if t < 4:
-                act(T.Ht[:, bs], S1, F.Identity, 128, ["S1"], ["Ht" + sb_], [6])
-                mm(sm(S2) + [(S2, T.SB[:, 512:640], T.Ht[:, bs])], 512, sk + ["Ht" + sb_, "SB4"], ["S2"], [6])
-                act(T.PW[:, new], S2, F.Identity, 128, ["S2"], ["P%do%d" % (t + 2, c)], [6])
+            if t < 4 and c < 3:
+                mm(sm(S2, 16), 128 * len(sm(S2)), sk, ["S2"], [6])
+                aff("V", T.Hs[:, :], S2, ct[:, 24:25], 0.0, 128, ["S2", "r4"], ["Hs"], [6])
+                tt(T.Ps[:, cs], S2, T.Hs[:, :], A.subtract, 128, ["S2", "Hs"], ["Ps" + sc], [6])
+                op("G", lambda t=t, c=c, cs=cs: fan(g, T, topo, core, r, T.Ps[:, cs],
+                                                    lambda d: T.PW[:, gcol(t + 2, d, c):gcol(t + 2, d, c) + 128],
+                                                    T.sem["ap%d" % t], T.sem["lp%d" % c]),
+                   800.0, ["Ps" + sc], ["sP%d" % (3 * t + c)], tok=("lp" + sc, ne * (t + 1)), lat=2500.0)
+                mm([(S1, T.Sh[:, :], T.Ps[:, cs])], 128, ["Sh", "Ps" + sc], ["S1"], [6])
+                act(T.PW[:, new], S1, F.Identity, 128, ["S1"], ["P%do%d" % (t + 2, c)], [6])
+            if t >= 3 or c == 3:
+                mm(sm(S1), 128 * len(sm(S1)), sk, ["S1"], [6])
+            if t < 4 and c == 3:
+                aff("V", T.Hs[:, :], S1, ct[:, 24:25], 0.0, 128, ["S1", "r4"], ["Hs"], [6])
+                tt(T.PW[:, new], S1, T.Hs[:, :], A.subtract, 128, ["S1", "Hs"], ["P%do%d" % (t + 2, c)], [6])
             if t >= 3:
                 act(T.hq[:, bs], S1, F.Identity, 128, ["S1"], ["hq" + sb_], [6], bias=196607.5, scale=-1.0)
-                mm(sm(S1) + [(S1, T.SB[:, 0:128], T.hq[:, bs])], 640, sk + ["hq" + sb_], ["S1"], [6])
-                act(T.LW[:, 256 * c + p:256 * c + 256:2], S1, F.Identity, 128, ["S1"],
-                    ["yo%d%d" % (p, c)] + ["L0o0", "L0o1", "L0o2", "L0o3", "L0g"] * (t == 3 and c == 0), [6], bias=512.0 - 393216.0)
+                mm(sm(S2) + [(S2, T.SB[:, 576:704], T.hq[:, bs])], 512, sk + ["hq" + sb_, "SB4"], ["S2"], [6])
+                act(T.LW[:, 256 * c + p:256 * c + 256:2], S2, F.Identity, 128, ["S2"],
+                    ["yo%d%d" % (p, c)] + ["L0o0", "L0o1", "L0o2", "L0o3", "L0g"] * (t == 3 and c == 0), [6], bias=512.0 - 196608.0)
             if t < 4 and c < 3:
                 q = 3 * t + c
-                for kind, hc, hb, win, lo_, ne in (("L", hL, T.hbL, T.LW, 8, 8), ("P", hP, T.hbP, T.PW, 0, 4)):
-                    def s_h(hc=hc, hb=hb, win=win, lo_=lo_, ne=ne, q=q, new=new):
-                        g.remote_dma_fused([RemoteDMATransfer(
-                            dst_ids=[did(topo, hc), did(topo, hc)], dma_engine_mask=emask(topo, core, hc, lo_, ne),
-                            remote_sem=T.sem["ha%d" % q], srcs=[win[:, new]],
-                            dsts=[hb[256 * q:256 * q + 128, :], hb[256 * q + 128:256 * q + 256, :]])], local_sem=T.sem.lsm)
-                        lsm[0] += ne
-                    send(s_h, ["%s%do%d" % (kind, t + 2, c)], ["s%s%d" % (kind, q)])
+
+                def s_h(q=q, new=new):
+                    g.remote_dma_fused([RemoteDMATransfer(
+                        dst_ids=[did(topo, hL), did(topo, hL)], dma_engine_mask=emask(topo, core, hL, 8, 8),
+                        remote_sem=T.sem["ha%d" % q], srcs=[T.LW[:, new]],
+                        dsts=[T.hbL[256 * q:256 * q + 128, :], T.hbL[256 * q + 128:256 * q + 256, :]])], local_sem=T.sem.lsm)
+                    lsm[0] += 8
+                send(s_h, ["L%do%d" % (t + 2, c)], ["sL%d" % q])
+            tag[0] = tg + 4
             for h in range(2):
-                tag[0] = tg + 4 + h
                 dk = ["d%d%d0" % (c, h), "d%d%d1" % (c, h)]
                 dv = T.dd[:, do + 1024 * h:do + 1024 * h + 1024]
-                for j in range(2):
-                    dq = T.dd[:, do + 1024 * h + 512 * j:do + 1024 * h + 512 * j + 512]
-                    act(dq, dq, F.Sigmoid, 512, [dk[j]], [dk[j]])
-                u = (8 * t + 2 * c + h) % NT
-                w = 2 * c + h
-                tt(T.tt[:, 1024 * u:1024 * u + 1024],
-                   T.xx[:, c * XW:(c + 1) * XW].indirect(T.um[:, 128 * c + 64 * h:128 * c + 64 * h + 64]), dv, A.mult, 1024,
-                   dk + ["x%d0" % c, "x%d1" % c, "xz" + sc, "um%d%d" % (c, h)], ["tt%d" % u], k=GA)
-                Ep = B[7][:, 64 * w:64 * w + 64]
-                ev = T.EE[:, 256 * c + 128 * h + p:256 * c + 128 * h + 128:2]
-                ek = "E%d%d%d" % (p, c, h)
-                its = [(Ep, T.If[:, :], T.tt[:, 1024 * u + s:1024 * u + 1024:16]) for s in range(16)] + [(Ep, T.If[:, :], ev)] * (t >= 2)
-                mm(its[:8], 8 * 256, ["tt%d" % u, "If"], ["Ep%d" % w, "Eg"], [7], last=False)
-                mm(its[8:], len(its[8:]) * 256, ["tt%d" % u, "If", "Ep%d" % w] + [ek] * (t >= 2), ["Ep%d" % w, "Eg"], [7], first=False)
-                if h == 1:
-                    act(T.EE[:, 256 * c + p:256 * c + 256:2], B[7][:, 128 * c:128 * c + 128], F.Identity, 128,
-                        ["Ep%d" % (w - 1), "Ep%d" % w], [ek, "E%d%d0" % (p, c)], [7])
+                act(dv, dv, F.Sigmoid, 1024, dk, dk)
+            u = (4 * t + c) % NT
+            direct = "%d%d" % (t, c) in DIR
+            for h0, h1 in parts:
+                tag[0] = tg + 4 + h0
+                w = 64 * (h1 - h0)
+                hs = range(h0, h1)
+                tk = [["tt%d%d%d" % (u, q, h) for h in hs] for q in range(NQ)]
+                to, m = 2048 * u + 1024 * h0, G * w
+                for q in range(NQ):
+                    o = 128 * c + 64 * h0 + w // NQ * q
+                    tt(T.tt[:, to + m * q:to + m * q + m], T.xx[:, c * XW:xo + 1024 * h1].indirect(T.um[:, o:o + w // NQ]),
+                       T.dd[:, do + 1024 * h0 + q:do + 1024 * h1:NQ], A.mult, m,
+                       ["d%d%d%d" % (c, h, j) for h in hs for j in range(2)] + ["x%d%d" % (c, h) for h in hs]
+                       + ["x%d0" % c, "xz" + sc] + ["um%d%d" % (c, h) for h in hs] + ["tf%d" % u] * (w == 64), tk[q], k=GA)
+                q = NQ
+                while q > 1 and not direct:
+                    q //= 2
+                    gdma("ad%d" % u, T.tt[:, to:to + m * q], T.tt[:, to + m * q:to + 2 * m * q], sum(tk[:2 * q], []),
+                         sum(tk[:q], []), 2400.0 + m * q)
+                Ep = B[7][:, 128 * c + 64 * h0:128 * c + 64 * h1]
+                ev = T.EE[:, 256 * c + 128 * h0 + p:256 * c + 128 * h1:2]
+                ek = ["E%d%d%d" % (p, c, h) for h in hs]
+                pk = ["Ep%d%d" % (c, h) for h in hs]
+                its = [(Ep, T.If[:, :], ev, ek)] * (t >= 2)
+                for j in range(q):
+                    its += [(Ep, T.If[:, :], T.tt[:, to + m * j + s:to + m * j + m:G], tk[j]) for s in range(G)]
+                cuts = list(range(len(its) % 4, len(its) + 1, 4))
+                cuts[0] = 0
+                for a, z in zip(cuts, cuts[1:]):
+                    mm([x[:3] for x in its[a:z]], 4 * w * (z - a), ["If"] + [k for x in its[a:z] for k in x[3]] + pk * (a > 0),
+                       pk + ["Eg"] + ["tf%d" % u] * (w == 128), [7], first=a == 0, last=z == len(its))
+            act(T.EE[:, 256 * c + p:256 * c + 256:2], B[7][:, 128 * c:128 * c + 128], F.Identity, 128,
+                ["Ep%d0" % c, "Ep%d1" % c], ["E%d%d0" % (p, c), "E%d%d1" % (p, c)], [7])
             if t == 4:
                 dma("S", [(T.ye[:, 256 * c:256 * c + 256], T.EE[:, 256 * c:256 * c + 256])],
                     ["E%d%d%d" % (a, c, h) for a in range(2) for h in range(2)], ["ye" + sc])
         if t < 4:
-            ext("al%d" % t, 72, ["sL%d" % (3 * t + c) for c in range(3)], ["L%dg" % (t + 2)], 7000.0)
-            ext("ap%d" % t, 72, ["sP%d" % (3 * t + c) for c in range(3)], ["P%dg" % (t + 2)], 6000.0)
+            ext("al%d" % t, 9 * ne, ["sL%d" % (3 * t + c) for c in range(3)], ["L%dg" % (t + 2)], 7000.0)
+            ext("ap%d" % t, 9 * ne, ["sP%d" % (3 * t + c) for c in range(3)], ["P%dg" % (t + 2)], 1000.0)
         if t < 3:
             tag[0] = 25 * t + 25
             Cq = B[2][:, 0:32]
             mm([(Cq, T.Wt[:, 15 - j:143 - j], T.cp[:, j:512:16]) for j in range(16)], 16 * 64,
-               ["cp%d" % c for c in range(4)] + ["Wt"], ["D1"], [2])
-            a0, a1, a2 = T.ty[:, 0:32], T.ty[:, 32:64], T.ty[:, 64:96]
-            ts(a0, Cq, 0.0, -float(R), A.is_ge, A.mult, 32, ["D1"], ["ty", "a0"], [2])
-            ts(a1, Cq, 0.0, 1.0 - 2 * p, A.is_ge, A.mult, 32, ["D1"], ["ty", "a1"], [2])
-            tt(a0, Cq, a0, A.add, 32, ["D1", "a0"], ["a0"], [2])
-            ts(a2, a0, float(R), 2.0, A.add, A.mult, 32, ["a0"], ["ty", "a2"])
-            tt(a1, a1, T.slf[:, :], A.subtract, 32, ["a1", "slf"], ["a1"])
-            ts(a0, a0, 511.5 - R, None, A.is_lt, None, 32, ["a0"], ["a0"])
-            tt(a1, a1, a2, A.add, 32, ["a1", "a2"], ["a1"])
-            tt(a2, a1, a0, A.mult, 32, ["a0", "a1"], ["a2"])
-            tt(a2, a2, T.slf[:, :], A.add, 32, ["a2", "slf"], ["a2"])
-            ts(T.ul[:, :], a2, float(p), None, A.add, None, 32, ["a2"], ["ul"])
+               ["cp%d" % c for c in range(4)] + ["Wt"], ["D0"], [2])
+            a0, a1 = T.ty[:, 0:32], T.ty[:, 32:64]
+            ts(a0, Cq, 0.0, 1.0 - 2 * p - 2 * R, A.is_ge, A.mult, 32, ["D0"], ["ty", "a0"], [2])
+            tt(a0, Cq, a0, A.add, 32, ["D0", "a0"], ["a0"], [2])
+            ts(a1, a0, 1023.5 - 2 * R - p, None, A.is_lt, None, 32, ["a0"], ["ty", "a1"])
+            tt(a0, a0, T.slf[:, :], A.subtract, 32, ["a0", "slf"], ["a0"])
+            tt(a0, a0, a1, A.mult, 32, ["a0", "a1"], ["a0"])
+            tt(a0, a0, T.slf[:, :], A.add, 32, ["a0", "slf"], ["a0"])
+            ts(T.ul[:, :], a0, 2.0 * R + p, None, A.add, None, 32, ["a0"], ["ul"])
             mk = "nb%d" % p
-            act(T.go[:, :], T.nbr[:, :].indirect(T.ul[:, :]), F.Identity, 512, ["ul", "nb0", "nb1"], ["go"], k=GA)
-            ts(T.t1[:, :], T.yy[:, :], 0.5, None, A.add, None, 512, ["yy%d" % c for c in range(4)], ["t10", "t11"])
-            ts(T.t2[:, :], T.t1[:, :], 1, None, A.bitwise_and, None, 512, ["t10", "t11"], ["t20", "t21"])
+            tt(T.go[:, :], T.nbs[:, :].indirect(T.ul[:, :]), T.nbr[:, p:1024:2], A.subtract, 512, ["ul", "nbs", mk], ["go"], k=GA)
             for h in range(2):
                 hs = slice(256 * h, 256 * h + 256)
                 e = T.nbr[:, 512 * h + p:512 * h + 512:2]
-                tt(Z, T.go[:, hs], e, A.subtract, 256, ["go", mk], ["Z"], [4], k=2.0)
-                tt(Z, Z, T.t2[:, hs], A.mult, 256, ["Z", "t2%d" % h], ["Z"], [4])
+                yk = ["yy%d" % (2 * h), "yy%d" % (2 * h + 1)]
+                ts(Z, T.yy[:, hs], 1.5 * 2 ** 24, 1.5 * 2 ** 24, A.add, A.subtract, 256, yk, ["Z"], [4])
+                tt(Z, Z, T.yy[:, hs], A.is_lt, 256, ["Z"] + yk, ["Z"], [4])
+                tt(Z, Z, T.go[:, hs], A.mult, 256, ["Z", "go"], ["Z"], [4])
                 tt(e, Z, e, A.add, 256, ["Z", mk], [mk], [4])
             decode(p)
+            if t < 2:
+                dma("S", [(T.nbs[:, :], T.nbr[:, :])], ["nb0", "nb1"], ["nbs"])
     dma("S", [(T.yp[:, :], T.LW[1:128:16, 0:1024])], ["yo%d%d" % (a, c) for a in range(2) for c in range(4)], ["yp"])
     return ops, lsm
 
@@ -544,113 +638,200 @@ def schedule(ops):
         for k in o["w"]:
             lw[k] = i
             rd[k] = []
+    pre = [sorted(d) for d in deps]
     suc = [[] for _ in range(n)]
     for i in range(n):
-        for j in deps[i]:
+        for j in pre[i]:
             suc[j].append(i)
-    bl = [0.0] * n
-    for i in range(n - 1, -1, -1):
-        bl[i] = ops[i]["c"] + ops[i]["lat"] + 150.0 + max([bl[j] for j in suc[i]] + [0.0])
-
-    def place(pred, succ, pri, back):
-        left = [len(d) for d in pred]
-        ready = [i for i in range(n) if left[i] == 0]
-        en, rt = [0.0] * n, [0.0] * n
-        busy = {k: [] for k in keys}
-        key = lambda x: pri[x]
-        edge = gap[back]
-        while ready:
-            i = max(ready, key=key) if len(ready) > 1 else ready[0]
-            ready.remove(i)
-            e, c, s, res = eng[i], cost[i], rt[i], need[i]
-            moved = True
-            while moved:
-                moved = False
-                for k, pad in res:
-                    iv = busy[k]
-                    m = len(iv)
-                    while m > 0 and iv[m - 1][1] + pad > s:
-                        m -= 1
-                    for a, z, w in iv[m:]:
-                        if a >= s + c + pad:
-                            break
-                        if z + pad > s and (pad == 0.0 or w != e):
-                            s = z + pad
-                            moved = len(res) > 1
-            for k, pad in res:
-                iv = busy[k]
-                m = len(iv)
-                while m > 0 and iv[m - 1][0] > s:
-                    m -= 1
-                iv.insert(m, (s, s + c, e))
-            s += c
-            en[i] = s
-            for j, d in edge[i]:
-                left[j] -= 1
-                if s + d > rt[j]:
-                    rt[j] = s + d
-                if left[j] == 0:
-                    ready.append(j)
-        return en
-
-    eng, cost = [o["e"] for o in ops], [o["c"] for o in ops]
-    need = [([(o["e"], 0.0)] if o["e"] != "X" else []) + [(b, XL) for b in o["b"]] for o in ops]
-    keys = set(k for x in need for k, _ in x)
-    gap = ([[(j, ops[i]["lat"] + (SL if eng[i] == eng[j] else XL)) for j in suc[i]] for i in range(n)],
-           [[(j, ops[j]["lat"] + (SL if eng[i] == eng[j] else XL)) for j in sorted(deps[i])] for i in range(n)])
-
-    arr = [i for i in range(n) if ops[i]["e"] == "X"]
-
-    def measure(end):
-        fin, free, bank = [0.0] * n, {}, {}
-        for i in sorted(range(n), key=lambda x: (end[x] - cost[x], end[x], x)):
-            e = eng[i]
-            s = free.get(e, 0.0) if e != "X" else 0.0
-            for j, d in back[i]:
-                if fin[j] + d > s:
-                    s = fin[j] + d
-            for b in ops[i]["b"]:
-                w = bank.get(b)
-                if w is not None and w[0] != e and w[1] > s:
-                    s = w[1]
-            s += slow[i]
-            fin[i] = free[e] = s
-            for b in ops[i]["b"]:
-                bank[b] = (e, s + XL)
-        return max(end[i] + ops[i]["lat"] for i in range(n)) + 0.05 * sum(end[i] for i in arr) + WS * max(fin)
-
-    back = [[(j, ops[j]["lat"] + (SL if eng[i] == eng[j] else XL)) for j in sorted(deps[i])] for i in range(n)]
-    slow = [o["c"] * (2.0 if o["e"] == "P" else 1.0) for o in ops]
-
-    best, pri = None, [bl[i] + 100.0 * OFF[ops[i]["tag"]] for i in range(n)]
-    for _ in range(ITER):
-        end = place(deps, suc, pri, False)
-        span = measure(end)
-        if best is None or span < best[0]:
-            best = (span, end)
-        pri = place(suc, deps, [end[i] + ops[i]["lat"] for i in range(n)], True)
+    eng = ["VAPGSX".index(o["e"]) for o in ops]
+    bks, lat, tag = [o["b"] for o in ops], [o["lat"] for o in ops], [o["tag"] for o in ops]
+    last = [i for i in range(n) if not suc[i]]
     seed = [SEED]
 
     def rnd():
         seed[0] = (seed[0] * 1103515245 + 12345) % 2147483648
         return seed[0] / 2147483648.0
-    cur = best
-    for _ in range(TRIES):
-        a = ops[int(rnd() * n)]
-        dl = (rnd() - 0.5) * (3000.0, 12000.0)[rnd() < 0.5]
-        one = rnd() < 0.5
-        pri = [ops[i]["c"] - cur[1][i] + (dl if ops[i]["tag"] == a["tag"] and (not one or ops[i]["e"] == a["e"]) else 0.0)
-               for i in range(n)]
-        end = place(deps, suc, pri, False)
-        if rnd() < 0.1:
-            end = place(deps, suc, place(suc, deps, [end[i] + ops[i]["lat"] for i in range(n)], True), False)
-        span = measure(end)
-        if span <= cur[0] + HEAT * rnd():
-            cur = (span, end)
-            if span < best[0]:
-                best = cur
-    end = best[1]
-    order = sorted(range(n), key=lambda i: (end[i] - ops[i]["c"], end[i], i))
+
+    def case(ga, pe, wt):
+        return [(eng[i], ops[i]["c"] * (pe if eng[i] == 2 else ga if ops[i]["g"] else 1.0),
+                 [(j, wt * (lat[j] + (SL if eng[i] == eng[j] else XL))) for j in pre[i]], bks[i]) for i in range(n)], wt
+    mean = case(*MEAN)
+    cost, back = [x[1] for x in mean[0]], [x[2] for x in mean[0]]
+    fwd = [[] for _ in range(n)]
+    for i in range(n):
+        for j, d in back[i]:
+            fwd[j].append((i, d))
+
+    def place(pri, rev):
+        pred, succ = (fwd, back) if rev else (back, fwd)
+        left = [len(x) for x in pred]
+        rt = [lat[i] if rev and not left[i] else 0.0 for i in range(n)]
+        ready = sorted(((pri[i], i) for i in range(n) if not left[i]), reverse=True)
+        st, en, ow = [[] for _ in range(14)], [[] for _ in range(14)], [[] for _ in range(14)]
+        fin = [0.0] * n
+        while ready:
+            i = ready.pop()[1]
+            e, c, s = eng[i], cost[i], rt[i]
+            if e < 5:
+                while True:
+                    a, z = st[e], en[e]
+                    m = k = len(a)
+                    while m and z[m - 1] > s:
+                        m -= 1
+                    while m < k and a[m] < s + c:
+                        s = z[m]
+                        m += 1
+                    s0 = s
+                    for b in bks[i]:
+                        a, z, w = st[6 + b], en[6 + b], ow[6 + b]
+                        q = k = len(a)
+                        while q and a[q - 1] > s - 4000.0:
+                            q -= 1
+                        while q < k and a[q] < s + c + XL:
+                            if w[q] != e and z[q] + XL > s:
+                                s = z[q] + XL
+                            q += 1
+                    if s == s0:
+                        break
+                st[e].insert(m, s)
+                en[e].insert(m, s + c)
+                for b in bks[i]:
+                    a = st[6 + b]
+                    q = len(a)
+                    while q and a[q - 1] > s:
+                        q -= 1
+                    a.insert(q, s)
+                    en[6 + b].insert(q, s + c)
+                    ow[6 + b].insert(q, e)
+            s += c
+            fin[i] = s
+            for j, d in succ[i]:
+                if s + d > rt[j]:
+                    rt[j] = s + d
+                left[j] -= 1
+                if not left[j]:
+                    q, x = len(ready), (pri[j], j)
+                    while q and ready[q - 1] < x:
+                        q -= 1
+                    ready.insert(q, x)
+        return fin
+
+    def pack(fin):
+        return place([-x for x in place([-x for x in fin], True)], False)
+
+    def shift(fin, tries, heat):
+        cur = best = (max(fin[i] + lat[i] for i in last), fin)
+        for _ in range(tries):
+            a = int(rnd() * n)
+            dl, one, f = (rnd() - 0.5) * (1500.0, 4000.0, 12000.0)[int(rnd() * 3)], rnd() < 0.5, cur[1]
+            end = place([f[i] - cost[i] + (dl if tag[i] == tag[a] and (not one or eng[i] == eng[a]) else 0.0) for i in range(n)], False)
+            if rnd() < 0.15:
+                end = pack(end)
+            v = max(end[i] + lat[i] for i in last)
+            if v <= cur[0] + heat * rnd():
+                cur = (v, end)
+                if v < best[0]:
+                    best = cur
+        return sorted(range(n), key=lambda i: (best[1][i] - cost[i], best[1][i], i))
+
+    def play(cs, seq, a, fin, why):
+        node, wt = cs
+        free, bank = [-1] * 6, [-1] * 8
+        k, miss, xl = a - 1, 13, XL * wt
+        while k >= 0 and miss:
+            i = seq[k]
+            if eng[i] < 5 and free[eng[i]] < 0:
+                free[eng[i]] = i
+                miss -= 1
+            for b in bks[i]:
+                if bank[b] < 0:
+                    bank[b] = i
+                    miss -= 1
+            k -= 1
+        for i in seq[a:]:
+            e, c, bk, bs = node[i]
+            w = free[e]
+            s = fin[w] if w >= 0 else 0.0
+            for j, d in bk:
+                if fin[j] + d > s:
+                    s, w = fin[j] + d, -2 - j
+            for b in bs:
+                j = bank[b]
+                if j >= 0 and eng[j] != e and fin[j] + xl > s:
+                    s, w = fin[j] + xl, j
+                bank[b] = i
+            fin[i], why[i] = s + c, w
+            if e < 5:
+                free[e] = i
+        return max((fin[i] + wt * lat[i], i) for i in last) + (fin, why)
+
+    def tighten(seq, cases, moves, heat):
+        now = [play(cs, seq, 0, [0.0] * n, [-1] * n) for _, cs in cases]
+        cur = sum(w * x[0] for (w, _), x in zip(cases, now))
+        best, pos, paths = (cur, seq, now[0][2]), [0] * n, None
+        for it in range(moves):
+            if paths is None:
+                for k, i in enumerate(seq):
+                    pos[i] = k
+                paths = {}
+            x, q = rnd(), 0
+            while q < len(cases) - 1 and x > cases[q][0]:
+                x -= cases[q][0]
+                q += 1
+            why = now[q][3]
+            if q not in paths:
+                path, i = [], now[q][1]
+                while i >= 0:
+                    path.append(i)
+                    i = why[i] if why[i] >= -1 else -2 - why[i]
+                path.reverse()
+                paths[q] = (path, [k for k in range(1, len(path)) if why[path[k]] >= 0])
+            path, cand = paths[q]
+            k = cand[int(rnd() * len(cand))]
+            early = rnd() < 0.5
+            if early:
+                m = k - 1
+                while m > 0 and why[path[m]] >= 0 and rnd() < 0.6:
+                    m -= 1
+                u, v = path[m], path[k]
+            else:
+                m = k
+                while m + 1 < len(path) and why[path[m + 1]] >= 0 and rnd() < 0.6:
+                    m += 1
+                u, v = path[k - 1], path[m]
+            a, z = pos[u], pos[v]
+            x, stop, near = (v, u, pre) if early else (u, v, suc)
+            mv, todo = {x}, [x]
+            while todo and stop not in mv:
+                for j in near[todo.pop()]:
+                    if a <= pos[j] <= z and j not in mv:
+                        mv.add(j)
+                        todo.append(j)
+            if stop in mv:
+                continue
+            mid = seq[a:z + 1]
+            new = seq[:a] + [j for j in mid if (j in mv) == early] + [j for j in mid if (j in mv) != early] + seq[z + 1:]
+            room = -heat * max(0.05, 1.0 - it / moves) * math.log(max(rnd(), 1e-9))
+            one = play(cases[q][1], new, a, now[q][2][:], why[:])
+            if one[0] > now[q][0] + room + 30.0 * (len(cases) > 1):
+                continue
+            nxt = [one if j == q else play(cases[j][1], new, a, now[j][2][:], now[j][3][:]) for j in range(len(cases))]
+            v = sum(w * x[0] for (w, _), x in zip(cases, nxt))
+            if v <= cur + room:
+                seq, now, cur, paths = new, nxt, v, None
+                if cur < best[0]:
+                    best = (cur, seq, now[0][2])
+        return best[1:]
+
+    bl = [0.0] * n
+    for i in range(n - 1, -1, -1):
+        bl[i] = cost[i] + max([bl[j] + d for j, d in fwd[i]] + [lat[i]])
+    end = pack(pack(place([-x for x in bl], False)))
+    for tries, heat in SHIFTS:
+        order, end = tighten(shift(end, tries, heat), [(1.0, mean)], MOVES[0], 40.0)
+    cases = [(c[0], case(*c[1:])) for c in CASES]
+    for _ in range(MOVES[2]):
+        order, end = tighten(order, cases, MOVES[1], 30.0)
     bank = {}
     for i in order:
         for b in ops[i]["b"]:
@@ -665,11 +846,8 @@ def rank_program(g, core, T, topo):
     r = T.rank_of(core)
     if r is None:
         for q, c in enumerate(T.cores):
-            hP, hL = helpers(c, T, topo)
-            if core == hP:
-                helper_program(g, core, T, topo, q, "P")
-            if core == hL:
-                helper_program(g, core, T, topo, q, "L")
+            if core == helper(c, T, topo):
+                helper_program(g, core, T, topo, q)
         return
     ops, lsm = build(g, core, T, topo, r)
     if "s" not in CACHE:

import math
from concourse.bass import DstId, RemoteDMATransfer
from concourse.mybir import AluOpType as A, ActivationFunctionType as F

R = 1664
XW = 2056
NQ = 2
G = 16 // NQ
TWO = [0, 2]
NT = 3
LN2 = math.log(2.0)
f32, bf, f16, i32, u16 = "float32", "bfloat16", "float16", "int32", "uint16"


def sb(n, t):
    return ("sbuf", [128, n], t)


SCRATCH = {
    "LW": sb(6 * R, f32), "PW": sb(6 * R, bf), "xx": sb(4 * XW, f32), "dd": sb(8192, f32),
    "sg": sb(4096, bf), "pg": sb(4096, bf), "tt": sb(NT * 2048, f32), "mm": sb(6144 - 2048 * len(TWO), f32),
    "uu": sb(512, f32), "nbr": sb(1024, i32), "nbs": sb(1024, i32), "EE": sb(1024, f32),
    "fad": sb(1024, bf), "lb": sb(768, bf),
    "ua": sb(1024, u16), "us": sb(512, u16), "um": sb(512, u16),
    "t1": sb(256, i32), "t2": sb(256, i32), "Ti": sb(256, i32),
    "ac": sb(512, f16), "Sd": sb(2048, bf), "p2": sb(512, bf), "fs": sb(256, bf), "yy": sb(512, f32),
    "la": sb(256, f16), "Sh": sb(128, bf), "hq": sb(256, bf), "cp": sb(512, f16), "go": sb(512, f32),
    "msk": sb(512, bf), "jc": sb(128, f16), "ul": sb(32, u16), "ty": sb(136, f32),
    "pc": sb(64, i32), "rc": sb(64, i32), "ps": sb(48, i32), "u1": sb(64, i32), "u2": sb(64, i32), "u3": sb(64, i32),
    "vh": sb(256, bf), "vl": sb(256, bf), "vs": sb(48, f32), "cs": sb(96, bf), "pl": sb(288, bf),
    "ci": sb(8, i32), "cj": sb(144, i32), "ct": sb(48, f32), "cb": sb(8, bf), "BL": sb(144, f32),
    "slf": sb(32, f32),
    "Wc": sb(144, bf), "W1": sb(272, f32), "Pm": sb(144 * NQ, bf),
    "Wp": sb(144, bf), "Wt": sb(144, f16), "NG": sb(128, bf), "Df": sb(1024, f16), "Rk": sb(1024, bf),
    "FW": sb(256, bf), "Ib": sb(128, bf), "Ih": sb(128, f16), "If": sb(128, f32), "SA": sb(144, f16),
    "SB": sb(720, bf), "Ps": sb(384, bf), "Hs": sb(128, bf), "mh": sb(4096, f16), "hl": sb(512 * len(TWO), i32), "Wh": sb(544, f16),
    "hbL": ("dram", [12 * 256, 128], f32),
}
SCRATCH["MM"] = ("psum", [128, 1024], f32)
for _i in range(2, 8):
    SCRATCH["B%d" % _i] = ("psum", [128, 512], f32)

SEMAPHORES = (["cV", "cA", "cP", "cG", "lsm", "ip", "il0", "il1"] + ["ha%d" % i for i in range(13)]
              + ["ap%d" % i for i in range(4)] + ["al%d" % i for i in range(4)] + ["d%d" % i for i in range(24)]
              + ["ad%d" % i for i in range(NT)] + ["lp0", "lp1", "lp2"])

CY, PCY, GA, OV = 0.83, 0.42, 1.56, 20.0
SL, XL, GD = 100.0, 250.0, 1300.0
MEAN = (1.05, 1.1, 1.1)
CASES = ((0.45, 1.0, 1.0, 1.15), (0.3, 1.3, 1.0, 0.85), (0.25, 0.75, 1.3, 1.4))
SEED, SHIFTS, MOVES = 5, ((2200, 100.0), (800, 50.0), (800, 50.0)), (6000, 2500, 11)
ONV = ["001", "011"]
NV = [[0, 15, 0, 0], [0] * 4, [0] * 4, [0] * 4, [0, 4, 0, 4]]
SGN = [3, 3, 3, 3, 3]
DIR = ["43"]
HALF = [0]
CACHE = {}


def helper(core, T, topo):
    ok = [c for c in topo.cores_of(core) if T.rank_of(c) is None
          and all(topo.may_write(c, o) for o in T.cores if o != core)]
    return ([c for c in ok if topo.die(c) != topo.die(core)] or ok)[0]


def emask(topo, src, dst, lo, n):
    return sum(1 << e for e in topo.engines(src, dst)[lo:lo + n])


def did(topo, c):
    a = topo.addr(c)
    return DstId(rid=a[0], pnc=a[1])


def fan(g, T, topo, me, r, src, dst_of, sem, loc):
    n = len(T.cores)
    to = [T.cores[(r + d) % n] for d in range(1, n)]
    m = topo.mask(me, to[0])
    for c in to:
        m &= topo.mask(me, c)
    g.remote_dma_fused([RemoteDMATransfer(dst_ids=[did(topo, c) for c in to], dma_engine_mask=m, remote_sem=sem,
                                          srcs=[src], dsts=[dst_of(d) for d in range(1, n)])], local_sem=loc)
    return bin(m).count("1")


def gcol(reg, d, c):
    return reg * R + 512 + (d - 1) * 384 + 128 * c


def helper_program(g, core, T, topo, r):
    g.wait_ge(T.sem.ha12, 8)
    tot = fan(g, T, topo, core, r, T.lb[:, 384:768],
              lambda d: T.sg[:, 1152 + (d - 1) * 384:1152 + d * 384], T.sem.il1, T.sem.lsm)
    for t in range(4):
        for c in range(3):
            q = 3 * t + c
            g.wait_ge(T.sem["ha%d" % q], 16)
            tot += fan(g, T, topo, core, r, T.hbL[256 * q + 16:256 * q + 144, :],
                       lambda d: T.LW[:, gcol(t + 2, d, c):gcol(t + 2, d, c) + 128], T.sem["al%d" % t], T.sem.lsm)
    g.wait_ge(T.sem.lsm, tot)


def build(g, core, T, topo, r):
    V, S, P, Y = g.vector, g.scalar, g.tensor, g.sync
    ops = []
    nd = [0]
    lsm = [0]
    tag = [0]
    hL = helper(core, T, topo)
    ne = min(len(topo.engines(core, c)) for c in T.cores if c != core)

    def op(e, fn, cost, rd, wr, bk=(), tok=None, lat=0.0, k=1.0):
        ops.append(dict(e=e, fn=fn, c=cost, r=list(rd), w=list(wr), b=list(bk), tok=tok, lat=lat, tag=tag[0], g=k == GA))

    def vc(n, k=1.0):
        return OV + CY * max(64.0, n * k)

    def ts(o, i, s1, s2, o0, o1, n, rd, wr, bk=(), k=1.0):
        if o1 is None:
            op("V", lambda: V.tensor_scalar(o, i, s1, None, o0), vc(n, k), rd, wr, bk)
        else:
            op("V", lambda: V.tensor_scalar(o, i, s1, s2, o0, o1), vc(n, k), rd, wr, bk)

    def tt(o, a, b, o0, n, rd, wr, bk=(), k=None):
        op("V", lambda: V.tensor_tensor(o, a, b, o0), vc(n, k or (1.0 if bk else 2.0)), rd, wr, bk, k=k)

    def cp(o, i, n, rd, wr, bk=(), k=1.0):
        op("V", lambda: V.tensor_copy(o, i), vc(n, k), rd, wr, bk, k=k)

    def act(o, i, f, n, rd, wr, bk=(), bias=0.0, scale=1.0, k=1.0):
        op("A", lambda: S.activation(o, i, f, bias=bias, scale=scale), vc(n, k), rd, wr, bk, k=k)

    def mm(items, cost, rd, wr, bk, first=True, last=True):
        def fn():
            for j, (o, l, x) in enumerate(items):
                ins = P.matmul(o, l, x, first and j == 0, last and j == len(items) - 1)
            return ins
        op("P", fn, OV + PCY * cost, rd, wr, bk)

    def dma(e, pairs, rd, wr, lat=2200.0):
        sem = "d%d" % nd[0]
        nd[0] += 1
        q = {"S": Y, "A": S, "G": g}[e]

        def fn():
            for o, i in pairs:
                q.dma_start(o, i).then_inc(T.sem[sem], 16)
        op(e, fn, (1000.0 if e == "G" else 100.0) * len(pairs), rd, wr, tok=(sem, 16 * len(pairs)), lat=lat)

    used = {}

    def gdma(sem, o, i, rd, wr, lat):
        used[sem] = used.get(sem, 0) + 16
        op("G", lambda: g.dma_start(o, i, accum_op=A.add).then_inc(T.sem[sem], 16), GD, rd, wr, tok=(sem, used[sem]), lat=lat)

    def aff(e, o, i, scale, bias, n, rd, wr, bk=()):
        if e == "V":
            ts(o, i, scale, bias, A.mult, A.add, n, rd, wr, bk)
        else:
            act(o, i, F.Identity, n, rd, wr, bk, bias=bias, scale=scale)

    def iota(o, pat, base, cm, n, wr, fl=False):
        if fl:
            op("G", lambda: g.iota(o, pat, base, cm, allow_small_or_imprecise_dtypes=True), 130 + 2 * CY * n, [], wr)
        else:
            op("G", lambda: g.iota(o, pat, base, cm), 130 + 2 * CY * n, [], wr)

    def send(fn, rd, wr):
        op("G", fn, 600.0, rd, wr, tok="none")

    def ext(sem, cnt, rd, wr, lat):
        op("X", None, 0.0, rd, wr, tok=(sem, cnt), lat=lat)

    B = [T.MM, T.MM] + [T["B%d" % i] for i in range(2, 8)]
    ct = T.ct

    dma("S", [(T.ps[0:112, :], T.ph0[1:8, 0:768]), (T.ps[112:128, :], T.ph0[0:1, 0:768])], [], ["ps"])
    dma("A", [(T.nbr[:, :], T.nb[:, :])], [], ["nb0", "nb1"])
    dma("S", [(T.pc[:, :], T.ph0[:, :]), (T.rc[:, :], T.rb[:, :])], [], ["pc"])
    dma("A", [(T.sg[0:112, 2304:3072], T.loud[16:128, 0:768]), (T.sg[112:128, 2304:3072], T.loud[0:16, 0:768])], [], ["los"])
    dma("S", [(T.sg[:, 3072:4096], T.loud[:, :]), (T.fad[:, :], T.fade[:, :])], [], ["lou", "fad"])
    dma("S", [(T.nbs[:, :], T.nb[:, :])], [], ["nbs"])
    op("V", lambda: V.memset(T.PW[:, 0:832], 0.0), vc(832, 0.5), [], ["Pz0"])
    dma("S", [(T.PW[:, 832 * j:832 * j + 832], T.PW[:, 0:832]) for j in range(1, 4)], ["Pz0"], ["Pz"])

    for p in range(2):
        ts(T.vs[:, 24 * p:24 * p + 24], T.ps[:, p:48:2], -512.0, None, A.add, None, 24, ["ps"], ["vs%d" % p])
    cp(T.cs[:, 0:48], T.vs[:, :], 48, ["vs0", "vs1"], ["cs0"])
    tt(T.cs[:, 48:96], T.vs[:, :], T.cs[:, 0:48], A.subtract, 48, ["vs0", "vs1", "cs0"], ["cs1"])

    def s_ip():
        lsm[0] += fan(g, T, topo, core, r, T.cs[:, :], lambda d: T.pl[:, 96 * (d - 1):96 * d], T.sem.ip, T.sem.lsm)
    send(s_ip, ["cs0", "cs1"], ["s_ip"])
    ext("ip", 3 * ne, ["s_ip"], ["pl"], 4000.0)
    for p in range(2):
        prs = []
        for d in range(1, 4):
            for h in range(2):
                o = 96 * (d - 1) + 48 * h + 24 * p
                prs.append((T.PW[h:128:16, gcol(p, d, 0):gcol(p, d, 0) + 384], T.pl[:, o:o + 24]))
        dma("SA"[p], prs, ["pl", "Pz"], ["P%dg" % p])
    for p in range(2):
        act(T.lb[:, 384 * p:384 * p + 384], T.sg[:, 2304 + p:3072:2], F.Identity, 384, ["los"], ["lb%d" % p])

    def s_l1():
        a = topo.addr(hL)
        g.remote_dma(T.lb[:, 384:768], T.lb[:, 384:768], T.sem.ha12, T.sem.lsm, a[1], a[0], emask(topo, core, hL, 8, 8))
        lsm[0] += 8

    def s_l0():
        lsm[0] += fan(g, T, topo, core, r, T.lb[:, 0:384], lambda d: T.sg[:, (d - 1) * 384:d * 384], T.sem.il0, T.sem.lsm)
    send(s_l1, ["lb1", "s_ip"], ["s_l1"])
    send(s_l0, ["lb0", "s_l1"], ["s_l0"])
    ext("il0", 3 * ne, ["s_l0"], ["ll0"], 6000.0)
    ext("il1", 3 * ne, ["s_l1"], ["ll1"], 8000.0)
    for p in range(2):
        dma("G", [(T.LW[:, p * R + 512:(p + 1) * R], T.sg[:, 1152 * p:1152 * p + 1152])], ["ll%d" % p, "s_l0"],
            ["L%dg" % p], lat=3000.0)
        act(T.LW[:, p * R:p * R + 512], T.sg[:, 3072 + p:4096:2], F.Identity, 512, ["lou"], ["L%do%d" % (p, c) for c in range(4)])

    def de(q, a, b, o0, rd, wr):
        for p in range(2):
            o = T.uu[:, 64 * q + 32 * p:64 * q + 32 * p + 32]
            if b is None:
                aff("A", o, a[:, p:64:2], 1.0, -512.0, 32, rd, [wr + str(p)])
            else:
                tt(o, a[:, p:64:2], b[:, p:64:2], o0, 32, rd, [wr + str(p)])
    de(0, T.pc, None, None, ["pc"], "va0")
    act(T.vh[:, 0:64], T.uu[:, 0:64], F.Identity, 64, ["va00", "va01"], ["vh0"])
    tt(T.vl[:, 0:64], T.uu[:, 0:64], T.vh[:, 0:64], A.subtract, 64, ["va00", "va01", "vh0"], ["vl0"])
    for p in range(2):
        dma("SA"[p], [(T.PW[h:128:16, p * R:p * R + 512], (T.vh, T.vl)[h][:, 32 * p:32 * p + 32]) for h in range(2)],
            ["vh0", "vl0", "Pz"], ["P%do%d" % (p, c) for c in range(4)])
    aff("A", T.u3[:, :], T.rc[:, :], 1.0, 512.0, 64, ["pc"], ["u3"])
    tt(T.u1[:, :], T.u3[:, :], T.pc[:, :], A.add, 64, ["u3", "pc"], ["u1"])
    ts(T.u1[:, :], T.u1[:, :], 1023, None, A.bitwise_and, None, 64, ["u1"], ["u1"])
    tt(T.u2[:, :], T.u3[:, :], T.u1[:, :], A.add, 64, ["u3", "u1"], ["u2"])
    ts(T.u2[:, :], T.u2[:, :], 1023, None, A.bitwise_and, None, 64, ["u2"], ["u2"])
    de(1, T.u1, T.pc, A.subtract, ["u1", "pc"], "va1")
    de(2, T.u2, T.u1, A.subtract, ["u1", "u2"], "va2")
    de(3, T.rc, None, None, ["pc"], "va3")
    vk = ["va%d%d" % (q, p) for q in range(1, 4) for p in range(2)]
    act(T.vh[:, 64:256], T.uu[:, 64:256], F.Identity, 192, vk, ["vh1"])
    tt(T.vl[:, 64:256], T.uu[:, 64:256], T.vh[:, 64:256], A.subtract, 192, vk + ["vh1"], ["vl1"])
    for p in range(2):
        dma("S", [(T.PW[2 * q + h:128:16, p * R:p * R + 512], (T.vh, T.vl)[h][:, 64 * q + 32 * p:64 * q + 32 * p + 32])
                  for q in range(1, 4 - p) for h in range(2)], ["vh1", "vl1", "Pz"], ["P%dd" % p])

    iota(T.ci[:, 0:1], [[1, 1]], 0, 1, 1, ["ci0"])
    iota(T.cj[:, :], [[1, 144]], 0, -1, 144, ["cj"])
    Am, Qw = T.EE[:, 256:384], T.EE[:, 384:528]
    iota(T.EE[:, 0:256], [[0, 2], [1, 8], [0, 16]], 0, 0, 256, ["tm0"], True)
    iota(T.msk[:, :], [[0, 32], [1, 16]], 0, 0, 512, ["msk"], True)
    iota(T.ty[:, 0:128], [[1, NQ], [16 * NQ, 128 // NQ]], 8 - 1024, 0, 128, ["ty"], True)
    ts(T.msk[:, :], T.msk[:, :], 1.0, None, A.min, None, 512, ["msk"], ["msk"], k=0.5)
    ts(T.ci[:, 1:2], T.ci[:, 0:1], 15, None, A.bitwise_and, None, 1, ["ci0"], ["ci1"])
    ts(T.ci[:, 2:3], T.ci[:, 0:1], 4, None, A.arith_shift_right, None, 1, ["ci0"], ["ci2"])
    cp(ct[:, 0:2], T.ci[:, 1:3], 2, ["ci1", "ci2"], ["k"])
    kc = ct[:, 0:1]
    ts(Qw, T.cj[:, :], kc, None, A.add, None, 144, ["cj", "k"], ["Qw"])
    ts(T.BL[:, :], T.EE[:, 0:144], ct[:, 1:2], None, A.is_equal, None, 144, ["tm0", "k"], ["BL"])
    BL = T.BL[:, 0:128]
    ts(ct[:, 2:3], kc, 1.5, 4096.0, A.is_lt, A.mult, 1, ["k"], ["c2"])
    ts(T.Wp[:, :], Qw, 15.0, ct[:, 2:3], A.is_equal, A.mult, 144, ["Qw", "c2"], ["Wp"])
    ts(ct[:, 7:8], kc, 1.5, -4096.0, A.is_lt, A.mult, 1, ["k"], ["c7"])
    act(T.NG[:, :], BL, F.Identity, 128, ["BL", "c7"], ["NG"], scale=ct[:, 7:8])
    ts(T.Ti[:, 0:128], T.cj[:, 0:128], 15, None, A.bitwise_and, None, 128, ["cj"], ["Ti00", "Ti01"])
    ts(B[1][:, 512:640], BL, 1.0, 100.0, A.subtract, A.mult, 128, ["BL"], ["M1"], [1])
    tt(Am, T.Ti[:, 0:128], B[1][:, 512:640], A.add, 128, ["Ti00", "Ti01", "M1"], ["Am"], [1])
    Ip = B[0][:, 0:128]
    ts(Ip, Am, 0.0, None, A.is_equal, None, 128, ["Am"], ["M0"], [0])
    act(T.If[:, :], Ip, F.Identity, 128, ["M0"], ["If"], [0])
    act(T.Ih[:, :], T.If[:, :], F.Identity, 128, ["If"], ["Ih"])
    iota(T.ty[:, 128:136], [[1, 8]], 1, 0, 8, ["I8"], True)
    ts(ct[:, 9:17], T.ty[:, 128:136], kc, 15.5, A.add, A.is_ge, 8, ["k", "I8"], ["bs"])
    ts(ct[:, 9:17], ct[:, 9:17], -4096.0, 2048.0, A.mult, A.add, 8, ["bs"], ["bs"])
    act(T.Ib[:, :], Ip, F.Identity, 128, ["M0"], ["Ib"], [0])
    for d in range(1, 9):
        o, x = T.Rk[:, 128 * (d - 1):128 * d], T.Sd[:, 128 * (d - 1):128 * d]
        k = "Sd0%d" % ((d - 1) // 4)
        ts(x, Am, float(d), None, A.is_equal, None, 128, ["Am"], [k, "x%d" % d])
        tt(x, Ip, x, A.subtract, 128, ["M0", "x%d" % d], ["x%d" % d], [0])
        if d == 8:
            act(o, T.Ib[:, :], F.Identity, 128, ["Ib", "bs"], ["Rq8"], scale=ct[:, 16:17])
            o = x
        act(o, x, F.Identity, 128, ["x%d" % d, "bs"], ["Rk%d" % d, k], scale=ct[:, 8 + d:9 + d])
        h, j = divmod(d - 1, 4)
        mm([(B[2 + h][:, 128 * j:128 * j + 128], o, T.Ib[:, :])], 128, ["Rk%d" % d, "Ib", k], ["D%d" % h], [2 + h])
    for h in range(2):
        aff("A", T.Df[:, 512 * h:512 * h + 512], B[2 + h][:, :], 2.0 ** -11, 0.0, 512, ["D%d" % h], ["Df%d" % h], [2 + h])
    ts(T.Wc[:, :], Qw, 15.0, None, A.is_equal, None, 144, ["Qw"], ["Wc"])
    ts(T.W1[:, 0:144], Qw, 14.0, None, A.is_equal, None, 144, ["Qw"], ["W1"])
    tt(T.W1[:, 0:144], T.Wc[:, :], T.W1[:, 0:144], A.subtract, 144, ["Wc", "W1"], ["W1"])
    ts(T.W1[:, 144:272], T.EE[:, 384:512], 0.0, None, A.is_equal, None, 128, ["Qw"], ["Z1"])
    for j in range(2):
        aff("A", T.Wh[:, 272 * j:272 * j + 272], T.W1[:, :], 64.0 ** -j, 0.0, 272, ["W1", "Z1"], ["Wh%d" % j])
    ts(Qw, Qw, float(NQ), kc, A.mult, A.subtract, 144, ["Qw", "k"], ["Qw"])
    for q in range(NQ):
        ts(T.Pm[:, 144 * q:144 * q + 144], Qw, float(NQ * (16 - G) - q), 4096.0, A.is_equal, A.mult, 144, ["Qw"], ["Pm%d" % q])
    aff("A", T.fad[:, :], T.fad[:, :], 0.125, 0.0, 1024, ["fad"], ["fad"])
    ts(ct[:, 3:4], kc, 0.0, None, A.is_equal, None, 1, ["k"], ["c3"])
    aff("A", T.Wt[:, :], T.Wc[:, :], ct[:, 3:4], 0.0, 144, ["Wc", "c3"], ["Wt"])
    ts(ct[:, 4:5], kc, -15.0, 4096.0, A.add, A.mult, 1, ["k"], ["c4"])
    ts(ct[:, 5:6], ct[:, 3:4], 16 * 30720.0, None, A.mult, None, 1, ["c3"], ["c5"])
    tt(ct[:, 4:5], ct[:, 4:5], ct[:, 5:6], A.add, 1, ["c4", "c5"], ["c4"])
    aff("A", ct[:, 5:6], ct[:, 4:5], 2.0, -2.0 * R, 1, ["c4"], ["c5"])
    aff("A", ct[:, 27:28], ct[:, 4:5], 65.0 / 64, 0.0, 1, ["c4"], ["c4h"])
    aff("A", ct[:, 28:29], ct[:, 27:28], 2.0, -2.0 * R, 1, ["c4h"], ["c5h"])
    ts(ct[:, 6:7], ct[:, 3:4], 16.0, kc, A.mult, A.add, 1, ["c3", "k"], ["c6"])
    act(T.cb[:, 0:1], ct[:, 6:7], F.Sigmoid, 1600, ["c6"], ["cb"], bias=-40.0 * LN2, scale=LN2)
    aff("A", ct[:, 30:31], T.cb[:, 0:1], 2.0 ** 59, 0.0, 1, ["cb"], ["c30"])
    aff("A", ct[:, 31:32], ct[:, 3:4], 2.0 ** 19, 0.0, 1, ["c3"], ["c31"])
    for j in range(2):
        aff("A", T.FW[:, 128 * j:128 * j + 128], BL, ct[:, 30 + j:31 + j], 0.0, 128, ["BL", "c3%d" % j], ["FW%d" % j])
    aff("A", ct[:, 26:27], kc, float(NQ), 0.0, 1, ["k"], ["k2"])
    aff("A", T.jc[:, :], T.ty[:, 0:128], 1.0, ct[:, 26:27], 128, ["ty", "k2"], ["jc"])
    aff("A", T.slf[:, :], T.jc[:, 0:32], 2.0 / NQ, 2032.0 / NQ - 2 * R, 32, ["jc"], ["slf"])
    act(T.SA[:, :], T.BL[:, :], F.Identity, 144, ["BL"], ["SA"])
    ts(T.cj[:, 0:128], T.cj[:, 0:128], 127, None, A.bitwise_and, None, 128, ["cj"], ["cj"])
    ts(T.Sh[:, :], T.cj[:, 0:128], 16.0, None, A.is_equal, None, 128, ["cj"], ["Sh"])
    ts(ct[:, 20:21], kc, 1.5, None, A.is_lt, None, 1, ["k"], ["r0"])
    ts(ct[:, 21:22], kc, 3.5, None, A.is_lt, None, 1, ["k"], ["r1"])
    ts(ct[:, 22:23], kc, 5.5, ct[:, 21:22], A.is_lt, A.subtract, 1, ["k", "r1"], ["r2"])
    ts(ct[:, 25:26], kc, 5.5, None, A.is_lt, None, 1, ["k"], ["r5"])
    ts(ct[:, 23:24], kc, 7.5, ct[:, 25:26], A.is_lt, A.subtract, 1, ["k", "r5"], ["r3"])
    ts(ct[:, 24:25], kc, 1.0, None, A.is_equal, None, 1, ["k"], ["r4"])
    for j in range(5):
        act(T.SB[:, 144 * j:144 * j + 144], T.BL[:, :], F.Identity, 144, ["BL", "r%d" % j], ["SB%d" % j],
            scale=ct[:, 20 + j:21 + j])
    for c in range(4):
        iota(T.xx[:, c * XW:c * XW + 8], [[0, 8]], 0, 0, 8, ["xz%d" % c], True)

    Z = B[4][:, 256:512]

    def decode(p):
        for h in range(2):
            e = T.nbr[:, 512 * h + p:512 * h + 512:2]
            ps_ = slice(512 * p + 256 * h, 512 * p + 256 * h + 256)
            ek, k = "nb%d" % p, "%d%d" % (p, h)
            ts(T.t1[:, :], e, 1, 2047, A.arith_shift_right, A.bitwise_and, 256, [ek], ["t1"])
            ts(T.t2[:, :], e, 1, None, A.bitwise_and, None, 256, [ek], ["t2"])
            aff("A", Z, T.t2[:, :], float(R - 2 * R * p), float(R * p), 256, ["t2"], ["Z"], [4])
            tt(T.ua[:, ps_], Z, T.t1[:, :], A.add, 256, ["Z", "t1"], ["ua" + k], [4])
            if 2 * h not in TWO:
                continue
            o = 256 * (len(TWO) * p + h)
            x = T.hl[:, o + 128:o + 256]
            aff("A", x, T.ua[:, ps_.start:ps_.start + 128], 64.0, 0.0, 128, ["ua" + k], ["lo" + k])
            ts(T.hl[:, o:o + 128], x, 6, 0xFC0, A.arith_shift_right, A.bitwise_and, 128, ["lo" + k], ["hi" + k])
            ts(x, x, 0xFC0, None, A.bitwise_and, None, 128, ["lo" + k], ["lo" + k])

    decode(0)
    decode(1)

    for t in range(5):
        p = t & 1
        Lk = ["L%d%s" % (q, s) for q in (t, t + 1) for s in ("o0", "o1", "o2", "o3", "g")]
        Pk = ["P%d%s" % (q, s) for q in (t, t + 1) for s in ("o0", "o1", "o2", "o3", "g")] + ["P0d", "P1d"] * (t < 2)
        Pk = [k for k in Pk if not (t == 1 and k == "P0d")]
        Lwin, Pwin = T.LW[:, t * R:(t + 2) * R], T.PW[:, t * R:(t + 2) * R]
        for c in range(4):
            b = c & 1
            cs = slice(128 * c, 128 * c + 128)
            pcs = slice(512 * p + 128 * c, 512 * p + 128 * c + 128)
            bs = slice(128 * b, 128 * b + 128)
            own = slice(t * R + 128 * c, t * R + 128 * c + 128)
            new = slice((t + 2) * R + 128 * c, (t + 2) * R + 128 * c + 128)
            sb_ = str(b)
            sc = str(c)
            hk = "%d%d" % (p, c // 2)
            tg = 1 + 25 * t + 6 * c
            tag[0] = tg
            for h in range(2):
                o = 512 * p + 128 * c + 64 * h
                po, pi = T.pg[:, 2048 * b + 1024 * h:2048 * b + 1024 * h + 1024], Pwin.indirect(T.ua[:, o:o + 64])
                if "%d%d%d" % (t, c, h) in ONV:
                    cp(po, pi, 1024, Pk + ["ua" + hk], ["pg%d%d" % (b, h)], k=GA)
                else:
                    act(po, pi, F.Identity, 1024, Pk + ["ua" + hk], ["pg%d%d" % (b, h)], k=GA)
            tag[0] = tg + 1
            for h0, h1 in ([(0, 1), (1, 2)] if c in HALF else [(0, 2)]):
                w = 64 * (h1 - h0)
                ky = lambda a: [a + str(h) for h in range(h0, h1)]
                sl = lambda o: slice(o + 64 * h0, o + 64 * h1)
                Tp = B[6][:, sl(384)]
                mm([(Tp, T.Wp[:, 15 - k:143 - k], T.pg[:, 2048 * b + 1024 * h0 + k:2048 * b + 1024 * h1:16]) for k in range(16)]
                   + [(Tp, T.NG[:, :], T.PW[:, sl(own.start)])], 17 * w, ky("pg" + sb_) + ["Wp", "NG", "P%do%d" % (t, c)], ky("T"), [6])
                tt(T.Ti[:, sl(128 * b)], Tp, T.nbr[:, 256 * c + 128 * h0 + p:256 * c + 128 * h1:2], A.add, w, ky("T") + ["nb%d" % p],
                   ky("Ti" + sb_), [6])
                ts(T.Ti[:, sl(128 * b)], T.Ti[:, sl(128 * b)], 12, 1023, A.arith_shift_right, A.bitwise_and, w, ky("Ti" + sb_), ky("Ti" + sb_))
                aff("V" if c in HALF else "A", T.ac[:, sl(128 * c)], T.Ti[:, sl(128 * b)], 1.0, -512.0, w, ky("Ti" + sb_), ky("ac" + sc))
                for h in range(h0, h1):
                    def dfn(h=h, x=T.ac[:, 128 * c + 64 * h:128 * c + 64 * h + 64]):
                        for j in range(8):
                            ins = P.matmul(B[2 + h][:, 64 * j:64 * j + 64], T.Df[:, 128 * j:128 * j + 128], x, True, True)
                        return ins
                    op("P", dfn, OV + PCY * 512, ["ac%d%d" % (c, h), "Df0", "Df1"], ["D%d" % h], [2 + h])
                    o = 1024 * b + 512 * h
                    act(T.Sd[:, o:o + 512], B[2 + h][:, :], F.Sign, 512, ["D%d" % h], ["Sd%d%d" % (b, h)], [2 + h], bias=-0.5)
                    mm([(B[5][:, 64 * h:64 * h + 64], T.Rk[:, 128 * j:128 * j + 128], T.Sd[:, o + 64 * j:o + 64 * j + 64]) for j in range(8)],
                       512, ["Sd%d%d" % (b, h), "Rq8"] + ["Rk%d" % d for d in range(1, 9)], ["R%d" % h], [5])
                Rp = B[5][:, sl(0)]
                two = c in TWO
                mk = lambda s: ky("m%d_%d_" % (2 if two else b, s))
                Op = B[4][:, sl(128 * b)]
                wt = lambda W, a, s: W[:, a + 15 - s:a + 143 - s] if s else W[:, a + 144:a + 272]
                if two:
                    mo = 128 * h0
                    for j in range(2):
                        tt(T.mh[:, mo + w * j:mo + w * j + w], Rp, T.hl[:, sl(256 * (len(TWO) * p + c // 2) + 128 * j)], A.add, w,
                           ky("R") + [("hi", "lo")[j] + hk], mk((0, 16)[j]), [5])
                    for s in range(1, 16):
                        ts(T.mh[:, mo + 256 * s:mo + 256 * s + 2 * w], T.mh[:, mo:mo + 2 * w], 30720.0 - 4096.0 * s, 0.0, A.add, A.max,
                           2 * w, mk(0) + mk(16), mk(s), k=0.5)
                    its = [(Op, wt(T.Wh, 272 * j, s), T.mh[:, mo + 256 * s + w * j:mo + 256 * s + w * j + w])
                           for s in range(16) for j in range(2)]
                    nq, cy = 2, 16 * w
                else:
                    mo = 2048 * (1 - b)
                    key = T.mm[:, sl(mo)]
                    tt(key, Rp, T.ua[:, sl(pcs.start)], A.add, w, ky("R") + ["ua" + hk], mk(0), [5])
                    onv = [s for s in range(1, 16) if (s * NV[t][c]) // 15 > ((s - 1) * NV[t][c]) // 15]
                    for s in range(1, 16):
                        o, th = T.mm[:, sl(mo + 128 * s)], 30720.0 - 4096.0 * s
                        if s in onv:
                            ts(o, key, th, 0.0, A.add, A.max, w, mk(0), mk(s))
                        else:
                            act(o, key, F.Relu, w, mk(0), mk(s), bias=th)
                    its = [(Op, wt(T.W1, 0, s), T.mm[:, sl(mo + 128 * s)]) for s in range(16)]
                    nq, cy = 4, 16 * w
                act(T.p2[:, sl(128 * c)], Rp, F.Sigmoid, w, ky("R"), ky("p2" + sc), [5], bias=-27.5 * LN2, scale=-LN2 / 4096)
                for q in range(nq):
                    m = len(its) // nq
                    mm(its[m * q:m * q + m], cy, ["Z1", "W1", "Wh0", "Wh1"] + ky("O" + sb_) * (q > 0) + mk(16) * two
                       + [k for s in range(16 // nq * q, 16 // nq * (q + 1)) for k in mk(s)], ky("O" + sb_) + ["G4"], [4],
                       first=q == 0, last=q == nq - 1)
                aff("A", T.us[:, sl(128 * c)], Op, 1.0, ct[:, 27:28] if two else ct[:, 4:5], w, ky("O" + sb_) + ["c4", "c4h"],
                    ky("us" + sc), [4])
            if t < 3:
                aff("A", T.cp[:, cs], B[4][:, bs], 2.0, ct[:, 28:29] if two else ct[:, 5:6], 128, ["O%d0" % b, "O%d1" % b, "c5", "c5h"],
                    ["cp" + sc], [4])
            tag[0] = tg + 2
            xo = c * XW + 8
            do = 2048 * c
            for h in range(2):
                xk, dk = "x%d%d" % (c, h), "d%d%d" % (c, h)
                act(T.xx[:, xo + 1024 * h:xo + 1024 * h + 1024], Lwin.indirect(T.us[:, 128 * c + 64 * h:128 * c + 64 * h + 64]),
                    F.Identity, 1024, Lk + ["us%d%d" % (c, h)], [xk], k=GA)
                for j in range(2):
                    o = 1024 * h + 512 * j
                    op("V", lambda j=j, o=o, xo=xo: V.tensor_tensor_scan(
                        T.MM[:, 512 * j:512 * j + 512], T.xx[:, xo + o - 1:xo + o + 511], T.msk[:, :], 0.0, A.max, A.mult), vc(512),
                       [xk, "msk", "xz" + sc] + ["x%d0" % c] * h, ["M%d" % j], [j])
                    tt(T.dd[:, do + o:do + o + 512], T.xx[:, xo + o:xo + o + 512], T.MM[:, 512 * j:512 * j + 512], A.subtract, 512,
                       [xk, "M%d" % j], [dk + str(j)], [j])
                if t < 4:
                    o = 1024 * h
                    tt(B[5][:, 384 + 64 * h:448 + 64 * h], T.xx[:, xo + o + 15:xo + o + 1024:16], T.MM[:, 15:1024:16], A.max, 64,
                       [xk, "M0", "M1"], ["X%d" % h], [0, 1, 5])
                so, dv = T.sg[:, 2048 * b + 1024 * h:2048 * b + 1024 * h + 1024], T.dd[:, do + 1024 * h:do + 1024 * h + 1024]
                sk = ["sg%d%d" % (b, h)]
                s0 = [dk + "0", dk + "1"] + ["L0g", "L1g", "lb0", "lb1", "L0o0", "L1o0"] * (t == 0 and c < 2)
                if c >= SGN[t]:
                    act(so, dv, F.Sign, 1024, s0, sk, bias=-1e-9)
                else:
                    for j in range(2):
                        o = 1024 * h + 512 * j
                        op("G", lambda a=T.sg[:, 2048 * b + o:2048 * b + o + 512], x=T.dd[:, do + o:do + o + 512]:
                           g.affine_select(a, x, [[0, 512]], A.is_ge, 0.0, 0, 0), 170 + 2 * CY * 512, [dk + str(j)] + s0[2:] + sk * j, sk)
                    ts(so, so, 0.0, 0.5, A.is_gt, A.subtract, 1024, sk, sk, k=0.5)
            if t < 4:
                X = B[5][:, 384:512]
                Xk = ["X%d" % q for q in range(2)]
                ok = "L%do%d" % (t, c)
                tt(X, X, T.LW[:, own], A.subtract, 128, Xk + [ok], Xk, [5])
                if c == 0:
                    act(T.uu[:, :], T.LW[:, t * R:t * R + 512], F.Identity, 512,
                        ["L%do%d" % (t, j) for j in range(4)] + ["vl0", "vl1"] * (t == 0), ["uu"], scale=8.0)
                tt(X, X, T.uu[:, cs], A.add, 128, Xk + ["uu"], Xk, [5])
                tt(T.LW[:, new], X, T.fad[:, 256 * c + p:256 * c + 256:2], A.mult, 128, Xk + ["fad"], ["L%do%d" % (t + 2, c)], [5])
            tag[0] = tg + 3
            parts = [(0, 1), (1, 2)] if (t, c) == (4, 3) else [(0, 2)]
            Up = B[5][:, 128:256]
            for h0, h1 in parts:
                w = 64 * (h1 - h0)
                ky = lambda a: [a + str(h) for h in range(h0, h1)]
                cq, fq = B[6][:, 64 * h0:64 * h1], T.fs[:, 128 * b + 64 * h0:128 * b + 64 * h1]
                mm([(cq, T.Wc[:, 15 - s:143 - s], T.sg[:, 2048 * b + 1024 * h0 + s:2048 * b + 1024 * h1:16]) for s in range(1, 16)],
                   15 * w, ky("sg" + sb_) + ["Wc"], ky("C"), [6])
                act(fq, cq, F.Sign, w, ky("C"), ky("fs" + sb_), [6], bias=11.0 if c >= SGN[t] else 5.5)

                def ufn(h0=h0, h1=h1, b=b, m=w // NQ):
                    for q in range(NQ):
                        o, a = B[5][:, 128 + 64 * h0 + m * q:128 + 64 * h0 + m * q + m], (128 * q + 64 * h0) // NQ
                        for vb in range(NQ):
                            z = 144 * q + 16 - G - G * vb
                            P.matmul(o, T.Pm[:, z:z + 128], T.fs[:, 128 * b + 64 * h0 + vb:128 * b + 64 * h1:NQ], vb == 0, False)
                        ins = P.matmul(o, T.Ih[:, :], T.jc[:, a:a + m], False, True)
                    return ins
                op("P", ufn, OV + PCY * 64 * NQ * (NQ + 1), ky("fs" + sb_) + ["Pm%d" % q for q in range(NQ)] + ["Ih", "jc"], ky("U"), [5])
                aff("A", T.um[:, 128 * c + 64 * h0:128 * c + 64 * h1], B[5][:, 128 + 64 * h0:128 + 64 * h1], 1.0, -3072.0, w,
                    ky("U"), ky("um" + sc), [5])
            Fp = B[5][:, 256:384]
            mm([(Fp, T.FW[:, 0:128], T.fs[:, bs]), (Fp, T.FW[:, 128:256], T.fs[:, bs])], 256, ["fs%d0" % b, "fs%d1" % b, "FW0", "FW1"],
               ["F"], [5])
            tt(T.yy[:, cs], Fp, T.p2[:, cs], A.mult, 128, ["F", "p2%d0" % c, "p2%d1" % c], ["yy" + sc], [5])
            ts(Fp, T.yy[:, cs], 2.0 ** 23 - 0.5, 2.0 ** 23 + 1, A.add, A.is_equal, 128, ["yy" + sc], ["F"], [5])
            tt(T.la[:, bs], Fp, T.ac[:, cs], A.mult, 128, ["F", "ac%d0" % c, "ac%d1" % c], ["la" + sb_], [5])
            base = slice(p * R + 128 * c, p * R + 128 * c + 128)

            def sm(o, a=0):
                its = [(o, T.SA[:, a:a + 128], T.la[:, bs])]
                if t < 2:
                    return its + [(o, T.SB[:, 144 + a:272 + a], T.PW[:, own])]
                j = 144 * (1 + t // 2) + a
                return its + [(o, T.SB[:, a:a + 128], T.PW[:, own]), (o, T.SB[:, j:j + 128], T.PW[:, base])]
            sk = ["la" + sb_, "SA", "SB0", "SB1", "SB2", "SB3", "P%do%d" % (t, c), "P%dd" % p, "P%do%d" % (p, c)]
            S1, S2 = B[6][:, 128:256], B[6][:, 256:384]
            if t < 4 and c < 3:
                mm(sm(S2, 16), 128 * len(sm(S2)), sk, ["S2"], [6])
                aff("V", T.Hs[:, :], S2, ct[:, 24:25], 0.0, 128, ["S2", "r4"], ["Hs"], [6])
                tt(T.Ps[:, cs], S2, T.Hs[:, :], A.subtract, 128, ["S2", "Hs"], ["Ps" + sc], [6])
                op("G", lambda t=t, c=c, cs=cs: fan(g, T, topo, core, r, T.Ps[:, cs],
                                                    lambda d: T.PW[:, gcol(t + 2, d, c):gcol(t + 2, d, c) + 128],
                                                    T.sem["ap%d" % t], T.sem["lp%d" % c]),
                   800.0, ["Ps" + sc], ["sP%d" % (3 * t + c)], tok=("lp" + sc, ne * (t + 1)), lat=2500.0)
                mm([(S1, T.Sh[:, :], T.Ps[:, cs])], 128, ["Sh", "Ps" + sc], ["S1"], [6])
                act(T.PW[:, new], S1, F.Identity, 128, ["S1"], ["P%do%d" % (t + 2, c)], [6])
            if t >= 3 or c == 3:
                mm(sm(S1), 128 * len(sm(S1)), sk, ["S1"], [6])
            if t < 4 and c == 3:
                aff("V", T.Hs[:, :], S1, ct[:, 24:25], 0.0, 128, ["S1", "r4"], ["Hs"], [6])
                tt(T.PW[:, new], S1, T.Hs[:, :], A.subtract, 128, ["S1", "Hs"], ["P%do%d" % (t + 2, c)], [6])
            if t >= 3:
                act(T.hq[:, bs], S1, F.Identity, 128, ["S1"], ["hq" + sb_], [6], bias=196607.5, scale=-1.0)
                mm(sm(S2) + [(S2, T.SB[:, 576:704], T.hq[:, bs])], 512, sk + ["hq" + sb_, "SB4"], ["S2"], [6])
                act(T.LW[:, 256 * c + p:256 * c + 256:2], S2, F.Identity, 128, ["S2"],
                    ["yo%d%d" % (p, c)] + ["L0o0", "L0o1", "L0o2", "L0o3", "L0g"] * (t == 3 and c == 0), [6], bias=512.0 - 196608.0)
            if t < 4 and c < 3:
                q = 3 * t + c

                def s_h(q=q, new=new):
                    g.remote_dma_fused([RemoteDMATransfer(
                        dst_ids=[did(topo, hL), did(topo, hL)], dma_engine_mask=emask(topo, core, hL, 8, 8),
                        remote_sem=T.sem["ha%d" % q], srcs=[T.LW[:, new]],
                        dsts=[T.hbL[256 * q:256 * q + 128, :], T.hbL[256 * q + 128:256 * q + 256, :]])], local_sem=T.sem.lsm)
                    lsm[0] += 8
                send(s_h, ["L%do%d" % (t + 2, c)], ["sL%d" % q])
            tag[0] = tg + 4
            for h in range(2):
                dk = ["d%d%d0" % (c, h), "d%d%d1" % (c, h)]
                dv = T.dd[:, do + 1024 * h:do + 1024 * h + 1024]
                act(dv, dv, F.Sigmoid, 1024, dk, dk)
            u = (4 * t + c) % NT
            direct = "%d%d" % (t, c) in DIR
            for h0, h1 in parts:
                tag[0] = tg + 4 + h0
                w = 64 * (h1 - h0)
                hs = range(h0, h1)
                tk = [["tt%d%d%d" % (u, q, h) for h in hs] for q in range(NQ)]
                to, m = 2048 * u + 1024 * h0, G * w
                for q in range(NQ):
                    o = 128 * c + 64 * h0 + w // NQ * q
                    tt(T.tt[:, to + m * q:to + m * q + m], T.xx[:, c * XW:xo + 1024 * h1].indirect(T.um[:, o:o + w // NQ]),
                       T.dd[:, do + 1024 * h0 + q:do + 1024 * h1:NQ], A.mult, m,
                       ["d%d%d%d" % (c, h, j) for h in hs for j in range(2)] + ["x%d%d" % (c, h) for h in hs]
                       + ["x%d0" % c, "xz" + sc] + ["um%d%d" % (c, h) for h in hs] + ["tf%d" % u] * (w == 64), tk[q], k=GA)
                q = NQ
                while q > 1 and not direct:
                    q //= 2
                    gdma("ad%d" % u, T.tt[:, to:to + m * q], T.tt[:, to + m * q:to + 2 * m * q], sum(tk[:2 * q], []),
                         sum(tk[:q], []), 2400.0 + m * q)
                Ep = B[7][:, 128 * c + 64 * h0:128 * c + 64 * h1]
                ev = T.EE[:, 256 * c + 128 * h0 + p:256 * c + 128 * h1:2]
                ek = ["E%d%d%d" % (p, c, h) for h in hs]
                pk = ["Ep%d%d" % (c, h) for h in hs]
                its = [(Ep, T.If[:, :], ev, ek)] * (t >= 2)
                for j in range(q):
                    its += [(Ep, T.If[:, :], T.tt[:, to + m * j + s:to + m * j + m:G], tk[j]) for s in range(G)]
                cuts = list(range(len(its) % 4, len(its) + 1, 4))
                cuts[0] = 0
                for a, z in zip(cuts, cuts[1:]):
                    mm([x[:3] for x in its[a:z]], 4 * w * (z - a), ["If"] + [k for x in its[a:z] for k in x[3]] + pk * (a > 0),
                       pk + ["Eg"] + ["tf%d" % u] * (w == 128), [7], first=a == 0, last=z == len(its))
            act(T.EE[:, 256 * c + p:256 * c + 256:2], B[7][:, 128 * c:128 * c + 128], F.Identity, 128,
                ["Ep%d0" % c, "Ep%d1" % c], ["E%d%d0" % (p, c), "E%d%d1" % (p, c)], [7])
            if t == 4:
                dma("S", [(T.ye[:, 256 * c:256 * c + 256], T.EE[:, 256 * c:256 * c + 256])],
                    ["E%d%d%d" % (a, c, h) for a in range(2) for h in range(2)], ["ye" + sc])
        if t < 4:
            ext("al%d" % t, 9 * ne, ["sL%d" % (3 * t + c) for c in range(3)], ["L%dg" % (t + 2)], 7000.0)
            ext("ap%d" % t, 9 * ne, ["sP%d" % (3 * t + c) for c in range(3)], ["P%dg" % (t + 2)], 1000.0)
        if t < 3:
            tag[0] = 25 * t + 25
            Cq = B[2][:, 0:32]
            mm([(Cq, T.Wt[:, 15 - j:143 - j], T.cp[:, j:512:16]) for j in range(16)], 16 * 64,
               ["cp%d" % c for c in range(4)] + ["Wt"], ["D0"], [2])
            a0, a1 = T.ty[:, 0:32], T.ty[:, 32:64]
            ts(a0, Cq, 0.0, 1.0 - 2 * p - 2 * R, A.is_ge, A.mult, 32, ["D0"], ["ty", "a0"], [2])
            tt(a0, Cq, a0, A.add, 32, ["D0", "a0"], ["a0"], [2])
            ts(a1, a0, 1023.5 - 2 * R - p, None, A.is_lt, None, 32, ["a0"], ["ty", "a1"])
            tt(a0, a0, T.slf[:, :], A.subtract, 32, ["a0", "slf"], ["a0"])
            tt(a0, a0, a1, A.mult, 32, ["a0", "a1"], ["a0"])
            tt(a0, a0, T.slf[:, :], A.add, 32, ["a0", "slf"], ["a0"])
            ts(T.ul[:, :], a0, 2.0 * R + p, None, A.add, None, 32, ["a0"], ["ul"])
            mk = "nb%d" % p
            tt(T.go[:, :], T.nbs[:, :].indirect(T.ul[:, :]), T.nbr[:, p:1024:2], A.subtract, 512, ["ul", "nbs", mk], ["go"], k=GA)
            for h in range(2):
                hs = slice(256 * h, 256 * h + 256)
                e = T.nbr[:, 512 * h + p:512 * h + 512:2]
                yk = ["yy%d" % (2 * h), "yy%d" % (2 * h + 1)]
                ts(Z, T.yy[:, hs], 1.5 * 2 ** 24, 1.5 * 2 ** 24, A.add, A.subtract, 256, yk, ["Z"], [4])
                tt(Z, Z, T.yy[:, hs], A.is_lt, 256, ["Z"] + yk, ["Z"], [4])
                tt(Z, Z, T.go[:, hs], A.mult, 256, ["Z", "go"], ["Z"], [4])
                tt(e, Z, e, A.add, 256, ["Z", mk], [mk], [4])
            decode(p)
            if t < 2:
                dma("S", [(T.nbs[:, :], T.nbr[:, :])], ["nb0", "nb1"], ["nbs"])
    dma("S", [(T.yp[:, :], T.LW[1:128:16, 0:1024])], ["yo%d%d" % (a, c) for a in range(2) for c in range(4)], ["yp"])
    return ops, lsm


def schedule(ops):
    n = len(ops)
    deps = [set() for _ in range(n)]
    lw, rd = {}, {}
    for i, o in enumerate(ops):
        for k in o["r"]:
            if k in lw:
                deps[i].add(lw[k])
        for k in o["w"]:
            if k in lw:
                deps[i].add(lw[k])
            deps[i].update(rd.get(k, ()))
        deps[i].discard(i)
        for k in o["r"]:
            rd.setdefault(k, []).append(i)
        for k in o["w"]:
            lw[k] = i
            rd[k] = []
    pre = [sorted(d) for d in deps]
    suc = [[] for _ in range(n)]
    for i in range(n):
        for j in pre[i]:
            suc[j].append(i)
    eng = ["VAPGSX".index(o["e"]) for o in ops]
    bks, lat, tag = [o["b"] for o in ops], [o["lat"] for o in ops], [o["tag"] for o in ops]
    last = [i for i in range(n) if not suc[i]]
    seed = [SEED]

    def rnd():
        seed[0] = (seed[0] * 1103515245 + 12345) % 2147483648
        return seed[0] / 2147483648.0

    def case(ga, pe, wt):
        return [(eng[i], ops[i]["c"] * (pe if eng[i] == 2 else ga if ops[i]["g"] else 1.0),
                 [(j, wt * (lat[j] + (SL if eng[i] == eng[j] else XL))) for j in pre[i]], bks[i]) for i in range(n)], wt
    mean = case(*MEAN)
    cost, back = [x[1] for x in mean[0]], [x[2] for x in mean[0]]
    fwd = [[] for _ in range(n)]
    for i in range(n):
        for j, d in back[i]:
            fwd[j].append((i, d))

    def place(pri, rev):
        pred, succ = (fwd, back) if rev else (back, fwd)
        left = [len(x) for x in pred]
        rt = [lat[i] if rev and not left[i] else 0.0 for i in range(n)]
        ready = sorted(((pri[i], i) for i in range(n) if not left[i]), reverse=True)
        st, en, ow = [[] for _ in range(14)], [[] for _ in range(14)], [[] for _ in range(14)]
        fin = [0.0] * n
        while ready:
            i = ready.pop()[1]
            e, c, s = eng[i], cost[i], rt[i]
            if e < 5:
                while True:
                    a, z = st[e], en[e]
                    m = k = len(a)
                    while m and z[m - 1] > s:
                        m -= 1
                    while m < k and a[m] < s + c:
                        s = z[m]
                        m += 1
                    s0 = s
                    for b in bks[i]:
                        a, z, w = st[6 + b], en[6 + b], ow[6 + b]
                        q = k = len(a)
                        while q and a[q - 1] > s - 4000.0:
                            q -= 1
                        while q < k and a[q] < s + c + XL:
                            if w[q] != e and z[q] + XL > s:
                                s = z[q] + XL
                            q += 1
                    if s == s0:
                        break
                st[e].insert(m, s)
                en[e].insert(m, s + c)
                for b in bks[i]:
                    a = st[6 + b]
                    q = len(a)
                    while q and a[q - 1] > s:
                        q -= 1
                    a.insert(q, s)
                    en[6 + b].insert(q, s + c)
                    ow[6 + b].insert(q, e)
            s += c
            fin[i] = s
            for j, d in succ[i]:
                if s + d > rt[j]:
                    rt[j] = s + d
                left[j] -= 1
                if not left[j]:
                    q, x = len(ready), (pri[j], j)
                    while q and ready[q - 1] < x:
                        q -= 1
                    ready.insert(q, x)
        return fin

    def pack(fin):
        return place([-x for x in place([-x for x in fin], True)], False)

    def shift(fin, tries, heat):
        cur = best = (max(fin[i] + lat[i] for i in last), fin)
        for _ in range(tries):
            a = int(rnd() * n)
            dl, one, f = (rnd() - 0.5) * (1500.0, 4000.0, 12000.0)[int(rnd() * 3)], rnd() < 0.5, cur[1]
            end = place([f[i] - cost[i] + (dl if tag[i] == tag[a] and (not one or eng[i] == eng[a]) else 0.0) for i in range(n)], False)
            if rnd() < 0.15:
                end = pack(end)
            v = max(end[i] + lat[i] for i in last)
            if v <= cur[0] + heat * rnd():
                cur = (v, end)
                if v < best[0]:
                    best = cur
        return sorted(range(n), key=lambda i: (best[1][i] - cost[i], best[1][i], i))

    def play(cs, seq, a, fin, why):
        node, wt = cs
        free, bank = [-1] * 6, [-1] * 8
        k, miss, xl = a - 1, 13, XL * wt
        while k >= 0 and miss:
            i = seq[k]
            if eng[i] < 5 and free[eng[i]] < 0:
                free[eng[i]] = i
                miss -= 1
            for b in bks[i]:
                if bank[b] < 0:
                    bank[b] = i
                    miss -= 1
            k -= 1
        for i in seq[a:]:
            e, c, bk, bs = node[i]
            w = free[e]
            s = fin[w] if w >= 0 else 0.0
            for j, d in bk:
                if fin[j] + d > s:
                    s, w = fin[j] + d, -2 - j
            for b in bs:
                j = bank[b]
                if j >= 0 and eng[j] != e and fin[j] + xl > s:
                    s, w = fin[j] + xl, j
                bank[b] = i
            fin[i], why[i] = s + c, w
            if e < 5:
                free[e] = i
        return max((fin[i] + wt * lat[i], i) for i in last) + (fin, why)

    def tighten(seq, cases, moves, heat):
        now = [play(cs, seq, 0, [0.0] * n, [-1] * n) for _, cs in cases]
        cur = sum(w * x[0] for (w, _), x in zip(cases, now))
        best, pos, paths = (cur, seq, now[0][2]), [0] * n, None
        for it in range(moves):
            if paths is None:
                for k, i in enumerate(seq):
                    pos[i] = k
                paths = {}
            x, q = rnd(), 0
            while q < len(cases) - 1 and x > cases[q][0]:
                x -= cases[q][0]
                q += 1
            why = now[q][3]
            if q not in paths:
                path, i = [], now[q][1]
                while i >= 0:
                    path.append(i)
                    i = why[i] if why[i] >= -1 else -2 - why[i]
                path.reverse()
                paths[q] = (path, [k for k in range(1, len(path)) if why[path[k]] >= 0])
            path, cand = paths[q]
            k = cand[int(rnd() * len(cand))]
            early = rnd() < 0.5
            if early:
                m = k - 1
                while m > 0 and why[path[m]] >= 0 and rnd() < 0.6:
                    m -= 1
                u, v = path[m], path[k]
            else:
                m = k
                while m + 1 < len(path) and why[path[m + 1]] >= 0 and rnd() < 0.6:
                    m += 1
                u, v = path[k - 1], path[m]
            a, z = pos[u], pos[v]
            x, stop, near = (v, u, pre) if early else (u, v, suc)
            mv, todo = {x}, [x]
            while todo and stop not in mv:
                for j in near[todo.pop()]:
                    if a <= pos[j] <= z and j not in mv:
                        mv.add(j)
                        todo.append(j)
            if stop in mv:
                continue
            mid = seq[a:z + 1]
            new = seq[:a] + [j for j in mid if (j in mv) == early] + [j for j in mid if (j in mv) != early] + seq[z + 1:]
            room = -heat * max(0.05, 1.0 - it / moves) * math.log(max(rnd(), 1e-9))
            one = play(cases[q][1], new, a, now[q][2][:], why[:])
            if one[0] > now[q][0] + room + 30.0 * (len(cases) > 1):
                continue
            nxt = [one if j == q else play(cases[j][1], new, a, now[j][2][:], now[j][3][:]) for j in range(len(cases))]
            v = sum(w * x[0] for (w, _), x in zip(cases, nxt))
            if v <= cur + room:
                seq, now, cur, paths = new, nxt, v, None
                if cur < best[0]:
                    best = (cur, seq, now[0][2])
        return best[1:]

    bl = [0.0] * n
    for i in range(n - 1, -1, -1):
        bl[i] = cost[i] + max([bl[j] + d for j, d in fwd[i]] + [lat[i]])
    end = pack(pack(place([-x for x in bl], False)))
    for tries, heat in SHIFTS:
        order, end = tighten(shift(end, tries, heat), [(1.0, mean)], MOVES[0], 40.0)
    cases = [(c[0], case(*c[1:])) for c in CASES]
    for _ in range(MOVES[2]):
        order, end = tighten(order, cases, MOVES[1], 30.0)
    bank = {}
    for i in order:
        for b in ops[i]["b"]:
            for e, j in bank.get(b, {}).items():
                if e != ops[i]["e"]:
                    deps[i].add(j)
            bank.setdefault(b, {})[ops[i]["e"]] = i
    return order, deps, [end[i] + ops[i]["lat"] for i in range(n)]


def rank_program(g, core, T, topo):
    r = T.rank_of(core)
    if r is None:
        for q, c in enumerate(T.cores):
            if core == helper(c, T, topo):
                helper_program(g, core, T, topo, q)
        return
    ops, lsm = build(g, core, T, topo, r)
    if "s" not in CACHE:
        CACHE["s"] = schedule(ops)
    order, deps, fin = CACHE["s"]
    Q = {"V": g.vector, "A": g.scalar, "P": g.tensor, "G": g, "S": g.sync}
    know = {e: {} for e in Q}
    cnt = {e: 0 for e in Q}
    tok, snap = {}, {}
    for i in order:
        o = ops[i]
        e = o["e"]
        if e == "X":
            tok[i], snap[i] = o["tok"], {}
            continue
        kn = know[e]
        need = {}
        for j in deps[i]:
            if tok[j] is not None and kn.get(tok[j][0], 0) < tok[j][1] and need.get(tok[j][0], (0, 0))[0] < tok[j][1]:
                need[tok[j][0]] = (tok[j][1], j)
        for s, (v, j) in sorted(need.items(), key=lambda x: -fin[x[1][1]]):
            if kn.get(s, 0) < v:
                Q[e].wait_ge(T.sem[s], v)
                kn[s] = v
                for s2, v2 in snap[j].items():
                    if kn.get(s2, 0) < v2:
                        kn[s2] = v2
        snap[i] = dict(kn)
        ins = o["fn"]()
        if o["tok"] is None:
            cnt[e] += 1
            ins.then_inc(T.sem["c" + e], 1)
            tok[i] = ("c" + e, cnt[e])
        else:
            tok[i] = None if o["tok"] == "none" else o["tok"]
    last = {}
    for t in tok.values():
        if t is not None:
            last[t[0]] = max(last.get(t[0], 0), t[1])
    g.wait_ge(T.sem.lsm, lsm[0])
    for s, v in last.items():
        if know["S"].get(s, 0) < v:
            g.sync.wait_ge(T.sem[s], v)
